import numpy as np
import ml_dtypes


def mxq(x, axis, fmt="e4m3"):
    dtype, down = {"e4m3": (ml_dtypes.float8_e4m3fn, 7), "e5m2": (ml_dtypes.float8_e5m2, 14)}[fmt]
    v = np.moveaxis(np.asarray(x, np.float32).astype(ml_dtypes.bfloat16).astype(np.float64), axis, -1)
    blocks = v.reshape(v.shape[:-1] + (-1, 32))
    amax = np.abs(blocks).max(-1, keepdims=True)
    byte = np.maximum(np.where(amax > 0, np.frexp(amax)[1] - 1 + 127, 0) - down, 1)
    scale = np.exp2(byte - 127.0)
    codes = (blocks / scale).astype(np.float32).astype(dtype).astype(np.float64)
    return np.moveaxis((codes * scale).reshape(v.shape), -1, axis)


WIDE = False


def mx_kscale(k):
    if not WIDE:
        return np.ones(k)
    levels = np.array([10, -10, 5, -5, 0])
    if k % 512:
        return np.exp2(np.random.permutation(np.resize(levels, k // 32))).repeat(32)
    a = np.empty((k // 512, 16))
    for p in range(k // 512):
        a[p, :8] = np.random.permutation(np.resize(levels, 8))
        for g in range(8):
            far = levels[np.abs(levels - a[p, g]) >= 10]
            a[p, g + 8] = far[np.random.randint(len(far))]
    return np.exp2(a.ravel()).repeat(32)


def f64(x):
    return np.asarray(x).astype(np.float64)


def striped(idx):
    return np.tile(idx.reshape(-1, 16).T, (8, 1)).astype(np.uint16)


def unstriped(offs):
    return offs[:16].T.reshape(-1).astype(np.int64)


E2M1 = np.array([0.0, 0.5, 1.0, 1.5, 2.0, 3.0, 4.0, 6.0, -0.0, -0.5, -1.0, -1.5, -2.0, -3.0, -4.0, -6.0])


def pack_weight(w, fmt):
    k, n = w.shape
    w = f64(np.asarray(w, np.float32).astype(ml_dtypes.bfloat16)).reshape(k // 32, 32, n)
    amax = np.abs(w).max(1)
    if fmt == "e4m3":
        byte = np.frexp(amax)[1] - 1 + 127 - 7
    else:
        mant, ex = np.frexp(amax / 6.0)
        byte = np.where(mant > 0.5, ex, ex - 1) + 127
    byte = np.clip(np.where(amax > 0, byte, 1), 1, 254)
    scaled = (w * np.exp2(127.0 - byte)[:, None, :]).reshape(k, n).astype(np.float32)
    by_word = np.ascontiguousarray(scaled.reshape(k // 512, 128, 4, n).transpose(0, 1, 3, 2))
    if fmt == "e4m3":
        words = by_word.astype(ml_dtypes.float8_e4m3fn).view(np.uint8)
    else:
        c = by_word.astype(ml_dtypes.float4_e2m1fn).view(np.uint8) & 0xF
        words = (c[..., 0::2] | (c[..., 1::2] << 4)).reshape(k // 512, 128, 2 * n)
    return np.ascontiguousarray(words), np.ascontiguousarray(byte.astype(np.uint8).reshape(k // 512, 16, n))


def unpack_weight(words, scales, fmt):
    g, _, n = scales.shape
    words = np.ascontiguousarray(words).reshape(g, 128, n, -1)
    if fmt == "e4m3":
        vals = words.view(ml_dtypes.float8_e4m3fn).astype(np.float64)
    else:
        nib = np.empty((g, 128, n, 4), np.uint8)
        nib[..., 0::2] = words & 0xF
        nib[..., 1::2] = words >> 4
        vals = E2M1[nib]
    vals = vals * np.repeat(np.exp2(scales.astype(np.float64) - 127.0), 8, axis=1)[..., None]
    return vals.transpose(0, 1, 3, 2).reshape(g * 512, n)


def relu(v):
    return np.maximum(v, 0.0)


K, T, E, C, N = 512, 768, 9, 256, 384
TOP = 3


def by_expert(wq, xq):
    return np.concatenate([wq[e].T @ xq[:, e * C:(e + 1) * C] for e in range(E)], axis=1)


def setup_inputs():
    n = np.random.standard_normal
    s = mx_kscale(K)[:, None]
    deal = np.repeat(np.arange(E), C).reshape(TOP, T)[:, np.random.permutation(T)]
    deal = np.take_along_axis(deal, np.argsort(np.random.rand(TOP, T), axis=0), axis=0)
    for _ in range(8):
        s_, t_ = np.random.permutation(T).reshape(2, -1); r = np.random.randint(TOP, size=T // 2); x, y = deal[r, s_].copy(), deal[r, t_].copy()
        ok = ~((deal[:, s_] == y).any(0) | (deal[:, t_] == x).any(0)); deal[r[ok], s_[ok]] = y[ok]; deal[r[ok], t_[ok]] = x[ok]
    order = np.lexsort((np.random.rand(TOP * T), deal.reshape(-1)))
    slot_token = order % T; pos = np.empty(TOP * T, np.int64); pos[order] = np.arange(TOP * T); pos = pos.reshape(TOP, T)
    g = np.random.uniform(0.5, 1.5, (TOP, T)); g = g / g.sum(0)
    w = [pack_weight(m, "e2m1") for m in n((E, K, N)) / np.sqrt(K) / s[None]]
    w_slot = np.empty(E * C)
    for r in range(TOP): w_slot[pos[r]] = g[r]
    return {
        "xT": (n((K, T)) * s).astype(np.float32),
        "w_words": np.stack([m[0] for m in w]),
        "w_scales": np.stack([m[1] for m in w]),
        "b": (0.3 * n((N, E))).astype(np.float32),
        "gate": np.tile(w_slot, (K, 1)).astype(np.float32),
        "offs": striped(slot_token),
        "pos1": striped(pos[0]),
        "pos2": striped(pos[1]),
        "pos3": striped(pos[2]),
    }


def reference(xT, w_words, w_scales, b, gate, offs, pos1, pos2, pos3):
    idx = unstriped(offs)
    w = np.stack([unpack_weight(w_words[e], w_scales[e], "e2m1") for e in range(E)])
    xq = mxq(f64(gate) * f64(xT)[:, idx], 0, "e4m3")
    y = by_expert(w, xq)
    y = relu(y + np.repeat(f64(b), C, axis=1))
    return y[:, unstriped(pos1)] + y[:, unstriped(pos2)] + y[:, unstriped(pos3)]

@@ -1,0 +1,192 @@
+from contextlib import ExitStack
+
+import concourse.mybir as mybir
+from concourse.masks import make_identity
+
+K, T, E, C, N = 512, 768, 9, 256, 384
+S = E * C
+FLOPS = 2 * K * N * S
+BYTES = 4 * K * T + E * K * N // 2 + E * (K // 32) * N + 4 * N * E + 4 * S + 2 * 128 * (S + 3 * T) // 16 + 4 * N * T
+
+F32 = mybir.dt.float32
+BF16 = mybir.dt.bfloat16
+I32 = mybir.dt.int32
+U32 = mybir.dt.uint32
+U16 = mybir.dt.uint16
+U8 = mybir.dt.uint8
+FP8X4 = mybir.dt.float8_e4m3fn_x4
+FP4X4 = mybir.dt.float4_e2m1fn_x4
+MULT = mybir.AluOpType.mult
+ADD = mybir.AluOpType.add
+RELU = mybir.ActivationFunctionType.Relu
+
+P = 128
+PACK = 4
+BANK = 512
+ROW_TILES = N // P
+TOKEN_BLOCKS = T // P
+HALF = T // 2
+
+CHUNKS = [(0, 512), (512, 512), (1024, 512), (1536, 384), (1920, 256), (2176, 128)]
+GATE_LOADS = [(0, 512), (512, 512), (1024, 1280)]
+
+
+def tile_moe_pre_lin_relu_kernel(tc, xT, w_words, w_scales, b, gate, offs, pos1, pos2, pos3, out):
+    nc = tc.nc
+    with ExitStack() as ctx:
+        keep = ctx.enter_context(tc.tile_pool(name="keep", bufs=1))
+        psum_a = ctx.enter_context(tc.psum_pool(name="psum_a", bufs=2))
+        psum_b = ctx.enter_context(tc.psum_pool(name="psum_b", bufs=6))
+
+        offs_sb = keep.tile([P, S // 16], U16, name="offs_sb")
+        pos_sb = [keep.tile([P, T // 16], U16, name="pos_sb%d" % r) for r in range(3)]
+        planes = [keep.tile([P, T], F32, name="plane%d" % j, align_bytes=64) for j in range(PACK)]
+        gates = [keep.tile([P, n], F32, name="gate%d" % i, align_bytes=64) for i, (s0, n) in enumerate(GATE_LOADS)]
+        w_sb = keep.tile([P, E, 2 * N], U8, name="w_sb", align_bytes=64)
+        ws_sb = keep.tile([P, E, N], U8, name="ws_sb", align_bytes=64)
+        b_sb = keep.tile([P, ROW_TILES, E], F32, name="b_sb", align_bytes=64)
+        ident = keep.tile([P, P], F32, name="ident", align_bytes=64)
+        x_bf = keep.tile([P, S * PACK], BF16, name="x_bf", align_bytes=64)
+        x_codes = keep.tile([P, S], U32, name="x_codes", align_bytes=64)
+        x_scales = keep.tile([P, S], U8, name="x_scales", align_bytes=64)
+        ys = [keep.tile([P, S], F32, name="y%d" % r, align_bytes=64) for r in range(ROW_TILES)]
+
+        nc.vector.memset(ws_sb[:].rearrange("p e n -> p (e n)").bitcast(I32), 0)
+        make_identity(nc, ident[:])
+
+        x_rows = xT.rearrange("(p j) t -> p j t", j=PACK)
+
+        def load_gate(i):
+            s0, n = GATE_LOADS[i]
+            nc.sync.dma_start(gates[i][:], gate[0:P, s0:s0 + n])
+
+        nc.sync.dma_start(offs_sb[:], offs)
+        nc.sync.dma_start(planes[0][:], x_rows[:, 0, :])
+        load_gate(0)
+        for j in range(1, PACK):
+            nc.sync.dma_start(planes[j][:], x_rows[:, j, :])
+        load_gate(1)
+        scale_rows = w_scales.rearrange("e a q n -> q (e a) n").bitcast(I32)
+        for q in range(4):
+            nc.sync.dma_start(ws_sb[32 * q:32 * q + 4, :, :].bitcast(I32), scale_rows[4 * q:4 * q + 4, :, :])
+        nc.sync.dma_start(w_sb[:].bitcast(I32), w_words.rearrange("e a p n -> p (e a) n").bitcast(I32))
+        nc.sync.dma_start(b_sb[:], b.rearrange("(r p) e -> p r e", p=P))
+        load_gate(2)
+        for r, pos in enumerate((pos1, pos2, pos3)):
+            nc.sync.dma_start(pos_sb[r][:], pos)
+
+        def gate_cols(s0, n):
+            for i, (g0, gn) in enumerate(GATE_LOADS):
+                if g0 <= s0 and s0 + n <= g0 + gn:
+                    return gates[i][:, s0 - g0:s0 - g0 + n]
+            raise ValueError("no gate tile")
+
+        def gather_chunk(c):
+            s0, n = CHUNKS[c]
+            gathered = keep.tile([P, PACK, n], F32, name="gathered%d" % c, align_bytes=64)
+            for j in range(PACK):
+                nc.vector.tensor_tensor(
+                    gathered[:, j, :],
+                    planes[j][:].indirect(offs_sb[:, s0 // 16:(s0 + n) // 16]),
+                    gate_cols(s0, n),
+                    MULT,
+                )
+            nc.scalar.copy(
+                x_bf[:, PACK * s0:PACK * (s0 + n)].rearrange("p (c i t) -> p c t i", i=4, t=PACK),
+                gathered[:].rearrange("p t (c i) -> p c t i", i=4),
+            )
+
+        def quantize(s0, n):
+            nc.vector.quantize_mx(
+                out=x_codes[:, s0:s0 + n].bitcast(FP8X4),
+                scales=x_scales[:, s0:s0 + n],
+                in_=x_bf[:, PACK * s0:PACK * (s0 + n)],
+            )
+
+        def experts(r, pieces, pool):
+            bank = pool.tile([P, BANK], F32, name="bank")
+            at = 0
+            for s0, n in pieces:
+                e = s0 // C
+                nc.tensor.matmul_mx(
+                    out=bank[:, at:at + n],
+                    lhsT=w_sb[:, e, 2 * P * r:2 * P * (r + 1)].bitcast(FP4X4),
+                    lhsT_scale=ws_sb[:, e, P * r:P * (r + 1)],
+                    rhs=x_codes[:, s0:s0 + n].bitcast(FP8X4),
+                    rhs_scale=x_scales[:, s0:s0 + n],
+                    start=True,
+                    stop=True,
+                )
+                at += n
+            at = 0
+            for s0, n in pieces:
+                e = s0 // C
+                nc.scalar.activation(ys[r][:, s0:s0 + n], bank[:, at:at + n], RELU, bias=b_sb[:, r, e:e + 1])
+                at += n
+
+        gather_chunk(0)
+        gather_chunk(1)
+        quantize(0, 512)
+        experts(0, [(0, C), (C, C)], psum_a)
+        gather_chunk(2)
+        quantize(512, 512)
+        experts(0, [(2 * C, C), (3 * C, C)], psum_a)
+        gather_chunk(3)
+        gather_chunk(4)
+        quantize(1024, 512)
+        experts(0, [(4 * C, C), (5 * C, C)], psum_a)
+        gather_chunk(5)
+        quantize(1536, 256)
+        experts(0, [(6 * C, C)], psum_a)
+        quantize(1792, 128)
+        quantize(1920, 256)
+        experts(0, [(7 * C, C), (8 * C, 128)], psum_a)
+        quantize(2176, 128)
+        experts(0, [(2176, 128)], psum_a)
+        for r in range(1, ROW_TILES):
+            for e0 in range(0, E, 2):
+                experts(r, [(e * C, C) for e in range(e0, min(e0 + 2, E))], psum_b)
+
+        def fetch(r, l, t0, n):
+            picked = keep.tile([P, n], F32, name="picked%d_%d_%d" % (r, l, t0), align_bytes=64)
+            nc.vector.tensor_copy(picked[:], ys[r][:].indirect(pos_sb[l][:, t0 // 16:(t0 + n) // 16]))
+            return picked
+
+        def tensor_sum(r, lists):
+            sums = [psum_b.tile([P, BANK], F32, name="bank") for blk in range(TOKEN_BLOCKS)]
+            for l in lists:
+                picked = fetch(r, l, 0, T)
+                for blk in range(TOKEN_BLOCKS):
+                    nc.tensor.matmul(
+                        sums[blk][:, 0:P],
+                        lhsT=picked[:, blk * P:(blk + 1) * P],
+                        rhs=ident[:],
+                        start=(l == lists[0]),
+                        stop=(l == lists[-1]),
+                        is_transpose=True,
+                    )
+            turned = keep.tile([P, T], F32, name="turned%d" % r, align_bytes=64)
+            total = keep.tile([P, T], F32, name="total%d" % r, align_bytes=64)
+            for h in range(2):
+                back = psum_a.tile([P, BANK], F32, name="bank")
+                for i in range(3):
+                    blk = 3 * h + i
+                    nc.scalar.copy(turned[:, blk * P:(blk + 1) * P], sums[blk][:, 0:P])
+                    nc.tensor.transpose(back[:, i * P:(i + 1) * P], turned[:, blk * P:(blk + 1) * P], ident[:])
+                nc.scalar.copy(total[:, h * HALF:(h + 1) * HALF], back[:, 0:HALF])
+            return total
+
+        def store(r, t0, n, src):
+            nc.sync.dma_start(out[r * P:(r + 1) * P, t0:t0 + n], src)
+
+        total0 = tensor_sum(0, [0, 1, 2])
+        store(0, 0, T, total0[:])
+        partial1 = tensor_sum(1, [0, 1])
+        total2 = tensor_sum(2, [0, 1, 2])
+        for h in range(2):
+            store(2, h * HALF, HALF, total2[:, h * HALF:(h + 1) * HALF])
+        lasts = [fetch(1, 2, h * HALF, HALF) for h in range(2)]
+        for h in range(2):
+            total1 = keep.tile([P, HALF], F32, name="total1_%d" % h, align_bytes=64)
+            nc.vector.tensor_tensor(total1[:], lasts[h][:], partial1[:, h * HALF:(h + 1) * HALF], ADD)
+            store(1, h * HALF, HALF, total1[:])

@@ -18,6 +18,7 @@ FP8X4 = mybir.dt.float8_e4m3fn_x4
 FP4X4 = mybir.dt.float4_e2m1fn_x4
 MULT = mybir.AluOpType.mult
 ADD = mybir.AluOpType.add
+MAX = mybir.AluOpType.max
 RELU = mybir.ActivationFunctionType.Relu
 
 P = 128
@@ -28,20 +29,21 @@ TOKEN_BLOCKS = T // P
 HALF = T // 2
 
 CHUNKS = [(0, 512), (512, 512), (1024, 512), (1536, 384), (1920, 256), (2176, 128)]
-GATE_LOADS = [(0, 512), (512, 512), (1024, 1280)]
+GATE_LOADS = [(0, 256), (256, 256), (512, 512), (1024, 1280)]
 
 
 def tile_moe_pre_lin_relu_kernel(tc, xT, w_words, w_scales, b, gate, offs, pos1, pos2, pos3, out):
     nc = tc.nc
     with ExitStack() as ctx:
         keep = ctx.enter_context(tc.tile_pool(name="keep", bufs=1))
+        ring = ctx.enter_context(tc.tile_pool(name="ring", bufs=2))
         psum_a = ctx.enter_context(tc.psum_pool(name="psum_a", bufs=2))
         psum_b = ctx.enter_context(tc.psum_pool(name="psum_b", bufs=6))
 
         offs_sb = keep.tile([P, S // 16], U16, name="offs_sb")
         pos_sb = [keep.tile([P, T // 16], U16, name="pos_sb%d" % r) for r in range(3)]
         planes = [keep.tile([P, T], F32, name="plane%d" % j, align_bytes=64) for j in range(PACK)]
-        gates = [keep.tile([P, n], F32, name="gate%d" % i, align_bytes=64) for i, (s0, n) in enumerate(GATE_LOADS)]
+        gate_sb = keep.tile([P, S], F32, name="gate_sb", align_bytes=64)
         w_sb = keep.tile([P, E, 2 * N], U8, name="w_sb", align_bytes=64)
         ws_sb = keep.tile([P, E, N], U8, name="ws_sb", align_bytes=64)
         b_sb = keep.tile([P, ROW_TILES, E], F32, name="b_sb", align_bytes=64)
@@ -51,46 +53,50 @@ def tile_moe_pre_lin_relu_kernel(tc, xT, w_words, w_scales, b, gate, offs, pos1,
         x_scales = keep.tile([P, S], U8, name="x_scales", align_bytes=64)
         ys = [keep.tile([P, S], F32, name="y%d" % r, align_bytes=64) for r in range(ROW_TILES)]
 
-        nc.vector.memset(ws_sb[:].rearrange("p e n -> p (e n)").bitcast(I32), 0)
         make_identity(nc, ident[:])
+        nc.gpsimd.memset(ws_sb[:].rearrange("p e n -> p (e n)").bitcast(I32), 0)
 
         x_rows = xT.rearrange("(p j) t -> p j t", j=PACK)
 
         def load_gate(i):
             s0, n = GATE_LOADS[i]
-            nc.sync.dma_start(gates[i][:], gate[0:P, s0:s0 + n])
+            nc.sync.dma_start(gate_sb[:, s0:s0 + n], gate[0:P, s0:s0 + n])
 
         nc.sync.dma_start(offs_sb[:], offs)
         nc.sync.dma_start(planes[0][:], x_rows[:, 0, :])
         load_gate(0)
+        load_gate(1)
         for j in range(1, PACK):
             nc.sync.dma_start(planes[j][:], x_rows[:, j, :])
-        load_gate(1)
-        scale_rows = w_scales.rearrange("e a q n -> q (e a) n").bitcast(I32)
-        for q in range(4):
-            nc.sync.dma_start(ws_sb[32 * q:32 * q + 4, :, :].bitcast(I32), scale_rows[4 * q:4 * q + 4, :, :])
-        nc.sync.dma_start(w_sb[:].bitcast(I32), w_words.rearrange("e a p n -> p (e a) n").bitcast(I32))
-        nc.sync.dma_start(b_sb[:], b.rearrange("(r p) e -> p r e", p=P))
         load_gate(2)
+        nc.sync.dma_start(b_sb[:], b.rearrange("(r p) e -> p r e", p=P))
+        load_gate(3)
+        scale_rows = w_scales.rearrange("e a q n -> q (e a) n").bitcast(I32)
+        for e0, e1 in ((0, 4), (4, E)):
+            for q in range(4):
+                nc.gpsimd.dma_start(ws_sb[32 * q:32 * q + 4, e0:e1, :].bitcast(I32), scale_rows[4 * q:4 * q + 4, e0:e1, :])
+        word_rows = w_words.rearrange("e a p n -> p (e a) n").bitcast(I32)
+
+        def load_words(e0, e1):
+            nc.sync.dma_start(w_sb[:, e0:e1, :].bitcast(I32), word_rows[:, e0:e1, :])
+
+        load_words(0, 4)
+        load_words(4, E)
         for r, pos in enumerate((pos1, pos2, pos3)):
             nc.sync.dma_start(pos_sb[r][:], pos)
 
-        def gate_cols(s0, n):
-            for i, (g0, gn) in enumerate(GATE_LOADS):
-                if g0 <= s0 and s0 + n <= g0 + gn:
-                    return gates[i][:, s0 - g0:s0 - g0 + n]
-            raise ValueError("no gate tile")
-
         def gather_chunk(c):
             s0, n = CHUNKS[c]
-            gathered = keep.tile([P, PACK, n], F32, name="gathered%d" % c, align_bytes=64)
+            gathered = ring.tile([P, PACK, n], F32, name="gathered", align_bytes=64)
             for j in range(PACK):
-                nc.vector.tensor_tensor(
-                    gathered[:, j, :],
-                    planes[j][:].indirect(offs_sb[:, s0 // 16:(s0 + n) // 16]),
-                    gate_cols(s0, n),
-                    MULT,
-                )
+                step = GATE_LOADS[0][1] if (c, j) == (0, 0) else n
+                for at in range(0, n, step):
+                    nc.vector.tensor_tensor(
+                        gathered[:, j, at:at + step],
+                        planes[j][:].indirect(offs_sb[:, (s0 + at) // 16:(s0 + at + step) // 16]),
+                        gate_sb[:, s0 + at:s0 + at + step],
+                        MULT,
+                    )
             nc.scalar.copy(
                 x_bf[:, PACK * s0:PACK * (s0 + n)].rearrange("p (c i t) -> p c t i", i=4, t=PACK),
                 gathered[:].rearrange("p t (c i) -> p c t i", i=4),
@@ -103,7 +109,7 @@ def tile_moe_pre_lin_relu_kernel(tc, xT, w_words, w_scales, b, gate, offs, pos1,
                 in_=x_bf[:, PACK * s0:PACK * (s0 + n)],
             )
 
-        def experts(r, pieces, pool):
+        def experts(r, pieces, pool, on_vector=False):
             bank = pool.tile([P, BANK], F32, name="bank")
             at = 0
             for s0, n in pieces:
@@ -121,72 +127,83 @@ def tile_moe_pre_lin_relu_kernel(tc, xT, w_words, w_scales, b, gate, offs, pos1,
             at = 0
             for s0, n in pieces:
                 e = s0 // C
-                nc.scalar.activation(ys[r][:, s0:s0 + n], bank[:, at:at + n], RELU, bias=b_sb[:, r, e:e + 1])
+                if on_vector:
+                    nc.vector.tensor_scalar(ys[r][:, s0:s0 + n], bank[:, at:at + n], b_sb[:, r, e:e + 1], 0.0, ADD, MAX)
+                else:
+                    nc.scalar.activation(ys[r][:, s0:s0 + n], bank[:, at:at + n], RELU, bias=b_sb[:, r, e:e + 1])
                 at += n
 
         gather_chunk(0)
         gather_chunk(1)
         quantize(0, 512)
-        experts(0, [(0, C), (C, C)], psum_a)
+        for r in range(ROW_TILES):
+            experts(r, [(0, C), (C, C)], psum_b if r else psum_a)
         gather_chunk(2)
         quantize(512, 512)
-        experts(0, [(2 * C, C), (3 * C, C)], psum_a)
+        for r in range(ROW_TILES):
+            experts(r, [(2 * C, C), (3 * C, C)], psum_b if r else psum_a)
         gather_chunk(3)
-        gather_chunk(4)
         quantize(1024, 512)
         experts(0, [(4 * C, C), (5 * C, C)], psum_a)
+        gather_chunk(4)
         gather_chunk(5)
         quantize(1536, 256)
         experts(0, [(6 * C, C)], psum_a)
         quantize(1792, 128)
         quantize(1920, 256)
-        experts(0, [(7 * C, C), (8 * C, 128)], psum_a)
+        experts(0, [(7 * C, C)], psum_a)
         quantize(2176, 128)
-        experts(0, [(2176, 128)], psum_a)
+        experts(0, [(8 * C, 128)], psum_b, True)
+        experts(0, [(2176, 128)], psum_b, True)
         for r in range(1, ROW_TILES):
-            for e0 in range(0, E, 2):
+            for e0 in range(4, E, 2):
                 experts(r, [(e * C, C) for e in range(e0, min(e0 + 2, E))], psum_b)
 
-        def fetch(r, l, t0, n):
-            picked = keep.tile([P, n], F32, name="picked%d_%d_%d" % (r, l, t0), align_bytes=64)
-            nc.vector.tensor_copy(picked[:], ys[r][:].indirect(pos_sb[l][:, t0 // 16:(t0 + n) // 16]))
+        picks = {}
+
+        def fetch(r, l, t0, n, into):
+            if into not in picks:
+                picks[into] = keep.tile([P, T], F32, name="picked%d_%d" % into, align_bytes=64)
+            picked = picks[into][:, t0:t0 + n]
+            nc.vector.tensor_copy(picked, ys[r][:].indirect(pos_sb[l][:, t0 // 16:(t0 + n) // 16]))
             return picked
 
-        def tensor_sum(r, lists):
+        def tensor_sum(r, fetches):
             sums = [psum_b.tile([P, BANK], F32, name="bank") for blk in range(TOKEN_BLOCKS)]
-            for l in lists:
-                picked = fetch(r, l, 0, T)
-                for blk in range(TOKEN_BLOCKS):
+            last = fetches[-1][0]
+            for l, t0, n in fetches:
+                picked = fetch(r, l, t0, n, (r, l))
+                for at in range(0, n, P):
                     nc.tensor.matmul(
-                        sums[blk][:, 0:P],
-                        lhsT=picked[:, blk * P:(blk + 1) * P],
+                        sums[(t0 + at) // P][:, 0:P],
+                        lhsT=picked[:, at:at + P],
                         rhs=ident[:],
-                        start=(l == lists[0]),
-                        stop=(l == lists[-1]),
+                        start=(l == 0),
+                        stop=(l == last),
                         is_transpose=True,
                     )
             turned = keep.tile([P, T], F32, name="turned%d" % r, align_bytes=64)
             total = keep.tile([P, T], F32, name="total%d" % r, align_bytes=64)
+            backs = [psum_a.tile([P, BANK], F32, name="bank") for h in range(2)]
+            for blk in range(TOKEN_BLOCKS):
+                h, i = divmod(blk, 3)
+                nc.scalar.copy(turned[:, blk * P:(blk + 1) * P], sums[blk][:, 0:P])
+                nc.tensor.transpose(backs[h][:, i * P:(i + 1) * P], turned[:, blk * P:(blk + 1) * P], ident[:])
             for h in range(2):
-                back = psum_a.tile([P, BANK], F32, name="bank")
-                for i in range(3):
-                    blk = 3 * h + i
-                    nc.scalar.copy(turned[:, blk * P:(blk + 1) * P], sums[blk][:, 0:P])
-                    nc.tensor.transpose(back[:, i * P:(i + 1) * P], turned[:, blk * P:(blk + 1) * P], ident[:])
-                nc.scalar.copy(total[:, h * HALF:(h + 1) * HALF], back[:, 0:HALF])
+                nc.scalar.copy(total[:, h * HALF:(h + 1) * HALF], backs[h][:, 0:HALF])
             return total
 
         def store(r, t0, n, src):
             nc.sync.dma_start(out[r * P:(r + 1) * P, t0:t0 + n], src)
 
-        total0 = tensor_sum(0, [0, 1, 2])
+        total0 = tensor_sum(0, [(0, 0, T), (1, 0, T), (2, 0, T)])
         store(0, 0, T, total0[:])
-        partial1 = tensor_sum(1, [0, 1])
-        total2 = tensor_sum(2, [0, 1, 2])
+        partial1 = tensor_sum(1, [(0, 0, T), (1, 0, T)])
+        total2 = tensor_sum(2, [(0, 0, T), (1, 0, T), (2, 0, HALF), (2, HALF, HALF)])
         for h in range(2):
             store(2, h * HALF, HALF, total2[:, h * HALF:(h + 1) * HALF])
-        lasts = [fetch(1, 2, h * HALF, HALF) for h in range(2)]
+        lasts = [fetch(1, 2, h * HALF, HALF, (2, 1)) for h in range(2)]
         for h in range(2):
             total1 = keep.tile([P, HALF], F32, name="total1_%d" % h, align_bytes=64)
-            nc.vector.tensor_tensor(total1[:], lasts[h][:], partial1[:, h * HALF:(h + 1) * HALF], ADD)
+            nc.vector.tensor_tensor(total1[:], lasts[h], partial1[:, h * HALF:(h + 1) * HALF], ADD)
             store(1, h * HALF, HALF, total1[:])

@@ -28,8 +28,8 @@ ROW_TILES = N // P
 TOKEN_BLOCKS = T // P
 HALF = T // 2
 
-CHUNKS = [(0, 512), (512, 512), (1024, 512), (1536, 384), (1920, 256), (2176, 128)]
-GATE_LOADS = [(0, 256), (256, 256), (512, 512), (1024, 1280)]
+CHUNKS = [(0, 640), (640, 512), (1152, 384), (1536, 384), (1920, 256), (2176, 128)]
+GATE_LOADS = [(0, 256), (256, 384), (640, 512), (1152, 1152)]
 
 
 def tile_moe_pre_lin_relu_kernel(tc, xT, w_words, w_scales, b, gate, offs, pos1, pos2, pos3, out):
@@ -72,9 +72,12 @@ def tile_moe_pre_lin_relu_kernel(tc, xT, w_words, w_scales, b, gate, offs, pos1,
         nc.sync.dma_start(b_sb[:], b.rearrange("(r p) e -> p r e", p=P))
         load_gate(3)
         scale_rows = w_scales.rearrange("e a q n -> q (e a) n").bitcast(I32)
-        for e0, e1 in ((0, 4), (4, E)):
+
+        def load_scales(queue, e0, e1):
             for q in range(4):
-                nc.gpsimd.dma_start(ws_sb[32 * q:32 * q + 4, e0:e1, :].bitcast(I32), scale_rows[4 * q:4 * q + 4, e0:e1, :])
+                queue.dma_start(ws_sb[32 * q:32 * q + 4, e0:e1, :].bitcast(I32), scale_rows[4 * q:4 * q + 4, e0:e1, :])
+
+        load_scales(nc.gpsimd, 0, 4)
         word_rows = w_words.rearrange("e a p n -> p (e a) n").bitcast(I32)
 
         def load_words(e0, e1):
@@ -82,6 +85,7 @@ def tile_moe_pre_lin_relu_kernel(tc, xT, w_words, w_scales, b, gate, offs, pos1,
 
         load_words(0, 4)
         load_words(4, E)
+        load_scales(nc.sync, 4, E)
         for r, pos in enumerate((pos1, pos2, pos3)):
             nc.sync.dma_start(pos_sb[r][:], pos)
 
@@ -89,8 +93,8 @@ def tile_moe_pre_lin_relu_kernel(tc, xT, w_words, w_scales, b, gate, offs, pos1,
             s0, n = CHUNKS[c]
             gathered = ring.tile([P, PACK, n], F32, name="gathered", align_bytes=64)
             for j in range(PACK):
-                step = GATE_LOADS[0][1] if (c, j) == (0, 0) else n
-                for at in range(0, n, step):
+                cuts = GATE_LOADS[0:2] if (c, j) == (0, 0) else [(0, n)]
+                for at, step in cuts:
                     nc.vector.tensor_tensor(
                         gathered[:, j, at:at + step],
                         planes[j][:].indirect(offs_sb[:, (s0 + at) // 16:(s0 + at + step) // 16]),
@@ -202,8 +206,9 @@ def tile_moe_pre_lin_relu_kernel(tc, xT, w_words, w_scales, b, gate, offs, pos1,
         total2 = tensor_sum(2, [(0, 0, T), (1, 0, T), (2, 0, HALF), (2, HALF, HALF)])
         for h in range(2):
             store(2, h * HALF, HALF, total2[:, h * HALF:(h + 1) * HALF])
-        lasts = [fetch(1, 2, h * HALF, HALF, (2, 1)) for h in range(2)]
-        for h in range(2):
-            total1 = keep.tile([P, HALF], F32, name="total1_%d" % h, align_bytes=64)
-            nc.vector.tensor_tensor(total1[:], lasts[h], partial1[:, h * HALF:(h + 1) * HALF], ADD)
-            store(1, h * HALF, HALF, total1[:])
+        ends = [(0, 480), (480, 288)]
+        lasts = [fetch(1, 2, t0, n, (2, 1)) for t0, n in ends]
+        for h, (t0, n) in enumerate(ends):
+            total1 = keep.tile([P, n], F32, name="total1_%d" % h, align_bytes=64)
+            nc.vector.tensor_tensor(total1[:], lasts[h], partial1[:, t0:t0 + n], ADD)
+            store(1, t0, n, total1[:])

@@ -163,20 +163,16 @@ def tile_moe_pre_lin_relu_kernel(tc, xT, w_words, w_scales, b, gate, offs, pos1,
             for e0 in range(4, E, 2):
                 experts(r, [(e * C, C) for e in range(e0, min(e0 + 2, E))], psum_b)
 
-        picks = {}
-
-        def fetch(r, l, t0, n, into):
-            if into not in picks:
-                picks[into] = keep.tile([P, T], F32, name="picked%d_%d" % into, align_bytes=64)
-            picked = picks[into][:, t0:t0 + n]
-            nc.vector.tensor_copy(picked, ys[r][:].indirect(pos_sb[l][:, t0 // 16:(t0 + n) // 16]))
+        def fetch(r, l, t0, n):
+            picked = keep.tile([P, n], F32, name="picked%d_%d_%d" % (r, l, t0), align_bytes=64)
+            nc.vector.tensor_copy(picked[:], ys[r][:].indirect(pos_sb[l][:, t0 // 16:(t0 + n) // 16]))
             return picked
 
         def tensor_sum(r, fetches):
             sums = [psum_b.tile([P, BANK], F32, name="bank") for blk in range(TOKEN_BLOCKS)]
             last = fetches[-1][0]
             for l, t0, n in fetches:
-                picked = fetch(r, l, t0, n, (r, l))
+                picked = fetch(r, l, t0, n)
                 for at in range(0, n, P):
                     nc.tensor.matmul(
                         sums[(t0 + at) // P][:, 0:P],
@@ -187,28 +183,23 @@ def tile_moe_pre_lin_relu_kernel(tc, xT, w_words, w_scales, b, gate, offs, pos1,
                         is_transpose=True,
                     )
             turned = keep.tile([P, T], F32, name="turned%d" % r, align_bytes=64)
-            total = keep.tile([P, T], F32, name="total%d" % r, align_bytes=64)
             backs = [psum_a.tile([P, BANK], F32, name="bank") for h in range(2)]
             for blk in range(TOKEN_BLOCKS):
                 h, i = divmod(blk, 3)
                 nc.scalar.copy(turned[:, blk * P:(blk + 1) * P], sums[blk][:, 0:P])
                 nc.tensor.transpose(backs[h][:, i * P:(i + 1) * P], turned[:, blk * P:(blk + 1) * P], ident[:])
+            return backs
+
+        for r in range(ROW_TILES - 1):
+            backs = tensor_sum(r, [(0, 0, T), (1, 0, T), (2, 0, T)])
+            total = keep.tile([P, T], F32, name="total%d" % r, align_bytes=64)
             for h in range(2):
                 nc.scalar.copy(total[:, h * HALF:(h + 1) * HALF], backs[h][:, 0:HALF])
-            return total
-
-        def store(r, t0, n, src):
-            nc.sync.dma_start(out[r * P:(r + 1) * P, t0:t0 + n], src)
-
-        total0 = tensor_sum(0, [(0, 0, T), (1, 0, T), (2, 0, T)])
-        store(0, 0, T, total0[:])
-        partial1 = tensor_sum(1, [(0, 0, T), (1, 0, T)])
-        total2 = tensor_sum(2, [(0, 0, T), (1, 0, T), (2, 0, HALF), (2, HALF, HALF)])
+            nc.sync.dma_start(out[r * P:(r + 1) * P, :], total[:])
+        r = ROW_TILES - 1
+        backs = tensor_sum(r, [(0, 0, T), (1, 0, HALF), (1, HALF, HALF)])
+        lasts = [fetch(r, 2, h * HALF, HALF) for h in range(2)]
         for h in range(2):
-            store(2, h * HALF, HALF, total2[:, h * HALF:(h + 1) * HALF])
-        ends = [(0, 480), (480, 288)]
-        lasts = [fetch(1, 2, t0, n, (2, 1)) for t0, n in ends]
-        for h, (t0, n) in enumerate(ends):
-            total1 = keep.tile([P, n], F32, name="total1_%d" % h, align_bytes=64)
-            nc.vector.tensor_tensor(total1[:], lasts[h], partial1[:, t0:t0 + n], ADD)
-            store(1, t0, n, total1[:])
+            total = keep.tile([P, HALF], F32, name="last_total%d" % h, align_bytes=64)
+            nc.vector.tensor_tensor(total[:], lasts[h][:], backs[h][:, 0:HALF], ADD)
+            nc.sync.dma_start(out[r * P:(r + 1) * P, h * HALF:(h + 1) * HALF], total[:])

@@ -1,7 +1,6 @@
 from contextlib import ExitStack
 
 import concourse.mybir as mybir
-from concourse.masks import make_identity
 
 K, T, E, C, N = 512, 768, 9, 256, 384
 S = E * C
@@ -25,20 +24,19 @@ P = 128
 PACK = 4
 BANK = 512
 ROW_TILES = N // P
-TOKEN_BLOCKS = T // P
-HALF = T // 2
 
-CHUNKS = [(0, 640), (640, 512), (1152, 384), (1536, 384), (1920, 256), (2176, 128)]
-GATE_LOADS = [(0, 256), (256, 384), (640, 512), (1152, 1152)]
+CHUNKS = [(0, 704), (704, 736), (1440, 448), (1888, 288), (2176, 128)]
+STAGE_AT = [0, 2048, 0, 2048, 0]
+STAGE = 2048 + 4 * 736
+GATE_LOADS = [(0, 224), (224, 480), (704, 736), (1440, 864)]
 
 
 def tile_moe_pre_lin_relu_kernel(tc, xT, w_words, w_scales, b, gate, offs, pos1, pos2, pos3, out):
     nc = tc.nc
     with ExitStack() as ctx:
         keep = ctx.enter_context(tc.tile_pool(name="keep", bufs=1))
-        ring = ctx.enter_context(tc.tile_pool(name="ring", bufs=2))
-        psum_a = ctx.enter_context(tc.psum_pool(name="psum_a", bufs=2))
-        psum_b = ctx.enter_context(tc.psum_pool(name="psum_b", bufs=6))
+        psum_a = ctx.enter_context(tc.psum_pool(name="psum_a", bufs=4))
+        psum_b = ctx.enter_context(tc.psum_pool(name="psum_b", bufs=4))
 
         offs_sb = keep.tile([P, S // 16], U16, name="offs_sb")
         pos_sb = [keep.tile([P, T // 16], U16, name="pos_sb%d" % r) for r in range(3)]
@@ -46,14 +44,14 @@ def tile_moe_pre_lin_relu_kernel(tc, xT, w_words, w_scales, b, gate, offs, pos1,
         gate_sb = keep.tile([P, S], F32, name="gate_sb", align_bytes=64)
         w_sb = keep.tile([P, E, 2 * N], U8, name="w_sb", align_bytes=64)
         ws_sb = keep.tile([P, E, N], U8, name="ws_sb", align_bytes=64)
-        b_sb = keep.tile([P, ROW_TILES, E], F32, name="b_sb", align_bytes=64)
-        ident = keep.tile([P, P], F32, name="ident", align_bytes=64)
+        stage = keep.tile([P, STAGE], F32, name="stage", align_bytes=64)
         x_bf = keep.tile([P, S * PACK], BF16, name="x_bf", align_bytes=64)
         x_codes = keep.tile([P, S], U32, name="x_codes", align_bytes=64)
         x_scales = keep.tile([P, S], U8, name="x_scales", align_bytes=64)
         ys = [keep.tile([P, S], F32, name="y%d" % r, align_bytes=64) for r in range(ROW_TILES)]
+        sums = [[keep.tile([P, T], F32, name="sum%d_%d" % (r, l), align_bytes=64) for l in range(3)] for r in range(ROW_TILES)]
+        bias = [sums[0][r][:, 0:E] for r in range(ROW_TILES)]
 
-        make_identity(nc, ident[:])
         nc.gpsimd.memset(ws_sb[:].rearrange("p e n -> p (e n)").bitcast(I32), 0)
 
         x_rows = xT.rearrange("(p j) t -> p j t", j=PACK)
@@ -69,7 +67,6 @@ def tile_moe_pre_lin_relu_kernel(tc, xT, w_words, w_scales, b, gate, offs, pos1,
         for j in range(1, PACK):
             nc.sync.dma_start(planes[j][:], x_rows[:, j, :])
         load_gate(2)
-        nc.sync.dma_start(b_sb[:], b.rearrange("(r p) e -> p r e", p=P))
         load_gate(3)
         scale_rows = w_scales.rearrange("e a q n -> q (e a) n").bitcast(I32)
 
@@ -77,33 +74,38 @@ def tile_moe_pre_lin_relu_kernel(tc, xT, w_words, w_scales, b, gate, offs, pos1,
             for q in range(4):
                 queue.dma_start(ws_sb[32 * q:32 * q + 4, e0:e1, :].bitcast(I32), scale_rows[4 * q:4 * q + 4, e0:e1, :])
 
-        load_scales(nc.gpsimd, 0, 4)
+        load_scales(nc.gpsimd, 0, 5)
         word_rows = w_words.rearrange("e a p n -> p (e a) n").bitcast(I32)
 
         def load_words(e0, e1):
             nc.sync.dma_start(w_sb[:, e0:e1, :].bitcast(I32), word_rows[:, e0:e1, :])
 
-        load_words(0, 4)
-        load_words(4, E)
-        load_scales(nc.sync, 4, E)
+        load_words(0, 2)
+        for r in range(ROW_TILES):
+            nc.sync.dma_start(bias[r], b[r * P:(r + 1) * P, :])
+        load_words(2, E)
+        load_scales(nc.sync, 5, E)
         for r, pos in enumerate((pos1, pos2, pos3)):
             nc.sync.dma_start(pos_sb[r][:], pos)
 
-        def gather_chunk(c):
+        def gather(c, order):
             s0, n = CHUNKS[c]
-            gathered = ring.tile([P, PACK, n], F32, name="gathered", align_bytes=64)
-            for j in range(PACK):
+            for j in order:
                 cuts = GATE_LOADS[0:2] if (c, j) == (0, 0) else [(0, n)]
                 for at, step in cuts:
+                    to = STAGE_AT[c] + j * n + at
                     nc.vector.tensor_tensor(
-                        gathered[:, j, at:at + step],
+                        stage[:, to:to + step],
                         planes[j][:].indirect(offs_sb[:, (s0 + at) // 16:(s0 + at + step) // 16]),
                         gate_sb[:, s0 + at:s0 + at + step],
                         MULT,
                     )
+
+        def weave(c):
+            s0, n = CHUNKS[c]
             nc.scalar.copy(
                 x_bf[:, PACK * s0:PACK * (s0 + n)].rearrange("p (c i t) -> p c t i", i=4, t=PACK),
-                gathered[:].rearrange("p t (c i) -> p c t i", i=4),
+                stage[:, STAGE_AT[c]:STAGE_AT[c] + PACK * n].rearrange("p (t c i) -> p c t i", t=PACK, i=4),
             )
 
         def quantize(s0, n):
@@ -113,93 +115,84 @@ def tile_moe_pre_lin_relu_kernel(tc, xT, w_words, w_scales, b, gate, offs, pos1,
                 in_=x_bf[:, PACK * s0:PACK * (s0 + n)],
             )
 
-        def experts(r, pieces, pool, on_vector=False):
-            bank = pool.tile([P, BANK], F32, name="bank")
-            at = 0
-            for s0, n in pieces:
-                e = s0 // C
-                nc.tensor.matmul_mx(
-                    out=bank[:, at:at + n],
-                    lhsT=w_sb[:, e, 2 * P * r:2 * P * (r + 1)].bitcast(FP4X4),
-                    lhsT_scale=ws_sb[:, e, P * r:P * (r + 1)],
-                    rhs=x_codes[:, s0:s0 + n].bitcast(FP8X4),
-                    rhs_scale=x_scales[:, s0:s0 + n],
-                    start=True,
-                    stop=True,
-                )
-                at += n
-            at = 0
-            for s0, n in pieces:
-                e = s0 // C
-                if on_vector:
-                    nc.vector.tensor_scalar(ys[r][:, s0:s0 + n], bank[:, at:at + n], b_sb[:, r, e:e + 1], 0.0, ADD, MAX)
-                else:
-                    nc.scalar.activation(ys[r][:, s0:s0 + n], bank[:, at:at + n], RELU, bias=b_sb[:, r, e:e + 1])
-                at += n
+        def multiply(bank, at, r, s0, n):
+            e = s0 // C
+            nc.tensor.matmul_mx(
+                out=bank[:, at:at + n],
+                lhsT=w_sb[:, e, 2 * P * r:2 * P * (r + 1)].bitcast(FP4X4),
+                lhsT_scale=ws_sb[:, e, P * r:P * (r + 1)],
+                rhs=x_codes[:, s0:s0 + n].bitcast(FP8X4),
+                rhs_scale=x_scales[:, s0:s0 + n],
+                start=True,
+                stop=True,
+            )
 
-        gather_chunk(0)
-        gather_chunk(1)
+        def relu(bank, at, r, s0, n, on_vector=False):
+            e = s0 // C
+            if on_vector:
+                nc.vector.tensor_scalar(ys[r][:, s0:s0 + n], bank[:, at:at + n], bias[r][:, e:e + 1], 0.0, ADD, MAX)
+            else:
+                nc.scalar.activation(ys[r][:, s0:s0 + n], bank[:, at:at + n], RELU, bias=bias[r][:, e:e + 1])
+
+        def experts(pool, r, *es):
+            bank = pool.tile([P, BANK], F32, name="bank")
+            for i, e in enumerate(es):
+                multiply(bank, i * C, r, e * C, C)
+            for i, e in enumerate(es):
+                relu(bank, i * C, r, e * C, C)
+
+        gather(0, (0, 1, 2, 3))
+        weave(0)
+        gather(1, (3, 2))
         quantize(0, 512)
         for r in range(ROW_TILES):
-            experts(r, [(0, C), (C, C)], psum_b if r else psum_a)
-        gather_chunk(2)
+            for e in (0, 1):
+                experts(psum_b if r else psum_a, r, e)
+        gather(1, (1, 0))
+        weave(1)
+        gather(2, (0, 1, 2, 3))
+        weave(2)
         quantize(512, 512)
-        for r in range(ROW_TILES):
-            experts(r, [(2 * C, C), (3 * C, C)], psum_b if r else psum_a)
-        gather_chunk(3)
+        experts(psum_a, 0, 2)
+        experts(psum_a, 0, 3)
+        experts(psum_b, 1, 2)
+        experts(psum_b, 1, 3)
+        gather(3, (0, 1, 2, 3))
+        weave(3)
         quantize(1024, 512)
-        experts(0, [(4 * C, C), (5 * C, C)], psum_a)
-        gather_chunk(4)
-        gather_chunk(5)
+        experts(psum_a, 0, 4)
+        gather(4, (0, 1, 2, 3))
+        weave(4)
+        experts(psum_a, 0, 5)
         quantize(1536, 256)
-        experts(0, [(6 * C, C)], psum_a)
-        quantize(1792, 128)
-        quantize(1920, 256)
-        experts(0, [(7 * C, C)], psum_a)
-        quantize(2176, 128)
-        experts(0, [(8 * C, 128)], psum_b, True)
-        experts(0, [(2176, 128)], psum_b, True)
-        for r in range(1, ROW_TILES):
-            for e0 in range(4, E, 2):
-                experts(r, [(e * C, C) for e in range(e0, min(e0 + 2, E))], psum_b)
+        experts(psum_a, 0, 6)
+        quantize(1792, 256)
+        experts(psum_a, 0, 7)
+        lasts = [psum_b.tile([P, BANK], F32, name="bank") for h in range(2)]
+        for h in range(2):
+            multiply(lasts[h], 0, 1, (4 + h) * C, C)
+        for h in range(2):
+            quantize(8 * C + h * P, P)
+            multiply(lasts[h], C, 0, 8 * C + h * P, P)
+            relu(lasts[h], C, 0, 8 * C + h * P, P, True)
+        for h in range(2):
+            relu(lasts[h], 0, 1, (4 + h) * C, C)
+        experts(psum_a, 1, 8)
+        experts(psum_a, 1, 6, 7)
+        for e0 in range(2, E, 2):
+            experts(psum_a, 2, *range(e0, min(e0 + 2, E)))
 
         def fetch(r, l, t0, n):
-            picked = keep.tile([P, n], F32, name="picked%d_%d_%d" % (r, l, t0), align_bytes=64)
-            nc.vector.tensor_copy(picked[:], ys[r][:].indirect(pos_sb[l][:, t0 // 16:(t0 + n) // 16]))
-            return picked
+            found = ys[r][:].indirect(pos_sb[l][:, t0 // 16:(t0 + n) // 16])
+            if l == 0:
+                nc.vector.tensor_copy(sums[r][l][:, t0:t0 + n], found)
+            else:
+                nc.vector.tensor_tensor(sums[r][l][:, t0:t0 + n], found, sums[r][l - 1][:, t0:t0 + n], ADD)
+            if l == 2:
+                nc.sync.dma_start(out[r * P:(r + 1) * P, t0:t0 + n], sums[r][l][:, t0:t0 + n])
 
-        def tensor_sum(r, fetches):
-            sums = [psum_b.tile([P, BANK], F32, name="bank") for blk in range(TOKEN_BLOCKS)]
-            last = fetches[-1][0]
-            for l, t0, n in fetches:
-                picked = fetch(r, l, t0, n)
-                for at in range(0, n, P):
-                    nc.tensor.matmul(
-                        sums[(t0 + at) // P][:, 0:P],
-                        lhsT=picked[:, at:at + P],
-                        rhs=ident[:],
-                        start=(l == 0),
-                        stop=(l == last),
-                        is_transpose=True,
-                    )
-            turned = keep.tile([P, T], F32, name="turned%d" % r, align_bytes=64)
-            backs = [psum_a.tile([P, BANK], F32, name="bank") for h in range(2)]
-            for blk in range(TOKEN_BLOCKS):
-                h, i = divmod(blk, 3)
-                nc.scalar.copy(turned[:, blk * P:(blk + 1) * P], sums[blk][:, 0:P])
-                nc.tensor.transpose(backs[h][:, i * P:(i + 1) * P], turned[:, blk * P:(blk + 1) * P], ident[:])
-            return backs
-
-        for r in range(ROW_TILES - 1):
-            backs = tensor_sum(r, [(0, 0, T), (1, 0, T), (2, 0, T)])
-            total = keep.tile([P, T], F32, name="total%d" % r, align_bytes=64)
-            for h in range(2):
-                nc.scalar.copy(total[:, h * HALF:(h + 1) * HALF], backs[h][:, 0:HALF])
-            nc.sync.dma_start(out[r * P:(r + 1) * P, :], total[:])
-        r = ROW_TILES - 1
-        backs = tensor_sum(r, [(0, 0, T), (1, 0, HALF), (1, HALF, HALF)])
-        lasts = [fetch(r, 2, h * HALF, HALF) for h in range(2)]
-        for h in range(2):
-            total = keep.tile([P, HALF], F32, name="last_total%d" % h, align_bytes=64)
-            nc.vector.tensor_tensor(total[:], lasts[h][:], backs[h][:, 0:HALF], ADD)
-            nc.sync.dma_start(out[r * P:(r + 1) * P, h * HALF:(h + 1) * HALF], total[:])
+        for r, l in ((0, 0), (1, 0), (0, 1), (1, 1), (2, 0), (0, 2), (2, 1), (1, 2)):
+            fetch(r, l, 0, T)
+        fetch(2, 2, 0, 512)
+        fetch(2, 2, 512, 128)
+        fetch(2, 2, 640, 128)

@@ -67,24 +67,23 @@ def tile_moe_pre_lin_relu_kernel(tc, xT, w_words, w_scales, b, gate, offs, pos1,
         for j in range(1, PACK):
             nc.sync.dma_start(planes[j][:], x_rows[:, j, :])
         load_gate(2)
-        load_gate(3)
         scale_rows = w_scales.rearrange("e a q n -> q (e a) n").bitcast(I32)
-
-        def load_scales(queue, e0, e1):
-            for q in range(4):
-                queue.dma_start(ws_sb[32 * q:32 * q + 4, e0:e1, :].bitcast(I32), scale_rows[4 * q:4 * q + 4, e0:e1, :])
-
-        load_scales(nc.gpsimd, 0, 5)
         word_rows = w_words.rearrange("e a p n -> p (e a) n").bitcast(I32)
+
+        def load_scales(e0, e1):
+            for q in range(4):
+                nc.sync.dma_start(ws_sb[32 * q:32 * q + 4, e0:e1, :].bitcast(I32), scale_rows[4 * q:4 * q + 4, e0:e1, :])
 
         def load_words(e0, e1):
             nc.sync.dma_start(w_sb[:, e0:e1, :].bitcast(I32), word_rows[:, e0:e1, :])
 
+        load_scales(0, 4)
         load_words(0, 2)
         for r in range(ROW_TILES):
             nc.sync.dma_start(bias[r], b[r * P:(r + 1) * P, :])
+        load_gate(3)
         load_words(2, E)
-        load_scales(nc.sync, 5, E)
+        load_scales(4, E)
         for r, pos in enumerate((pos1, pos2, pos3)):
             nc.sync.dma_start(pos_sb[r][:], pos)
 
@@ -174,7 +173,7 @@ def tile_moe_pre_lin_relu_kernel(tc, xT, w_words, w_scales, b, gate, offs, pos1,
         for h in range(2):
             quantize(8 * C + h * P, P)
             multiply(lasts[h], C, 0, 8 * C + h * P, P)
-            relu(lasts[h], C, 0, 8 * C + h * P, P, True)
+            relu(lasts[h], C, 0, 8 * C + h * P, P, h == 0)
         for h in range(2):
             relu(lasts[h], 0, 1, (4 + h) * C, C)
         experts(psum_a, 1, 8)

@@ -28,7 +28,7 @@ ROW_TILES = N // P
 CHUNKS = [(0, 704), (704, 736), (1440, 448), (1888, 288), (2176, 128)]
 STAGE_AT = [0, 2048, 0, 2048, 0]
 STAGE = 2048 + 4 * 736
-GATE_LOADS = [(0, 224), (224, 480), (704, 736), (1440, 864)]
+GATE_LOADS = [(0, 256), (256, 448), (704, 736), (1440, 864)]
 
 
 def tile_moe_pre_lin_relu_kernel(tc, xT, w_words, w_scales, b, gate, offs, pos1, pos2, pos3, out):
@@ -192,6 +192,6 @@ def tile_moe_pre_lin_relu_kernel(tc, xT, w_words, w_scales, b, gate, offs, pos1,
 
         for r, l in ((0, 0), (1, 0), (0, 1), (1, 1), (2, 0), (0, 2), (2, 1), (1, 2)):
             fetch(r, l, 0, T)
-        fetch(2, 2, 0, 512)
-        fetch(2, 2, 512, 128)
+        fetch(2, 2, 0, 384)
+        fetch(2, 2, 384, 256)
         fetch(2, 2, 640, 128)

@@ -25,10 +25,11 @@ PACK = 4
 BANK = 512
 ROW_TILES = N // P
 
-CHUNKS = [(0, 704), (704, 736), (1440, 448), (1888, 288), (2176, 128)]
-STAGE_AT = [0, 2048, 0, 2048, 0]
-STAGE = 2048 + 4 * 736
-GATE_LOADS = [(0, 256), (256, 448), (704, 736), (1440, 864)]
+WINDOW = 896
+CHUNKS = [(0, 864), (864, 864), (1728, 448), (2176, 128)]
+STAGE_AT = [0, 2560, 0, 2560]
+STAGE = 2560 + 4 * 864
+GATE_LOADS = [(0, 256), (256, 608), (864, 864), (1728, 576)]
 
 
 def tile_moe_pre_lin_relu_kernel(tc, xT, w_words, w_scales, b, gate, offs, pos1, pos2, pos3, out):
@@ -40,16 +41,17 @@ def tile_moe_pre_lin_relu_kernel(tc, xT, w_words, w_scales, b, gate, offs, pos1,
 
         offs_sb = keep.tile([P, S // 16], U16, name="offs_sb")
         pos_sb = [keep.tile([P, T // 16], U16, name="pos_sb%d" % r) for r in range(3)]
-        planes = [keep.tile([P, T], F32, name="plane%d" % j, align_bytes=64) for j in range(PACK)]
+        planes = [keep.tile([P, WINDOW], F32, name="plane%d" % j, align_bytes=64) for j in range(PACK)]
         gate_sb = keep.tile([P, S], F32, name="gate_sb", align_bytes=64)
         w_sb = keep.tile([P, E, 2 * N], U8, name="w_sb", align_bytes=64)
         ws_sb = keep.tile([P, E, N], U8, name="ws_sb", align_bytes=64)
         stage = keep.tile([P, STAGE], F32, name="stage", align_bytes=64)
-        x_bf = keep.tile([P, S * PACK], BF16, name="x_bf", align_bytes=64)
+        x_bf = keep.tile([P, CHUNKS[-1][0] * PACK], BF16, name="x_bf", align_bytes=64)
         x_codes = keep.tile([P, S], U32, name="x_codes", align_bytes=64)
         x_scales = keep.tile([P, S], U8, name="x_scales", align_bytes=64)
         ys = [keep.tile([P, S], F32, name="y%d" % r, align_bytes=64) for r in range(ROW_TILES)]
-        sums = [[keep.tile([P, T], F32, name="sum%d_%d" % (r, l), align_bytes=64) for l in range(3)] for r in range(ROW_TILES)]
+        sum_tiles = [keep.tile([P, 3, T], F32, name="sum%d" % r, align_bytes=64) for r in range(ROW_TILES)]
+        sums = [[sum_tiles[r][:, l, :] for l in range(3)] for r in range(ROW_TILES)]
         bias = [sums[0][r][:, 0:E] for r in range(ROW_TILES)]
 
         nc.gpsimd.memset(ws_sb[:].rearrange("p e n -> p (e n)").bitcast(I32), 0)
@@ -61,11 +63,11 @@ def tile_moe_pre_lin_relu_kernel(tc, xT, w_words, w_scales, b, gate, offs, pos1,
             nc.sync.dma_start(gate_sb[:, s0:s0 + n], gate[0:P, s0:s0 + n])
 
         nc.sync.dma_start(offs_sb[:], offs)
-        nc.sync.dma_start(planes[0][:], x_rows[:, 0, :])
+        nc.sync.dma_start(planes[0][:, 0:T], x_rows[:, 0, :])
         load_gate(0)
         load_gate(1)
         for j in range(1, PACK):
-            nc.sync.dma_start(planes[j][:], x_rows[:, j, :])
+            nc.sync.dma_start(planes[j][:, 0:T], x_rows[:, j, :])
         load_gate(2)
         scale_rows = w_scales.rearrange("e a q n -> q (e a) n").bitcast(I32)
         word_rows = w_words.rearrange("e a p n -> p (e a) n").bitcast(I32)
@@ -77,12 +79,11 @@ def tile_moe_pre_lin_relu_kernel(tc, xT, w_words, w_scales, b, gate, offs, pos1,
         def load_words(e0, e1):
             nc.sync.dma_start(w_sb[:, e0:e1, :].bitcast(I32), word_rows[:, e0:e1, :])
 
+        nc.sync.dma_start(sum_tiles[0][:, :, 0:E], b.rearrange("(r p) e -> p r e", p=P))
         load_scales(0, 4)
-        load_words(0, 2)
-        for r in range(ROW_TILES):
-            nc.sync.dma_start(bias[r], b[r * P:(r + 1) * P, :])
+        load_words(0, 3)
         load_gate(3)
-        load_words(2, E)
+        load_words(3, E)
         load_scales(4, E)
         for r, pos in enumerate((pos1, pos2, pos3)):
             nc.sync.dma_start(pos_sb[r][:], pos)
@@ -100,18 +101,25 @@ def tile_moe_pre_lin_relu_kernel(tc, xT, w_words, w_scales, b, gate, offs, pos1,
                         MULT,
                     )
 
-        def weave(c):
+        def rounded(s0, n):
+            if s0 == CHUNKS[-1][0]:
+                return ys[0][:, 6 * C + P:7 * C + P].bitcast(BF16)
+            return x_bf[:, PACK * s0:PACK * (s0 + n)]
+
+        def weave(c, at=0, step=None):
             s0, n = CHUNKS[c]
+            step = step or n
+            staged = stage[:, STAGE_AT[c]:STAGE_AT[c] + PACK * n].rearrange("p (t s) -> p t s", t=PACK)
             nc.scalar.copy(
-                x_bf[:, PACK * s0:PACK * (s0 + n)].rearrange("p (c i t) -> p c t i", i=4, t=PACK),
-                stage[:, STAGE_AT[c]:STAGE_AT[c] + PACK * n].rearrange("p (t c i) -> p c t i", t=PACK, i=4),
+                rounded(s0 + at, step).rearrange("p (c i t) -> p c t i", i=4, t=PACK),
+                staged[:, :, at:at + step].rearrange("p t (c i) -> p c t i", i=4),
             )
 
         def quantize(s0, n):
             nc.vector.quantize_mx(
                 out=x_codes[:, s0:s0 + n].bitcast(FP8X4),
                 scales=x_scales[:, s0:s0 + n],
-                in_=x_bf[:, PACK * s0:PACK * (s0 + n)],
+                in_=rounded(s0, n),
             )
 
         def multiply(bank, at, r, s0, n):
@@ -141,42 +149,42 @@ def tile_moe_pre_lin_relu_kernel(tc, xT, w_words, w_scales, b, gate, offs, pos1,
                 relu(bank, i * C, r, e * C, C)
 
         gather(0, (0, 1, 2, 3))
-        weave(0)
+        weave(0, 0, 512)
+        weave(0, 512, 352)
         gather(1, (3, 2))
         quantize(0, 512)
+        quantize(512, 256)
         for r in range(ROW_TILES):
-            for e in (0, 1):
-                experts(psum_b if r else psum_a, r, e)
+            for e in range(3 if r < 2 else 2):
+                experts(psum_b if r and e < 2 else psum_a, r, e)
         gather(1, (1, 0))
         weave(1)
         gather(2, (0, 1, 2, 3))
         weave(2)
-        quantize(512, 512)
-        experts(psum_a, 0, 2)
+        quantize(768, 512)
+        quantize(1280, 256)
         experts(psum_a, 0, 3)
-        experts(psum_b, 1, 2)
-        experts(psum_b, 1, 3)
         gather(3, (0, 1, 2, 3))
         weave(3)
-        quantize(1024, 512)
         experts(psum_a, 0, 4)
-        gather(4, (0, 1, 2, 3))
-        weave(4)
         experts(psum_a, 0, 5)
-        quantize(1536, 256)
-        experts(psum_a, 0, 6)
-        quantize(1792, 256)
-        experts(psum_a, 0, 7)
+        late = [psum_b.tile([P, BANK], F32, name="bank") for h in range(2)]
         lasts = [psum_b.tile([P, BANK], F32, name="bank") for h in range(2)]
         for h in range(2):
-            multiply(lasts[h], 0, 1, (4 + h) * C, C)
+            multiply(lasts[h], 0, 1, (3 + h) * C, C)
+        for h in range(2):
+            quantize((6 + h) * C, C)
+            multiply(late[h], 0, 0, (6 + h) * C, C)
         for h in range(2):
             quantize(8 * C + h * P, P)
             multiply(lasts[h], C, 0, 8 * C + h * P, P)
-            relu(lasts[h], C, 0, 8 * C + h * P, P, h == 0)
         for h in range(2):
-            relu(lasts[h], 0, 1, (4 + h) * C, C)
+            relu(lasts[h], C, 0, 8 * C + h * P, P)
+            relu(late[h], 0, 0, (6 + h) * C, C, True)
+        for h in range(2):
+            relu(lasts[h], 0, 1, (3 + h) * C, C)
         experts(psum_a, 1, 8)
+        experts(psum_a, 1, 5)
         experts(psum_a, 1, 6, 7)
         for e0 in range(2, E, 2):
             experts(psum_a, 2, *range(e0, min(e0 + 2, E)))

@@ -25,11 +25,11 @@ PACK = 4
 BANK = 512
 ROW_TILES = N // P
 
-WINDOW = 896
-CHUNKS = [(0, 864), (864, 864), (1728, 448), (2176, 128)]
-STAGE_AT = [0, 2560, 0, 2560]
-STAGE = 2560 + 4 * 864
-GATE_LOADS = [(0, 256), (256, 608), (864, 864), (1728, 576)]
+WINDOW = 1024
+CHUNKS = [(0, 992), (992, 768), (1760, 416), (2176, 128)]
+STAGE_AT = [3 * 768 - 32, 0, 4 * 768, 0]
+STAGE = 3 * 768 - 32 + 4 * 992
+GATE_LOADS = [(0, 352), (352, 640), (992, 768), (1760, 544)]
 
 
 def tile_moe_pre_lin_relu_kernel(tc, xT, w_words, w_scales, b, gate, offs, pos1, pos2, pos3, out):
@@ -103,7 +103,7 @@ def tile_moe_pre_lin_relu_kernel(tc, xT, w_words, w_scales, b, gate, offs, pos1,
 
         def rounded(s0, n):
             if s0 == CHUNKS[-1][0]:
-                return ys[0][:, 6 * C + P:7 * C + P].bitcast(BF16)
+                return ys[0][:, 7 * C:8 * C].bitcast(BF16)
             return x_bf[:, PACK * s0:PACK * (s0 + n)]
 
         def weave(c, at=0, step=None):
@@ -150,14 +150,17 @@ def tile_moe_pre_lin_relu_kernel(tc, xT, w_words, w_scales, b, gate, offs, pos1,
 
         gather(0, (0, 1, 2, 3))
         weave(0, 0, 512)
-        weave(0, 512, 352)
-        gather(1, (3, 2))
+        weave(0, 512, 480)
+        gather(1, (0, 1))
         quantize(0, 512)
-        quantize(512, 256)
         for r in range(ROW_TILES):
-            for e in range(3 if r < 2 else 2):
-                experts(psum_b if r and e < 2 else psum_a, r, e)
-        gather(1, (1, 0))
+            for e in range(2):
+                experts(psum_b if r else psum_a, r, e)
+        gather(1, (2,))
+        quantize(512, 256)
+        for r in range(2):
+            experts(psum_a, r, 2)
+        gather(1, (3,))
         weave(1)
         gather(2, (0, 1, 2, 3))
         weave(2)
@@ -179,8 +182,9 @@ def tile_moe_pre_lin_relu_kernel(tc, xT, w_words, w_scales, b, gate, offs, pos1,
             quantize(8 * C + h * P, P)
             multiply(lasts[h], C, 0, 8 * C + h * P, P)
         for h in range(2):
+            relu(late[h], 0, 0, (6 + h) * C, C, h == 1)
+        for h in range(2):
             relu(lasts[h], C, 0, 8 * C + h * P, P)
-            relu(late[h], 0, 0, (6 + h) * C, C, True)
         for h in range(2):
             relu(lasts[h], 0, 1, (3 + h) * C, C)
         experts(psum_a, 1, 8)

@@ -25,19 +25,18 @@ PACK = 4
 BANK = 512
 ROW_TILES = N // P
 
-WINDOW = 1024
-CHUNKS = [(0, 992), (992, 768), (1760, 416), (2176, 128)]
-STAGE_AT = [3 * 768 - 32, 0, 4 * 768, 0]
-STAGE = 3 * 768 - 32 + 4 * 992
-GATE_LOADS = [(0, 352), (352, 640), (992, 768), (1760, 544)]
+WINDOW = 896
+CHUNKS = [(0, 832), (832, 672), (1504, 416), (1920, 256), (2176, 128)]
+STAGE_AT = [3 * 672 - 32, 0, 4 * 672, 0, 4 * 672]
+STAGE = 3 * 672 - 32 + 4 * 832
+GATE_LOADS = [(0, 320), (320, 512), (832, 672), (1504, 416), (1920, 384)]
 
 
 def tile_moe_pre_lin_relu_kernel(tc, xT, w_words, w_scales, b, gate, offs, pos1, pos2, pos3, out):
     nc = tc.nc
     with ExitStack() as ctx:
         keep = ctx.enter_context(tc.tile_pool(name="keep", bufs=1))
-        psum_a = ctx.enter_context(tc.psum_pool(name="psum_a", bufs=4))
-        psum_b = ctx.enter_context(tc.psum_pool(name="psum_b", bufs=4))
+        psum = ctx.enter_context(tc.psum_pool(name="psum", bufs=1))
 
         offs_sb = keep.tile([P, S // 16], U16, name="offs_sb")
         pos_sb = [keep.tile([P, T // 16], U16, name="pos_sb%d" % r) for r in range(3)]
@@ -50,8 +49,9 @@ def tile_moe_pre_lin_relu_kernel(tc, xT, w_words, w_scales, b, gate, offs, pos1,
         x_codes = keep.tile([P, S], U32, name="x_codes", align_bytes=64)
         x_scales = keep.tile([P, S], U8, name="x_scales", align_bytes=64)
         ys = [keep.tile([P, S], F32, name="y%d" % r, align_bytes=64) for r in range(ROW_TILES)]
-        sum_tiles = [keep.tile([P, 3, T], F32, name="sum%d" % r, align_bytes=64) for r in range(ROW_TILES)]
-        sums = [[sum_tiles[r][:, l, :] for l in range(3)] for r in range(ROW_TILES)]
+        parts = [keep.tile([P, T], F32, name="part%d" % i, align_bytes=64) for i in range(8)]
+        sums = [parts[0:3], [parts[3], parts[4], parts[1]], parts[5:8]]
+        banks = [psum.tile([P, BANK], F32, name="bank%d" % i) for i in range(8)]
         bias = [sums[0][r][:, 0:E] for r in range(ROW_TILES)]
 
         nc.gpsimd.memset(ws_sb[:].rearrange("p e n -> p (e n)").bitcast(I32), 0)
@@ -79,11 +79,14 @@ def tile_moe_pre_lin_relu_kernel(tc, xT, w_words, w_scales, b, gate, offs, pos1,
         def load_words(e0, e1):
             nc.sync.dma_start(w_sb[:, e0:e1, :].bitcast(I32), word_rows[:, e0:e1, :])
 
-        nc.sync.dma_start(sum_tiles[0][:, :, 0:E], b.rearrange("(r p) e -> p r e", p=P))
         load_scales(0, 4)
         load_words(0, 3)
+        for r in range(ROW_TILES):
+            nc.sync.dma_start(bias[r], b[r * P:(r + 1) * P, :])
         load_gate(3)
-        load_words(3, E)
+        load_words(3, 6)
+        load_gate(4)
+        load_words(6, E)
         load_scales(4, E)
         for r, pos in enumerate((pos1, pos2, pos3)):
             nc.sync.dma_start(pos_sb[r][:], pos)
@@ -141,8 +144,8 @@ def tile_moe_pre_lin_relu_kernel(tc, xT, w_words, w_scales, b, gate, offs, pos1,
             else:
                 nc.scalar.activation(ys[r][:, s0:s0 + n], bank[:, at:at + n], RELU, bias=bias[r][:, e:e + 1])
 
-        def experts(pool, r, *es):
-            bank = pool.tile([P, BANK], F32, name="bank")
+        def experts(i_bank, r, *es):
+            bank = banks[i_bank]
             for i, e in enumerate(es):
                 multiply(bank, i * C, r, e * C, C)
             for i, e in enumerate(es):
@@ -150,48 +153,49 @@ def tile_moe_pre_lin_relu_kernel(tc, xT, w_words, w_scales, b, gate, offs, pos1,
 
         gather(0, (0, 1, 2, 3))
         weave(0, 0, 512)
-        weave(0, 512, 480)
+        weave(0, 512, 320)
         gather(1, (0, 1))
         quantize(0, 512)
-        for r in range(ROW_TILES):
+        for r in range(2):
             for e in range(2):
-                experts(psum_b if r else psum_a, r, e)
+                experts(2 * r + e, r, e)
         gather(1, (2,))
         quantize(512, 256)
         for r in range(2):
-            experts(psum_a, r, 2)
+            experts(4 + r, r, 2)
         gather(1, (3,))
         weave(1)
         gather(2, (0, 1, 2, 3))
         weave(2)
         quantize(768, 512)
-        quantize(1280, 256)
-        experts(psum_a, 0, 3)
+        experts(0, 0, 3)
+        experts(1, 0, 4)
+        experts(2, 1, 3)
         gather(3, (0, 1, 2, 3))
         weave(3)
-        experts(psum_a, 0, 4)
-        experts(psum_a, 0, 5)
-        late = [psum_b.tile([P, BANK], F32, name="bank") for h in range(2)]
-        lasts = [psum_b.tile([P, BANK], F32, name="bank") for h in range(2)]
+        quantize(1280, 256)
+        experts(3, 0, 5)
+        gather(4, (0, 1, 2, 3))
+        weave(4)
         for h in range(2):
-            multiply(lasts[h], 0, 1, (3 + h) * C, C)
+            multiply(banks[4 + h], 0, 1, (4 + h) * C, C)
         for h in range(2):
             quantize((6 + h) * C, C)
-            multiply(late[h], 0, 0, (6 + h) * C, C)
+            multiply(banks[6 + h], 0, 0, (6 + h) * C, C)
         for h in range(2):
             quantize(8 * C + h * P, P)
-            multiply(lasts[h], C, 0, 8 * C + h * P, P)
+            multiply(banks[4 + h], C, 0, 8 * C + h * P, P)
         for h in range(2):
-            relu(late[h], 0, 0, (6 + h) * C, C, h == 1)
+            relu(banks[6 + h], 0, 0, (6 + h) * C, C, h == 1)
         for h in range(2):
-            relu(lasts[h], C, 0, 8 * C + h * P, P)
+            relu(banks[4 + h], C, 0, 8 * C + h * P, P)
         for h in range(2):
-            relu(lasts[h], 0, 1, (3 + h) * C, C)
-        experts(psum_a, 1, 8)
-        experts(psum_a, 1, 5)
-        experts(psum_a, 1, 6, 7)
-        for e0 in range(2, E, 2):
-            experts(psum_a, 2, *range(e0, min(e0 + 2, E)))
+            relu(banks[4 + h], 0, 1, (4 + h) * C, C)
+        experts(0, 1, 8)
+        for h in range(2):
+            experts(6 + h, 1, 6 + h)
+        for i_bank, e0 in zip((4, 5, 0, 6, 7), range(0, E, 2)):
+            experts(i_bank, 2, *range(e0, min(e0 + 2, E)))
 
         def fetch(r, l, t0, n):
             found = ys[r][:].indirect(pos_sb[l][:, t0 // 16:(t0 + n) // 16])

@@ -25,11 +25,11 @@ PACK = 4
 BANK = 512
 ROW_TILES = N // P
 
-WINDOW = 896
-CHUNKS = [(0, 832), (832, 672), (1504, 416), (1920, 256), (2176, 128)]
-STAGE_AT = [3 * 672 - 32, 0, 4 * 672, 0, 4 * 672]
-STAGE = 3 * 672 - 32 + 4 * 832
-GATE_LOADS = [(0, 320), (320, 512), (832, 672), (1504, 416), (1920, 384)]
+WINDOW = 1024
+CHUNKS = [(0, 992), (992, 768), (1760, 416), (2176, 128)]
+STAGE_AT = [3 * 768 - 32, 0, 4 * 768, 0]
+STAGE = 3 * 768 - 32 + 4 * 992
+GATE_LOADS = [(0, 352), (352, 640), (992, 768), (1760, 416), (2176, 128)]
 
 
 def tile_moe_pre_lin_relu_kernel(tc, xT, w_words, w_scales, b, gate, offs, pos1, pos2, pos3, out):
@@ -49,10 +49,10 @@ def tile_moe_pre_lin_relu_kernel(tc, xT, w_words, w_scales, b, gate, offs, pos1,
         x_codes = keep.tile([P, S], U32, name="x_codes", align_bytes=64)
         x_scales = keep.tile([P, S], U8, name="x_scales", align_bytes=64)
         ys = [keep.tile([P, S], F32, name="y%d" % r, align_bytes=64) for r in range(ROW_TILES)]
-        parts = [keep.tile([P, T], F32, name="part%d" % i, align_bytes=64) for i in range(8)]
-        sums = [parts[0:3], [parts[3], parts[4], parts[1]], parts[5:8]]
+        parts = [keep.tile([P, T], F32, name="part%d" % i, align_bytes=64) for i in range(9)]
+        sums = [parts[0:3], parts[3:6], parts[6:9]]
         banks = [psum.tile([P, BANK], F32, name="bank%d" % i) for i in range(8)]
-        bias = [sums[0][r][:, 0:E] for r in range(ROW_TILES)]
+        bias = [part[:, 0:E] for part in (sums[0][0], sums[0][2], sums[1][1])]
 
         nc.gpsimd.memset(ws_sb[:].rearrange("p e n -> p (e n)").bitcast(I32), 0)
 
@@ -153,7 +153,7 @@ def tile_moe_pre_lin_relu_kernel(tc, xT, w_words, w_scales, b, gate, offs, pos1,
 
         gather(0, (0, 1, 2, 3))
         weave(0, 0, 512)
-        weave(0, 512, 320)
+        weave(0, 512, 480)
         gather(1, (0, 1))
         quantize(0, 512)
         for r in range(2):
@@ -168,20 +168,17 @@ def tile_moe_pre_lin_relu_kernel(tc, xT, w_words, w_scales, b, gate, offs, pos1,
         gather(2, (0, 1, 2, 3))
         weave(2)
         quantize(768, 512)
+        quantize(1280, 256)
         experts(0, 0, 3)
-        experts(1, 0, 4)
-        experts(2, 1, 3)
         gather(3, (0, 1, 2, 3))
         weave(3)
-        quantize(1280, 256)
-        experts(3, 0, 5)
-        gather(4, (0, 1, 2, 3))
-        weave(4)
-        for h in range(2):
-            multiply(banks[4 + h], 0, 1, (4 + h) * C, C)
+        experts(1, 0, 4)
+        experts(2, 0, 5)
         for h in range(2):
             quantize((6 + h) * C, C)
             multiply(banks[6 + h], 0, 0, (6 + h) * C, C)
+        for h in range(2):
+            multiply(banks[4 + h], 0, 1, (3 + h) * C, C)
         for h in range(2):
             quantize(8 * C + h * P, P)
             multiply(banks[4 + h], C, 0, 8 * C + h * P, P)
@@ -190,11 +187,10 @@ def tile_moe_pre_lin_relu_kernel(tc, xT, w_words, w_scales, b, gate, offs, pos1,
         for h in range(2):
             relu(banks[4 + h], C, 0, 8 * C + h * P, P)
         for h in range(2):
-            relu(banks[4 + h], 0, 1, (4 + h) * C, C)
-        experts(0, 1, 8)
-        for h in range(2):
-            experts(6 + h, 1, 6 + h)
-        for i_bank, e0 in zip((4, 5, 0, 6, 7), range(0, E, 2)):
+            relu(banks[4 + h], 0, 1, (3 + h) * C, C)
+        experts(3, 1, 8, 5)
+        experts(6, 1, 6, 7)
+        for i_bank, e0 in zip((4, 5, 3, 6, 7), range(0, E, 2)):
             experts(i_bank, 2, *range(e0, min(e0 + 2, E)))
 
         def fetch(r, l, t0, n):
@@ -206,7 +202,10 @@ def tile_moe_pre_lin_relu_kernel(tc, xT, w_words, w_scales, b, gate, offs, pos1,
             if l == 2:
                 nc.sync.dma_start(out[r * P:(r + 1) * P, t0:t0 + n], sums[r][l][:, t0:t0 + n])
 
-        for r, l in ((0, 0), (1, 0), (0, 1), (1, 1), (2, 0), (0, 2), (2, 1), (1, 2)):
+        for l in range(2):
+            for t0 in (0, T // 2):
+                fetch(0, l, t0, T // 2)
+        for r, l in ((1, 0), (0, 2), (2, 0), (1, 1), (2, 1), (1, 2)):
             fetch(r, l, 0, T)
         fetch(2, 2, 0, 384)
         fetch(2, 2, 384, 256)

@@ -25,11 +25,15 @@ PACK = 4
 BANK = 512
 ROW_TILES = N // P
 
-WINDOW = 1024
-CHUNKS = [(0, 992), (992, 768), (1760, 416), (2176, 128)]
-STAGE_AT = [3 * 768 - 32, 0, 4 * 768, 0]
-STAGE = 3 * 768 - 32 + 4 * 992
-GATE_LOADS = [(0, 352), (352, 640), (992, 768), (1760, 416), (2176, 128)]
+CHUNKS = [(0, 1024), (1024, 736), (1760, 416), (2176, 128)]
+WINDOW = 1088
+FIRST_WEAVE = 512
+OVERLAP = 32
+STAGE_AT = [3 * CHUNKS[1][1] - OVERLAP, 0, PACK * CHUNKS[1][1], 0]
+STAGE = STAGE_AT[0] + PACK * CHUNKS[0][1]
+FIRST_GATE = 384
+GATE_LOADS = [(0, FIRST_GATE), (FIRST_GATE, CHUNKS[0][1] - FIRST_GATE)] + CHUNKS[1:]
+LAST_PIECES = [(0, 384), (384, 256), (640, 128)]
 
 
 def tile_moe_pre_lin_relu_kernel(tc, xT, w_words, w_scales, b, gate, offs, pos1, pos2, pos3, out):
@@ -39,7 +43,7 @@ def tile_moe_pre_lin_relu_kernel(tc, xT, w_words, w_scales, b, gate, offs, pos1,
         psum = ctx.enter_context(tc.psum_pool(name="psum", bufs=1))
 
         offs_sb = keep.tile([P, S // 16], U16, name="offs_sb")
-        pos_sb = [keep.tile([P, T // 16], U16, name="pos_sb%d" % r) for r in range(3)]
+        pos_sb = [keep.tile([P, T // 16], U16, name="pos_sb%d" % l) for l in range(3)]
         planes = [keep.tile([P, WINDOW], F32, name="plane%d" % j, align_bytes=64) for j in range(PACK)]
         gate_sb = keep.tile([P, S], F32, name="gate_sb", align_bytes=64)
         w_sb = keep.tile([P, E, 2 * N], U8, name="w_sb", align_bytes=64)
@@ -49,28 +53,20 @@ def tile_moe_pre_lin_relu_kernel(tc, xT, w_words, w_scales, b, gate, offs, pos1,
         x_codes = keep.tile([P, S], U32, name="x_codes", align_bytes=64)
         x_scales = keep.tile([P, S], U8, name="x_scales", align_bytes=64)
         ys = [keep.tile([P, S], F32, name="y%d" % r, align_bytes=64) for r in range(ROW_TILES)]
-        parts = [keep.tile([P, T], F32, name="part%d" % i, align_bytes=64) for i in range(9)]
-        sums = [parts[0:3], parts[3:6], parts[6:9]]
+        parts = [keep.tile([P, T], F32, name="part%d" % i, align_bytes=64) for i in range(3 * ROW_TILES)]
+        sums = [parts[3 * r:3 * r + 3] for r in range(ROW_TILES)]
         banks = [psum.tile([P, BANK], F32, name="bank%d" % i) for i in range(8)]
         bias = [part[:, 0:E] for part in (sums[0][0], sums[0][2], sums[1][1])]
 
         nc.gpsimd.memset(ws_sb[:].rearrange("p e n -> p (e n)").bitcast(I32), 0)
 
         x_rows = xT.rearrange("(p j) t -> p j t", j=PACK)
+        scale_rows = w_scales.rearrange("e a q n -> q (e a) n").bitcast(I32)
+        word_rows = w_words.rearrange("e a p n -> p (e a) n").bitcast(I32)
 
         def load_gate(i):
             s0, n = GATE_LOADS[i]
             nc.sync.dma_start(gate_sb[:, s0:s0 + n], gate[0:P, s0:s0 + n])
-
-        nc.sync.dma_start(offs_sb[:], offs)
-        nc.sync.dma_start(planes[0][:, 0:T], x_rows[:, 0, :])
-        load_gate(0)
-        load_gate(1)
-        for j in range(1, PACK):
-            nc.sync.dma_start(planes[j][:, 0:T], x_rows[:, j, :])
-        load_gate(2)
-        scale_rows = w_scales.rearrange("e a q n -> q (e a) n").bitcast(I32)
-        word_rows = w_words.rearrange("e a p n -> p (e a) n").bitcast(I32)
 
         def load_scales(e0, e1):
             for q in range(4):
@@ -79,6 +75,13 @@ def tile_moe_pre_lin_relu_kernel(tc, xT, w_words, w_scales, b, gate, offs, pos1,
         def load_words(e0, e1):
             nc.sync.dma_start(w_sb[:, e0:e1, :].bitcast(I32), word_rows[:, e0:e1, :])
 
+        nc.sync.dma_start(offs_sb[:], offs)
+        nc.sync.dma_start(planes[0][:, 0:T], x_rows[:, 0, :])
+        load_gate(0)
+        load_gate(1)
+        for j in range(1, PACK):
+            nc.sync.dma_start(planes[j][:, 0:T], x_rows[:, j, :])
+        load_gate(2)
         load_scales(0, 4)
         load_words(0, 3)
         for r in range(ROW_TILES):
@@ -88,47 +91,46 @@ def tile_moe_pre_lin_relu_kernel(tc, xT, w_words, w_scales, b, gate, offs, pos1,
         load_gate(4)
         load_words(6, E)
         load_scales(4, E)
-        for r, pos in enumerate((pos1, pos2, pos3)):
-            nc.sync.dma_start(pos_sb[r][:], pos)
+        for l, pos in enumerate((pos1, pos2, pos3)):
+            nc.sync.dma_start(pos_sb[l][:], pos)
 
-        def gather(c, order):
+        def gather(c, which):
             s0, n = CHUNKS[c]
-            for j in order:
-                cuts = GATE_LOADS[0:2] if (c, j) == (0, 0) else [(0, n)]
-                for at, step in cuts:
+            for j in which:
+                pieces = GATE_LOADS[0:2] if (c, j) == (0, 0) else [(0, n)]
+                for at, count in pieces:
                     to = STAGE_AT[c] + j * n + at
                     nc.vector.tensor_tensor(
-                        stage[:, to:to + step],
-                        planes[j][:].indirect(offs_sb[:, (s0 + at) // 16:(s0 + at + step) // 16]),
-                        gate_sb[:, s0 + at:s0 + at + step],
+                        stage[:, to:to + count],
+                        planes[j][:].indirect(offs_sb[:, (s0 + at) // 16:(s0 + at + count) // 16]),
+                        gate_sb[:, s0 + at:s0 + at + count],
                         MULT,
                     )
 
-        def rounded(s0, n):
+        def woven(s0, n):
             if s0 == CHUNKS[-1][0]:
                 return ys[0][:, 7 * C:8 * C].bitcast(BF16)
             return x_bf[:, PACK * s0:PACK * (s0 + n)]
 
-        def weave(c, at=0, step=None):
+        def weave(c, at, count):
             s0, n = CHUNKS[c]
-            step = step or n
             staged = stage[:, STAGE_AT[c]:STAGE_AT[c] + PACK * n].rearrange("p (t s) -> p t s", t=PACK)
             nc.scalar.copy(
-                rounded(s0 + at, step).rearrange("p (c i t) -> p c t i", i=4, t=PACK),
-                staged[:, :, at:at + step].rearrange("p t (c i) -> p c t i", i=4),
+                woven(s0 + at, count).rearrange("p (c i t) -> p c t i", i=4, t=PACK),
+                staged[:, :, at:at + count].rearrange("p t (c i) -> p c t i", i=4),
             )
 
         def quantize(s0, n):
             nc.vector.quantize_mx(
                 out=x_codes[:, s0:s0 + n].bitcast(FP8X4),
                 scales=x_scales[:, s0:s0 + n],
-                in_=rounded(s0, n),
+                in_=woven(s0, n),
             )
 
         def multiply(bank, at, r, s0, n):
             e = s0 // C
             nc.tensor.matmul_mx(
-                out=bank[:, at:at + n],
+                out=banks[bank][:, at:at + n],
                 lhsT=w_sb[:, e, 2 * P * r:2 * P * (r + 1)].bitcast(FP4X4),
                 lhsT_scale=ws_sb[:, e, P * r:P * (r + 1)],
                 rhs=x_codes[:, s0:s0 + n].bitcast(FP8X4),
@@ -137,61 +139,61 @@ def tile_moe_pre_lin_relu_kernel(tc, xT, w_words, w_scales, b, gate, offs, pos1,
                 stop=True,
             )
 
-        def relu(bank, at, r, s0, n, on_vector=False):
+        def relu(bank, at, r, s0, n):
             e = s0 // C
-            if on_vector:
-                nc.vector.tensor_scalar(ys[r][:, s0:s0 + n], bank[:, at:at + n], bias[r][:, e:e + 1], 0.0, ADD, MAX)
-            else:
-                nc.scalar.activation(ys[r][:, s0:s0 + n], bank[:, at:at + n], RELU, bias=bias[r][:, e:e + 1])
+            nc.scalar.activation(ys[r][:, s0:s0 + n], banks[bank][:, at:at + n], RELU, bias=bias[r][:, e:e + 1])
 
-        def experts(i_bank, r, *es):
-            bank = banks[i_bank]
+        def relu_on_vector(bank, at, r, s0, n):
+            e = s0 // C
+            nc.vector.tensor_scalar(ys[r][:, s0:s0 + n], banks[bank][:, at:at + n], bias[r][:, e:e + 1], 0.0, ADD, MAX)
+
+        def experts(bank, r, *es):
             for i, e in enumerate(es):
                 multiply(bank, i * C, r, e * C, C)
             for i, e in enumerate(es):
                 relu(bank, i * C, r, e * C, C)
 
-        gather(0, (0, 1, 2, 3))
-        weave(0, 0, 512)
-        weave(0, 512, 480)
+        gather(0, range(PACK))
+        weave(0, 0, FIRST_WEAVE)
+        weave(0, FIRST_WEAVE, CHUNKS[0][1] - FIRST_WEAVE)
         gather(1, (0, 1))
-        quantize(0, 512)
+        quantize(0, 2 * C)
         for r in range(2):
             for e in range(2):
                 experts(2 * r + e, r, e)
         gather(1, (2,))
-        quantize(512, 256)
-        for r in range(2):
-            experts(4 + r, r, 2)
+        quantize(2 * C, C)
+        experts(4, 0, 2)
         gather(1, (3,))
-        weave(1)
-        gather(2, (0, 1, 2, 3))
-        weave(2)
-        quantize(768, 512)
-        quantize(1280, 256)
+        weave(1, 0, CHUNKS[1][1])
+        gather(2, range(PACK))
+        weave(2, 0, CHUNKS[2][1])
+        quantize(3 * C, 2 * C)
+        quantize(5 * C, C)
         experts(0, 0, 3)
-        gather(3, (0, 1, 2, 3))
-        weave(3)
+        gather(3, range(PACK))
+        weave(3, 0, CHUNKS[3][1])
         experts(1, 0, 4)
         experts(2, 0, 5)
         for h in range(2):
             quantize((6 + h) * C, C)
-            multiply(banks[6 + h], 0, 0, (6 + h) * C, C)
+            multiply(6 + h, 0, 0, (6 + h) * C, C)
         for h in range(2):
-            multiply(banks[4 + h], 0, 1, (3 + h) * C, C)
+            multiply(4 + h, 0, 1, (3 + h) * C, C)
         for h in range(2):
             quantize(8 * C + h * P, P)
-            multiply(banks[4 + h], C, 0, 8 * C + h * P, P)
+            multiply(4 + h, C, 0, 8 * C + h * P, P)
+        relu(6, 0, 0, 6 * C, C)
+        relu_on_vector(7, 0, 0, 7 * C, C)
         for h in range(2):
-            relu(banks[6 + h], 0, 0, (6 + h) * C, C, h == 1)
+            relu(4 + h, C, 0, 8 * C + h * P, P)
         for h in range(2):
-            relu(banks[4 + h], C, 0, 8 * C + h * P, P)
-        for h in range(2):
-            relu(banks[4 + h], 0, 1, (3 + h) * C, C)
+            relu(4 + h, 0, 1, (3 + h) * C, C)
         experts(3, 1, 8, 5)
         experts(6, 1, 6, 7)
-        for i_bank, e0 in zip((4, 5, 3, 6, 7), range(0, E, 2)):
-            experts(i_bank, 2, *range(e0, min(e0 + 2, E)))
+        experts(7, 1, 2)
+        for bank, e0 in zip((4, 5, 3, 6, 7), range(0, E, 2)):
+            experts(bank, 2, *range(e0, min(e0 + 2, E)))
 
         def fetch(r, l, t0, n):
             found = ys[r][:].indirect(pos_sb[l][:, t0 // 16:(t0 + n) // 16])
@@ -207,6 +209,5 @@ def tile_moe_pre_lin_relu_kernel(tc, xT, w_words, w_scales, b, gate, offs, pos1,
                 fetch(0, l, t0, T // 2)
         for r, l in ((1, 0), (0, 2), (2, 0), (1, 1), (2, 1), (1, 2)):
             fetch(r, l, 0, T)
-        fetch(2, 2, 0, 384)
-        fetch(2, 2, 384, 256)
-        fetch(2, 2, 640, 128)
+        for t0, n in LAST_PIECES:
+            fetch(2, 2, t0, n)

@@ -31,8 +31,8 @@ FIRST_WEAVE = 512
 OVERLAP = 32
 STAGE_AT = [3 * CHUNKS[1][1] - OVERLAP, 0, PACK * CHUNKS[1][1], 0]
 STAGE = STAGE_AT[0] + PACK * CHUNKS[0][1]
-FIRST_GATE = 384
-GATE_LOADS = [(0, FIRST_GATE), (FIRST_GATE, CHUNKS[0][1] - FIRST_GATE)] + CHUNKS[1:]
+FIRST_GATES = [(0, 128), (128, 288), (416, 608)]
+GATE_LOADS = FIRST_GATES + CHUNKS[1:]
 LAST_PIECES = [(0, 384), (384, 256), (640, 128)]
 
 
@@ -77,19 +77,18 @@ def tile_moe_pre_lin_relu_kernel(tc, xT, w_words, w_scales, b, gate, offs, pos1,
 
         nc.sync.dma_start(offs_sb[:], offs)
         nc.sync.dma_start(planes[0][:, 0:T], x_rows[:, 0, :])
-        load_gate(0)
-        load_gate(1)
+        for i in range(len(FIRST_GATES)):
+            load_gate(i)
         for j in range(1, PACK):
             nc.sync.dma_start(planes[j][:, 0:T], x_rows[:, j, :])
-        load_gate(2)
+        load_gate(len(FIRST_GATES))
         load_scales(0, 4)
         load_words(0, 3)
         for r in range(ROW_TILES):
             nc.sync.dma_start(bias[r], b[r * P:(r + 1) * P, :])
-        load_gate(3)
-        load_words(3, 6)
-        load_gate(4)
-        load_words(6, E)
+        load_gate(len(FIRST_GATES) + 1)
+        load_gate(len(FIRST_GATES) + 2)
+        load_words(3, E)
         load_scales(4, E)
         for l, pos in enumerate((pos1, pos2, pos3)):
             nc.sync.dma_start(pos_sb[l][:], pos)
@@ -97,7 +96,7 @@ def tile_moe_pre_lin_relu_kernel(tc, xT, w_words, w_scales, b, gate, offs, pos1,
         def gather(c, which):
             s0, n = CHUNKS[c]
             for j in which:
-                pieces = GATE_LOADS[0:2] if (c, j) == (0, 0) else [(0, n)]
+                pieces = FIRST_GATES if (c, j) == (0, 0) else [(0, n)]
                 for at, count in pieces:
                     to = STAGE_AT[c] + j * n + at
                     nc.vector.tensor_tensor(

@@ -75,8 +75,8 @@ def tile_moe_pre_lin_relu_kernel(tc, xT, w_words, w_scales, b, gate, offs, pos1,
         def load_words(e0, e1):
             nc.sync.dma_start(w_sb[:, e0:e1, :].bitcast(I32), word_rows[:, e0:e1, :])
 
-        nc.sync.dma_start(offs_sb[:], offs)
         nc.sync.dma_start(planes[0][:, 0:T], x_rows[:, 0, :])
+        nc.sync.dma_start(offs_sb[:], offs)
         for i in range(len(FIRST_GATES)):
             load_gate(i)
         for j in range(1, PACK):

@@ -24,6 +24,7 @@ P = 128
 PACK = 4
 BANK = 512
 ROW_TILES = N // P
+STRETCH = 64 * 1024
 
 CHUNKS = [(0, 1024), (1024, 736), (1760, 416), (2176, 128)]
 WINDOW = 1088
@@ -40,20 +41,28 @@ def tile_moe_pre_lin_relu_kernel(tc, xT, w_words, w_scales, b, gate, offs, pos1,
     nc = tc.nc
     with ExitStack() as ctx:
         keep = ctx.enter_context(tc.tile_pool(name="keep", bufs=1))
+        data = ctx.enter_context(tc.tile_pool(name="data", bufs=1))
         psum = ctx.enter_context(tc.psum_pool(name="psum", bufs=1))
 
         offs_sb = keep.tile([P, S // 16], U16, name="offs_sb")
         pos_sb = [keep.tile([P, T // 16], U16, name="pos_sb%d" % l) for l in range(3)]
-        planes = [keep.tile([P, WINDOW], F32, name="plane%d" % j, align_bytes=64) for j in range(PACK)]
-        gate_sb = keep.tile([P, S], F32, name="gate_sb", align_bytes=64)
-        w_sb = keep.tile([P, E, 2 * N], U8, name="w_sb", align_bytes=64)
-        ws_sb = keep.tile([P, E, N], U8, name="ws_sb", align_bytes=64)
-        stage = keep.tile([P, STAGE], F32, name="stage", align_bytes=64)
-        x_bf = keep.tile([P, CHUNKS[-1][0] * PACK], BF16, name="x_bf", align_bytes=64)
-        x_codes = keep.tile([P, S], U32, name="x_codes", align_bytes=64)
-        x_scales = keep.tile([P, S], U8, name="x_scales", align_bytes=64)
-        ys = [keep.tile([P, S], F32, name="y%d" % r, align_bytes=64) for r in range(ROW_TILES)]
-        parts = [keep.tile([P, T], F32, name="part%d" % i, align_bytes=64) for i in range(3 * ROW_TILES)]
+        free = [q * STRETCH for q in range(4)]
+
+        def place(q, shape, dtype, size, name):
+            at = free[q]
+            free[q] = at + -(-size // 256) * 256
+            return data.tile(shape, dtype, name=name, align_bytes=256, offset=at)
+
+        planes = [place(0, [P, WINDOW], F32, 4 * WINDOW, "plane%d" % j) for j in range(PACK)]
+        parts = [place(0, [P, T], F32, 4 * T, "part%d" % i) for i in range(3 * ROW_TILES)]
+        stage = place(1, [P, STAGE], F32, 4 * STAGE, "stage")
+        gate_sb = place(2, [P, S], F32, 4 * S, "gate_sb")
+        x_bf = place(2, [P, CHUNKS[-1][0] * PACK], BF16, 2 * PACK * CHUNKS[-1][0], "x_bf")
+        ys = [place(1 + r, [P, S], F32, 4 * S, "y%d" % r) for r in range(ROW_TILES)]
+        w_sb = place(3, [P, E, 2 * N], U8, 2 * E * N, "w_sb")
+        ws_sb = place(3, [P, E, N], U8, E * N, "ws_sb")
+        x_codes = place(3, [P, S], U32, 4 * S, "x_codes")
+        x_scales = place(3, [P, S], U8, S, "x_scales")
         sums = [parts[3 * r:3 * r + 3] for r in range(ROW_TILES)]
         banks = [psum.tile([P, BANK], F32, name="bank%d" % i) for i in range(8)]
         bias = [part[:, 0:E] for part in (sums[0][0], sums[0][2], sums[1][1])]

@@ -19,21 +19,17 @@ MULT = mybir.AluOpType.mult
 ADD = mybir.AluOpType.add
 MAX = mybir.AluOpType.max
 RELU = mybir.ActivationFunctionType.Relu
+COPY = mybir.ActivationFunctionType.Copy
 
 P = 128
 PACK = 4
 BANK = 512
 ROW_TILES = N // P
-STRETCH = 64 * 1024
+HALF = T // 2
 
-CHUNKS = [(0, 1024), (1024, 736), (1760, 416), (2176, 128)]
-WINDOW = 1088
-FIRST_WEAVE = 512
-OVERLAP = 32
-STAGE_AT = [3 * CHUNKS[1][1] - OVERLAP, 0, PACK * CHUNKS[1][1], 0]
-STAGE = STAGE_AT[0] + PACK * CHUNKS[0][1]
-FIRST_GATES = [(0, 128), (128, 288), (416, 608)]
-GATE_LOADS = FIRST_GATES + CHUNKS[1:]
+CHUNKS = [(0, 640), (640, 768), (1408, 384), (1792, 256), (2048, 256)]
+WINDOW = 800
+FIRST_GATES = [(0, 128), (128, 192), (320, 320)]
 LAST_PIECES = [(0, 384), (384, 256), (640, 128)]
 
 
@@ -46,26 +42,22 @@ def tile_moe_pre_lin_relu_kernel(tc, xT, w_words, w_scales, b, gate, offs, pos1,
 
         offs_sb = keep.tile([P, S // 16], U16, name="offs_sb")
         pos_sb = [keep.tile([P, T // 16], U16, name="pos_sb%d" % l) for l in range(3)]
-        free = [q * STRETCH for q in range(4)]
 
-        def place(q, shape, dtype, size, name):
-            at = free[q]
-            free[q] = at + -(-size // 256) * 256
-            return data.tile(shape, dtype, name=name, align_bytes=256, offset=at)
+        def tile(shape, dtype, name):
+            return data.tile(shape, dtype, name=name, align_bytes=256)
 
-        planes = [place(0, [P, WINDOW], F32, 4 * WINDOW, "plane%d" % j) for j in range(PACK)]
-        parts = [place(0, [P, T], F32, 4 * T, "part%d" % i) for i in range(3 * ROW_TILES)]
-        stage = place(1, [P, STAGE], F32, 4 * STAGE, "stage")
-        gate_sb = place(2, [P, S], F32, 4 * S, "gate_sb")
-        x_bf = place(2, [P, CHUNKS[-1][0] * PACK], BF16, 2 * PACK * CHUNKS[-1][0], "x_bf")
-        ys = [place(1 + r, [P, S], F32, 4 * S, "y%d" % r) for r in range(ROW_TILES)]
-        w_sb = place(3, [P, E, 2 * N], U8, 2 * E * N, "w_sb")
-        ws_sb = place(3, [P, E, N], U8, E * N, "ws_sb")
-        x_codes = place(3, [P, S], U32, 4 * S, "x_codes")
-        x_scales = place(3, [P, S], U8, S, "x_scales")
-        sums = [parts[3 * r:3 * r + 3] for r in range(ROW_TILES)]
+        planes = [tile([P, WINDOW], F32, "plane%d" % j) for j in range(PACK)]
+        stages = [tile([P, PACK * n], F32, "stage%d" % c) for c, (s0, n) in enumerate(CHUNKS)]
+        gate_sb = tile([P, S], F32, "gate_sb")
+        x_bf = tile([P, 7 * C * PACK], BF16, "x_bf")
+        ys = [tile([P, S], F32, "y%d" % r) for r in range(ROW_TILES)]
+        w_sb = tile([P, E, 2 * N], U8, "w_sb")
+        ws_sb = tile([P, E, N], U8, "ws_sb")
+        x_codes = tile([P, S], U32, "x_codes")
+        x_scales = tile([P, S], U8, "x_scales")
+        bias = tile([P, ROW_TILES, E], F32, "bias")
+        sums = [[tile([P, T], F32, "sum%d_%d" % (r, l)) for l in range(3)] for r in range(ROW_TILES)]
         banks = [psum.tile([P, BANK], F32, name="bank%d" % i) for i in range(8)]
-        bias = [part[:, 0:E] for part in (sums[0][0], sums[0][2], sums[1][1])]
 
         nc.gpsimd.memset(ws_sb[:].rearrange("p e n -> p (e n)").bitcast(I32), 0)
 
@@ -73,149 +65,133 @@ def tile_moe_pre_lin_relu_kernel(tc, xT, w_words, w_scales, b, gate, offs, pos1,
         scale_rows = w_scales.rearrange("e a q n -> q (e a) n").bitcast(I32)
         word_rows = w_words.rearrange("e a p n -> p (e a) n").bitcast(I32)
 
-        def load_gate(i):
-            s0, n = GATE_LOADS[i]
+        def load_gate(s0, n):
             nc.sync.dma_start(gate_sb[:, s0:s0 + n], gate[0:P, s0:s0 + n])
-
-        def load_scales(e0, e1):
-            for q in range(4):
-                nc.sync.dma_start(ws_sb[32 * q:32 * q + 4, e0:e1, :].bitcast(I32), scale_rows[4 * q:4 * q + 4, e0:e1, :])
-
-        def load_words(e0, e1):
-            nc.sync.dma_start(w_sb[:, e0:e1, :].bitcast(I32), word_rows[:, e0:e1, :])
 
         nc.sync.dma_start(planes[0][:, 0:T], x_rows[:, 0, :])
         nc.sync.dma_start(offs_sb[:], offs)
-        for i in range(len(FIRST_GATES)):
-            load_gate(i)
+        for s0, n in FIRST_GATES:
+            load_gate(s0, n)
         for j in range(1, PACK):
             nc.sync.dma_start(planes[j][:, 0:T], x_rows[:, j, :])
-        load_gate(len(FIRST_GATES))
-        load_scales(0, 4)
-        load_words(0, 3)
-        for r in range(ROW_TILES):
-            nc.sync.dma_start(bias[r], b[r * P:(r + 1) * P, :])
-        load_gate(len(FIRST_GATES) + 1)
-        load_gate(len(FIRST_GATES) + 2)
-        load_words(3, E)
-        load_scales(4, E)
+        load_gate(*CHUNKS[1])
+        load_gate(CHUNKS[2][0], S - CHUNKS[2][0])
+        for q in range(4):
+            nc.sync.dma_start(ws_sb[32 * q:32 * q + 4, :, :].bitcast(I32), scale_rows[4 * q:4 * q + 4, :, :])
+        nc.sync.dma_start(w_sb[:].bitcast(I32), word_rows)
+        nc.sync.dma_start(bias[:], b.rearrange("(r p) e -> p r e", p=P))
         for l, pos in enumerate((pos1, pos2, pos3)):
             nc.sync.dma_start(pos_sb[l][:], pos)
 
-        def gather(c, which):
+        def window(j, s0, n):
+            return planes[j][:].indirect(offs_sb[:, s0 // 16:(s0 + n) // 16])
+
+        def gather_times_gate():
+            n = CHUNKS[0][1]
+            for j in range(PACK):
+                for at, count in (FIRST_GATES if j == 0 else [(0, n)]):
+                    nc.vector.tensor_tensor(stages[0][:, j * n + at:j * n + at + count], window(j, at, count), gate_sb[:, at:at + count], MULT)
+
+        def gather(c):
             s0, n = CHUNKS[c]
-            for j in which:
-                pieces = FIRST_GATES if (c, j) == (0, 0) else [(0, n)]
-                for at, count in pieces:
-                    to = STAGE_AT[c] + j * n + at
-                    nc.vector.tensor_tensor(
-                        stage[:, to:to + count],
-                        planes[j][:].indirect(offs_sb[:, (s0 + at) // 16:(s0 + at + count) // 16]),
-                        gate_sb[:, s0 + at:s0 + at + count],
-                        MULT,
-                    )
+            for j in range(PACK):
+                nc.scalar.activation(stages[c][:, j * n:(j + 1) * n], window(j, s0, n), COPY)
 
         def woven(s0, n):
-            if s0 == CHUNKS[-1][0]:
-                return ys[0][:, 7 * C:8 * C].bitcast(BF16)
+            if s0 >= 8 * C:
+                return ys[1][:, 3 * C:5 * C].bitcast(BF16)
+            if s0 >= 7 * C:
+                return ys[1][:, 5 * C:7 * C].bitcast(BF16)
             return x_bf[:, PACK * s0:PACK * (s0 + n)]
 
-        def weave(c, at, count):
-            s0, n = CHUNKS[c]
-            staged = stage[:, STAGE_AT[c]:STAGE_AT[c] + PACK * n].rearrange("p (t s) -> p t s", t=PACK)
-            nc.scalar.copy(
-                woven(s0 + at, count).rearrange("p (c i t) -> p c t i", i=4, t=PACK),
-                staged[:, :, at:at + count].rearrange("p t (c i) -> p c t i", i=4),
-            )
+        def weave(c, s0, n):
+            at = s0 - CHUNKS[c][0]
+            staged = stages[c][:].rearrange("p (t s) -> p t s", t=PACK)[:, :, at:at + n].rearrange("p t (c i) -> p c t i", i=4)
+            to = woven(s0, n).rearrange("p (c i t) -> p c t i", i=4, t=PACK)
+            if c == 0:
+                nc.vector.tensor_copy(to, staged)
+            else:
+                weights = gate_sb[:, s0:s0 + n].rearrange("p (c i) -> p c i", i=4).unsqueeze(2).to_broadcast([P, n // 4, PACK, 4])
+                nc.vector.tensor_tensor(to, staged, weights, MULT)
 
         def quantize(s0, n):
-            nc.vector.quantize_mx(
-                out=x_codes[:, s0:s0 + n].bitcast(FP8X4),
-                scales=x_scales[:, s0:s0 + n],
-                in_=woven(s0, n),
-            )
+            nc.vector.quantize_mx(out=x_codes[:, s0:s0 + n].bitcast(FP8X4), scales=x_scales[:, s0:s0 + n], in_=woven(s0, n))
 
-        def multiply(bank, at, r, s0, n):
-            e = s0 // C
+        made = []
+
+        def expert(r, e, on_vector=False):
+            bank = banks[len(made) % 8]
+            made.append((r, e))
+            cols = slice(e * C, (e + 1) * C)
             nc.tensor.matmul_mx(
-                out=banks[bank][:, at:at + n],
+                out=bank[:, 0:C],
                 lhsT=w_sb[:, e, 2 * P * r:2 * P * (r + 1)].bitcast(FP4X4),
                 lhsT_scale=ws_sb[:, e, P * r:P * (r + 1)],
-                rhs=x_codes[:, s0:s0 + n].bitcast(FP8X4),
-                rhs_scale=x_scales[:, s0:s0 + n],
+                rhs=x_codes[:, cols].bitcast(FP8X4),
+                rhs_scale=x_scales[:, cols],
                 start=True,
                 stop=True,
             )
+            if on_vector:
+                nc.vector.tensor_scalar(ys[r][:, cols], bank[:, 0:C], bias[:, r, e:e + 1], 0.0, ADD, MAX)
+            else:
+                nc.scalar.activation(ys[r][:, cols], bank[:, 0:C], RELU, bias=bias[:, r, e:e + 1])
 
-        def relu(bank, at, r, s0, n):
-            e = s0 // C
-            nc.scalar.activation(ys[r][:, s0:s0 + n], banks[bank][:, at:at + n], RELU, bias=bias[r][:, e:e + 1])
-
-        def relu_on_vector(bank, at, r, s0, n):
-            e = s0 // C
-            nc.vector.tensor_scalar(ys[r][:, s0:s0 + n], banks[bank][:, at:at + n], bias[r][:, e:e + 1], 0.0, ADD, MAX)
-
-        def experts(bank, r, *es):
-            for i, e in enumerate(es):
-                multiply(bank, i * C, r, e * C, C)
-            for i, e in enumerate(es):
-                relu(bank, i * C, r, e * C, C)
-
-        gather(0, range(PACK))
-        weave(0, 0, FIRST_WEAVE)
-        weave(0, FIRST_WEAVE, CHUNKS[0][1] - FIRST_WEAVE)
-        gather(1, (0, 1))
-        quantize(0, 2 * C)
-        for r in range(2):
-            for e in range(2):
-                experts(2 * r + e, r, e)
-        gather(1, (2,))
-        quantize(2 * C, C)
-        experts(4, 0, 2)
-        gather(1, (3,))
-        weave(1, 0, CHUNKS[1][1])
-        gather(2, range(PACK))
-        weave(2, 0, CHUNKS[2][1])
-        quantize(3 * C, 2 * C)
-        quantize(5 * C, C)
-        experts(0, 0, 3)
-        gather(3, range(PACK))
-        weave(3, 0, CHUNKS[3][1])
-        experts(1, 0, 4)
-        experts(2, 0, 5)
-        for h in range(2):
-            quantize((6 + h) * C, C)
-            multiply(6 + h, 0, 0, (6 + h) * C, C)
-        for h in range(2):
-            multiply(4 + h, 0, 1, (3 + h) * C, C)
-        for h in range(2):
-            quantize(8 * C + h * P, P)
-            multiply(4 + h, C, 0, 8 * C + h * P, P)
-        relu(6, 0, 0, 6 * C, C)
-        relu_on_vector(7, 0, 0, 7 * C, C)
-        for h in range(2):
-            relu(4 + h, C, 0, 8 * C + h * P, P)
-        for h in range(2):
-            relu(4 + h, 0, 1, (3 + h) * C, C)
-        experts(3, 1, 8, 5)
-        experts(6, 1, 6, 7)
-        experts(7, 1, 2)
-        for bank, e0 in zip((4, 5, 3, 6, 7), range(0, E, 2)):
-            experts(bank, 2, *range(e0, min(e0 + 2, E)))
-
-        def fetch(r, l, t0, n):
+        def fetch(r, l, t0, n, on_scalar=False):
             found = ys[r][:].indirect(pos_sb[l][:, t0 // 16:(t0 + n) // 16])
-            if l == 0:
+            if on_scalar:
+                nc.scalar.activation(sums[r][l][:, t0:t0 + n], found, COPY)
+            elif l == 0:
                 nc.vector.tensor_copy(sums[r][l][:, t0:t0 + n], found)
             else:
                 nc.vector.tensor_tensor(sums[r][l][:, t0:t0 + n], found, sums[r][l - 1][:, t0:t0 + n], ADD)
             if l == 2:
                 nc.sync.dma_start(out[r * P:(r + 1) * P, t0:t0 + n], sums[r][l][:, t0:t0 + n])
 
-        for l in range(2):
-            for t0 in (0, T // 2):
-                fetch(0, l, t0, T // 2)
-        for r, l in ((1, 0), (0, 2), (2, 0), (1, 1), (2, 1), (1, 2)):
-            fetch(r, l, 0, T)
+        gather_times_gate()
+        for c in range(1, len(CHUNKS)):
+            gather(c)
+        weave(0, 0, 640)
+        weave(1, 640, 384)
+        quantize(0, 2 * C)
+        for r in range(2):
+            for e in range(2):
+                expert(r, e)
+        weave(1, 1024, 384)
+        quantize(2 * C, 2 * C)
+        expert(0, 2)
+        expert(0, 3)
+        expert(1, 2)
+        weave(2, *CHUNKS[2])
+        quantize(4 * C, C)
+        expert(0, 4)
+        weave(3, *CHUNKS[3])
+        quantize(5 * C, 2 * C)
+        expert(0, 5)
+        expert(0, 6)
+        weave(4, *CHUNKS[4])
+        quantize(7 * C, C)
+        quantize(8 * C, C)
+        expert(0, 7, on_vector=True)
+        expert(0, 8)
+
+        fetch(0, 0, 0, HALF)
+        fetch(0, 0, HALF, HALF, on_scalar=True)
+        for e in range(3, E):
+            expert(1, e)
+        for h in range(2):
+            fetch(1, 0, h * HALF, HALF, on_scalar=True)
+        for e in range(E):
+            expert(2, e)
+        for h in range(2):
+            fetch(2, 0, h * HALF, HALF, on_scalar=True)
+        for l in (1, 2):
+            for h in (1, 0):
+                fetch(0, l, h * HALF, HALF)
+        for l in (1, 2):
+            for h in range(2):
+                fetch(1, l, h * HALF, HALF)
+        for h in range(2):
+            fetch(2, 1, h * HALF, HALF)
         for t0, n in LAST_PIECES:
             fetch(2, 2, t0, n)

@@ -27,9 +27,9 @@ BANK = 512
 ROW_TILES = N // P
 HALF = T // 2
 
-CHUNKS = [(0, 640), (640, 768), (1408, 384), (1792, 256), (2048, 256)]
+CHUNKS = [(0, 768), (768, 768), (1536, 768)]
 WINDOW = 800
-FIRST_GATES = [(0, 128), (128, 192), (320, 320)]
+FIRST_GATES = [(0, 128), (128, 256), (384, 384)]
 LAST_PIECES = [(0, 384), (384, 256), (640, 128)]
 
 
@@ -43,13 +43,18 @@ def tile_moe_pre_lin_relu_kernel(tc, xT, w_words, w_scales, b, gate, offs, pos1,
         offs_sb = keep.tile([P, S // 16], U16, name="offs_sb")
         pos_sb = [keep.tile([P, T // 16], U16, name="pos_sb%d" % l) for l in range(3)]
 
-        def tile(shape, dtype, name):
-            return data.tile(shape, dtype, name=name, align_bytes=256)
+        def tile(shape, dtype, name, tag=None):
+            return data.tile(shape, dtype, name=name, tag=tag or name, align_bytes=256)
 
         planes = [tile([P, WINDOW], F32, "plane%d" % j) for j in range(PACK)]
-        stages = [tile([P, PACK * n], F32, "stage%d" % c) for c, (s0, n) in enumerate(CHUNKS)]
-        gate_sb = tile([P, S], F32, "gate_sb")
-        x_bf = tile([P, 7 * C * PACK], BF16, "x_bf")
+        gate_sb = [tile([P, n], F32, "gate%d" % c, "shared" if c == 1 else None) for c, (s0, n) in enumerate(CHUNKS)]
+        stages = [tile([P, PACK * n], F32, "stage%d" % c, "shared" if c == 2 else None)[:] for c, (s0, n) in enumerate(CHUNKS)]
+
+        def gates(s0, n):
+            c = s0 // CHUNKS[0][1]
+            return gate_sb[c][:, s0 - CHUNKS[c][0]:s0 + n - CHUNKS[c][0]]
+
+        x_bf = tile([P, 6 * C * PACK], BF16, "x_bf")
         ys = [tile([P, S], F32, "y%d" % r) for r in range(ROW_TILES)]
         w_sb = tile([P, E, 2 * N], U8, "w_sb")
         ws_sb = tile([P, E, N], U8, "ws_sb")
@@ -57,7 +62,12 @@ def tile_moe_pre_lin_relu_kernel(tc, xT, w_words, w_scales, b, gate, offs, pos1,
         x_scales = tile([P, S], U8, "x_scales")
         bias = tile([P, ROW_TILES, E], F32, "bias")
         sums = [[tile([P, T], F32, "sum%d_%d" % (r, l)) for l in range(3)] for r in range(ROW_TILES)]
+        extra = [None] + [tile([P, T], F32, "extra%d" % r) for r in (1, 2)]
         banks = [psum.tile([P, BANK], F32, name="bank%d" % i) for i in range(8)]
+
+        spare = tile([P, 2], F32, "spare")
+        nc.gpsimd.memset(spare[:, 0:1], 0.0)
+        nc.scalar.activation(spare[:, 1:2], spare[:, 0:1], RELU)
 
         nc.gpsimd.memset(ws_sb[:].rearrange("p e n -> p (e n)").bitcast(I32), 0)
 
@@ -66,16 +76,16 @@ def tile_moe_pre_lin_relu_kernel(tc, xT, w_words, w_scales, b, gate, offs, pos1,
         word_rows = w_words.rearrange("e a p n -> p (e a) n").bitcast(I32)
 
         def load_gate(s0, n):
-            nc.sync.dma_start(gate_sb[:, s0:s0 + n], gate[0:P, s0:s0 + n])
+            nc.sync.dma_start(gates(s0, n), gate[0:P, s0:s0 + n])
 
         nc.sync.dma_start(planes[0][:, 0:T], x_rows[:, 0, :])
         nc.sync.dma_start(offs_sb[:], offs)
-        for s0, n in FIRST_GATES:
-            load_gate(s0, n)
+        for at, n in FIRST_GATES:
+            load_gate(CHUNKS[1][0] + at, n)
         for j in range(1, PACK):
             nc.sync.dma_start(planes[j][:, 0:T], x_rows[:, j, :])
-        load_gate(*CHUNKS[1])
-        load_gate(CHUNKS[2][0], S - CHUNKS[2][0])
+        load_gate(*CHUNKS[0])
+        load_gate(*CHUNKS[2])
         for q in range(4):
             nc.sync.dma_start(ws_sb[32 * q:32 * q + 4, :, :].bitcast(I32), scale_rows[4 * q:4 * q + 4, :, :])
         nc.sync.dma_start(w_sb[:].bitcast(I32), word_rows)
@@ -87,10 +97,10 @@ def tile_moe_pre_lin_relu_kernel(tc, xT, w_words, w_scales, b, gate, offs, pos1,
             return planes[j][:].indirect(offs_sb[:, s0 // 16:(s0 + n) // 16])
 
         def gather_times_gate():
-            n = CHUNKS[0][1]
+            s0, n = CHUNKS[1]
             for j in range(PACK):
                 for at, count in (FIRST_GATES if j == 0 else [(0, n)]):
-                    nc.vector.tensor_tensor(stages[0][:, j * n + at:j * n + at + count], window(j, at, count), gate_sb[:, at:at + count], MULT)
+                    nc.vector.tensor_tensor(stages[1][:, j * n + at:j * n + at + count], window(j, s0 + at, count), gates(s0 + at, count), MULT)
 
         def gather(c):
             s0, n = CHUNKS[c]
@@ -98,44 +108,45 @@ def tile_moe_pre_lin_relu_kernel(tc, xT, w_words, w_scales, b, gate, offs, pos1,
                 nc.scalar.activation(stages[c][:, j * n:(j + 1) * n], window(j, s0, n), COPY)
 
         def woven(s0, n):
-            if s0 >= 8 * C:
-                return ys[1][:, 3 * C:5 * C].bitcast(BF16)
-            if s0 >= 7 * C:
-                return ys[1][:, 5 * C:7 * C].bitcast(BF16)
+            if s0 >= 6 * C:
+                s0 = s0 % C + 2 * (s0 // C - 6) * C
             return x_bf[:, PACK * s0:PACK * (s0 + n)]
 
         def weave(c, s0, n):
             at = s0 - CHUNKS[c][0]
-            staged = stages[c][:].rearrange("p (t s) -> p t s", t=PACK)[:, :, at:at + n].rearrange("p t (c i) -> p c t i", i=4)
+            staged = stages[c].rearrange("p (t s) -> p t s", t=PACK)[:, :, at:at + n].rearrange("p t (c i) -> p c t i", i=4)
             to = woven(s0, n).rearrange("p (c i t) -> p c t i", i=4, t=PACK)
-            if c == 0:
+            if c == 1:
                 nc.vector.tensor_copy(to, staged)
             else:
-                weights = gate_sb[:, s0:s0 + n].rearrange("p (c i) -> p c i", i=4).unsqueeze(2).to_broadcast([P, n // 4, PACK, 4])
+                weights = gates(s0, n).rearrange("p (c i) -> p c i", i=4).unsqueeze(2).to_broadcast([P, n // 4, PACK, 4])
                 nc.vector.tensor_tensor(to, staged, weights, MULT)
 
         def quantize(s0, n):
             nc.vector.quantize_mx(out=x_codes[:, s0:s0 + n].bitcast(FP8X4), scales=x_scales[:, s0:s0 + n], in_=woven(s0, n))
 
-        made = []
-
-        def expert(r, e, on_vector=False):
-            bank = banks[len(made) % 8]
-            made.append((r, e))
-            cols = slice(e * C, (e + 1) * C)
+        def multiply(bank, at, r, s0, n):
+            e = s0 // C
             nc.tensor.matmul_mx(
-                out=bank[:, 0:C],
+                out=banks[bank][:, at:at + n],
                 lhsT=w_sb[:, e, 2 * P * r:2 * P * (r + 1)].bitcast(FP4X4),
                 lhsT_scale=ws_sb[:, e, P * r:P * (r + 1)],
-                rhs=x_codes[:, cols].bitcast(FP8X4),
-                rhs_scale=x_scales[:, cols],
+                rhs=x_codes[:, s0:s0 + n].bitcast(FP8X4),
+                rhs_scale=x_scales[:, s0:s0 + n],
                 start=True,
                 stop=True,
             )
+
+        def relu(bank, at, r, s0, n, on_vector=False):
+            e = s0 // C
             if on_vector:
-                nc.vector.tensor_scalar(ys[r][:, cols], bank[:, 0:C], bias[:, r, e:e + 1], 0.0, ADD, MAX)
+                nc.vector.tensor_scalar(ys[r][:, s0:s0 + n], banks[bank][:, at:at + n], bias[:, r, e:e + 1], 0.0, ADD, MAX)
             else:
-                nc.scalar.activation(ys[r][:, cols], bank[:, 0:C], RELU, bias=bias[:, r, e:e + 1])
+                nc.scalar.activation(ys[r][:, s0:s0 + n], banks[bank][:, at:at + n], RELU, bias=bias[:, r, e:e + 1])
+
+        def expert(bank, r, e):
+            multiply(bank, 0, r, e * C, C)
+            relu(bank, 0, r, e * C, C)
 
         def fetch(r, l, t0, n, on_scalar=False):
             found = ys[r][:].indirect(pos_sb[l][:, t0 // 16:(t0 + n) // 16])
@@ -149,49 +160,68 @@ def tile_moe_pre_lin_relu_kernel(tc, xT, w_words, w_scales, b, gate, offs, pos1,
                 nc.sync.dma_start(out[r * P:(r + 1) * P, t0:t0 + n], sums[r][l][:, t0:t0 + n])
 
         gather_times_gate()
-        for c in range(1, len(CHUNKS)):
-            gather(c)
-        weave(0, 0, 640)
-        weave(1, 640, 384)
+        gather(0)
+        gather(2)
+        weave(0, *CHUNKS[0])
+        weave(1, *CHUNKS[1])
         quantize(0, 2 * C)
-        for r in range(2):
+        for r in range(ROW_TILES):
             for e in range(2):
-                expert(r, e)
-        weave(1, 1024, 384)
+                expert(2 * r + e, r, e)
         quantize(2 * C, 2 * C)
-        expert(0, 2)
-        expert(0, 3)
-        expert(1, 2)
-        weave(2, *CHUNKS[2])
-        quantize(4 * C, C)
-        expert(0, 4)
-        weave(3, *CHUNKS[3])
-        quantize(5 * C, 2 * C)
-        expert(0, 5)
-        expert(0, 6)
-        weave(4, *CHUNKS[4])
+        for r in range(ROW_TILES):
+            for e in (2, 3):
+                expert((6 + 2 * r + e - 2) % 8, r, e)
+        weave(2, 6 * C, C)
+        quantize(4 * C, 2 * C)
+        for r in range(2):
+            for e in (4, 5):
+                expert(4 + 2 * r + e - 4, r, e)
+        weave(2, 7 * C, C)
+        quantize(6 * C, C)
+        multiply(0, 0, 0, 6 * C, C)
+        for h in range(2):
+            multiply(2 + h, 0, 2, (4 + h) * C, C)
+        weave(2, 8 * C, C)
         quantize(7 * C, C)
-        quantize(8 * C, C)
-        expert(0, 7, on_vector=True)
-        expert(0, 8)
+        multiply(1, 0, 0, 7 * C, C)
+        for h in range(2):
+            quantize(8 * C + h * P, P)
+            multiply(2 + h, C, 0, 8 * C + h * P, P)
+        for h in range(2):
+            relu(h, 0, 0, (6 + h) * C, C, on_vector=True)
+        for h in range(2):
+            relu(2 + h, C, 0, 8 * C + h * P, P)
 
         fetch(0, 0, 0, HALF)
         fetch(0, 0, HALF, HALF, on_scalar=True)
-        for e in range(3, E):
-            expert(1, e)
+        for bank, e in ((4, 8), (0, 6), (1, 7)):
+            expert(bank, 1, e)
+        fetch(1, 0, 0, T, on_scalar=True)
+        fetch(1, 1, HALF, HALF, on_scalar=True)
         for h in range(2):
-            fetch(1, 0, h * HALF, HALF, on_scalar=True)
-        for e in range(E):
-            expert(2, e)
-        for h in range(2):
-            fetch(2, 0, h * HALF, HALF, on_scalar=True)
+            relu(2 + h, 0, 2, (4 + h) * C, C)
+        for bank, e in ((5, 8), (0, 6), (1, 7)):
+            expert(bank, 2, e)
+        for l in range(2):
+            for h in range(2):
+                fetch(2, l, h * HALF, HALF, on_scalar=True)
+
+        def third(r, t0, n):
+            nc.vector.tensor_tensor(extra[r][:, t0:t0 + n], ys[r][:].indirect(pos_sb[2][:, t0 // 16:(t0 + n) // 16]), sums[r][0][:, t0:t0 + n], ADD)
+
+        def finish(r, t0, n):
+            nc.vector.tensor_tensor(sums[r][2][:, t0:t0 + n], extra[r][:, t0:t0 + n], sums[r][1][:, t0:t0 + n], ADD)
+            nc.sync.dma_start(out[r * P:(r + 1) * P, t0:t0 + n], sums[r][2][:, t0:t0 + n])
+
         for l in (1, 2):
             for h in (1, 0):
                 fetch(0, l, h * HALF, HALF)
-        for l in (1, 2):
-            for h in range(2):
-                fetch(1, l, h * HALF, HALF)
+        fetch(1, 1, 0, HALF)
+        third(1, HALF, HALF)
+        fetch(1, 2, 0, HALF)
+        finish(1, HALF, HALF)
         for h in range(2):
-            fetch(2, 1, h * HALF, HALF)
+            third(2, h * HALF, HALF)
         for t0, n in LAST_PIECES:
-            fetch(2, 2, t0, n)
+            finish(2, t0, n)

@@ -27,9 +27,9 @@ BANK = 512
 ROW_TILES = N // P
 HALF = T // 2
 
-CHUNKS = [(0, 768), (768, 768), (1536, 768)]
-WINDOW = 800
-FIRST_GATES = [(0, 128), (128, 256), (384, 384)]
+CHUNKS = [(0, 736), (736, 800), (1536, 768)]
+WINDOW = 832
+FIRST_GATES = [(0, 128), (128, 256), (384, 352)]
 LAST_PIECES = [(0, 384), (384, 256), (640, 128)]
 
 
@@ -47,11 +47,11 @@ def tile_moe_pre_lin_relu_kernel(tc, xT, w_words, w_scales, b, gate, offs, pos1,
             return data.tile(shape, dtype, name=name, tag=tag or name, align_bytes=256)
 
         planes = [tile([P, WINDOW], F32, "plane%d" % j) for j in range(PACK)]
-        gate_sb = [tile([P, n], F32, "gate%d" % c, "shared" if c == 1 else None) for c, (s0, n) in enumerate(CHUNKS)]
+        gate_sb = [tile([P, n], F32, "gate%d" % c, "shared" if c == 0 else None) for c, (s0, n) in enumerate(CHUNKS)]
         stages = [tile([P, PACK * n], F32, "stage%d" % c, "shared" if c == 2 else None)[:] for c, (s0, n) in enumerate(CHUNKS)]
 
         def gates(s0, n):
-            c = s0 // CHUNKS[0][1]
+            c = max(i for i, (first, count) in enumerate(CHUNKS) if first <= s0)
             return gate_sb[c][:, s0 - CHUNKS[c][0]:s0 + n - CHUNKS[c][0]]
 
         x_bf = tile([P, 6 * C * PACK], BF16, "x_bf")
@@ -81,15 +81,15 @@ def tile_moe_pre_lin_relu_kernel(tc, xT, w_words, w_scales, b, gate, offs, pos1,
         nc.sync.dma_start(planes[0][:, 0:T], x_rows[:, 0, :])
         nc.sync.dma_start(offs_sb[:], offs)
         for at, n in FIRST_GATES:
-            load_gate(CHUNKS[1][0] + at, n)
+            load_gate(at, n)
         for j in range(1, PACK):
             nc.sync.dma_start(planes[j][:, 0:T], x_rows[:, j, :])
-        load_gate(*CHUNKS[0])
-        load_gate(*CHUNKS[2])
+        load_gate(*CHUNKS[1])
         for q in range(4):
             nc.sync.dma_start(ws_sb[32 * q:32 * q + 4, :, :].bitcast(I32), scale_rows[4 * q:4 * q + 4, :, :])
         nc.sync.dma_start(w_sb[:].bitcast(I32), word_rows)
         nc.sync.dma_start(bias[:], b.rearrange("(r p) e -> p r e", p=P))
+        load_gate(*CHUNKS[2])
         for l, pos in enumerate((pos1, pos2, pos3)):
             nc.sync.dma_start(pos_sb[l][:], pos)
 
@@ -97,10 +97,10 @@ def tile_moe_pre_lin_relu_kernel(tc, xT, w_words, w_scales, b, gate, offs, pos1,
             return planes[j][:].indirect(offs_sb[:, s0 // 16:(s0 + n) // 16])
 
         def gather_times_gate():
-            s0, n = CHUNKS[1]
+            s0, n = CHUNKS[0]
             for j in range(PACK):
                 for at, count in (FIRST_GATES if j == 0 else [(0, n)]):
-                    nc.vector.tensor_tensor(stages[1][:, j * n + at:j * n + at + count], window(j, s0 + at, count), gates(s0 + at, count), MULT)
+                    nc.vector.tensor_tensor(stages[0][:, j * n + at:j * n + at + count], window(j, s0 + at, count), gates(s0 + at, count), MULT)
 
         def gather(c):
             s0, n = CHUNKS[c]
@@ -109,14 +109,14 @@ def tile_moe_pre_lin_relu_kernel(tc, xT, w_words, w_scales, b, gate, offs, pos1,
 
         def woven(s0, n):
             if s0 >= 6 * C:
-                s0 = s0 % C + 2 * (s0 // C - 6) * C
+                s0 = s0 % C + (2, 4, 0)[s0 // C - 6] * C
             return x_bf[:, PACK * s0:PACK * (s0 + n)]
 
         def weave(c, s0, n):
             at = s0 - CHUNKS[c][0]
             staged = stages[c].rearrange("p (t s) -> p t s", t=PACK)[:, :, at:at + n].rearrange("p t (c i) -> p c t i", i=4)
             to = woven(s0, n).rearrange("p (c i t) -> p c t i", i=4, t=PACK)
-            if c == 1:
+            if c == 0:
                 nc.vector.tensor_copy(to, staged)
             else:
                 weights = gates(s0, n).rearrange("p (c i) -> p c i", i=4).unsqueeze(2).to_broadcast([P, n // 4, PACK, 4])
@@ -160,52 +160,51 @@ def tile_moe_pre_lin_relu_kernel(tc, xT, w_words, w_scales, b, gate, offs, pos1,
                 nc.sync.dma_start(out[r * P:(r + 1) * P, t0:t0 + n], sums[r][l][:, t0:t0 + n])
 
         gather_times_gate()
-        gather(0)
+        gather(1)
         gather(2)
         weave(0, *CHUNKS[0])
         weave(1, *CHUNKS[1])
-        quantize(0, 2 * C)
-        for r in range(ROW_TILES):
-            for e in range(2):
-                expert(2 * r + e, r, e)
-        quantize(2 * C, 2 * C)
-        for r in range(ROW_TILES):
-            for e in (2, 3):
-                expert((6 + 2 * r + e - 2) % 8, r, e)
+        for e in (0, 2, 4):
+            quantize(e * C, 2 * C)
+        for e in range(2):
+            multiply(e, 0, 0, e * C, C)
+            relu(e, 0, 0, e * C, C, on_vector=True)
+        early = [(r, e) for r in (1, 2) for e in (0, 1)] + [(r, e) for r in range(3) for e in (2, 3)] + [(0, 4), (0, 5), (1, 4), (1, 5)]
+        for i, (r, e) in enumerate(early):
+            expert((2 + i) % 8, r, e)
         weave(2, 6 * C, C)
-        quantize(4 * C, 2 * C)
-        for r in range(2):
-            for e in (4, 5):
-                expert(4 + 2 * r + e - 4, r, e)
         weave(2, 7 * C, C)
         quantize(6 * C, C)
-        multiply(0, 0, 0, 6 * C, C)
-        for h in range(2):
-            multiply(2 + h, 0, 2, (4 + h) * C, C)
+        multiply(1, 0, 0, 6 * C, C)
+        multiply(1, C, 2, 5 * C, C)
+        multiply(4, 0, 1, 6 * C, C)
         weave(2, 8 * C, C)
         quantize(7 * C, C)
-        multiply(1, 0, 0, 7 * C, C)
+        multiply(2, C, 2, 4 * C, C)
+        multiply(2, 0, 0, 7 * C, C)
         for h in range(2):
             quantize(8 * C + h * P, P)
-            multiply(2 + h, C, 0, 8 * C + h * P, P)
+            multiply(3 + h, C, 0, 8 * C + h * P, P)
         for h in range(2):
-            relu(h, 0, 0, (6 + h) * C, C, on_vector=True)
+            relu(1 + h, 0, 0, (6 + h) * C, C, on_vector=True)
         for h in range(2):
-            relu(2 + h, C, 0, 8 * C + h * P, P)
+            relu(3 + h, C, 0, 8 * C + h * P, P)
+        for h in range(2):
+            relu(2 - h, C, 2, (4 + h) * C, C, on_vector=True)
 
         fetch(0, 0, 0, HALF)
         fetch(0, 0, HALF, HALF, on_scalar=True)
-        for bank, e in ((4, 8), (0, 6), (1, 7)):
+        relu(4, 0, 1, 6 * C, C)
+        for bank, e in ((5, 8), (3, 7)):
             expert(bank, 1, e)
         fetch(1, 0, 0, T, on_scalar=True)
-        fetch(1, 1, HALF, HALF, on_scalar=True)
-        for h in range(2):
-            relu(2 + h, 0, 2, (4 + h) * C, C)
-        for bank, e in ((5, 8), (0, 6), (1, 7)):
+        for bank, e in ((6, 8), (4, 6), (2, 7)):
             expert(bank, 2, e)
-        for l in range(2):
-            for h in range(2):
-                fetch(2, l, h * HALF, HALF, on_scalar=True)
+        fetch(2, 0, 0, HALF, on_scalar=True)
+        fetch(1, 1, 0, T, on_scalar=True)
+        fetch(2, 0, HALF, HALF, on_scalar=True)
+        for h in range(2):
+            fetch(2, 1, h * HALF, HALF, on_scalar=True)
 
         def third(r, t0, n):
             nc.vector.tensor_tensor(extra[r][:, t0:t0 + n], ys[r][:].indirect(pos_sb[2][:, t0 // 16:(t0 + n) // 16]), sums[r][0][:, t0:t0 + n], ADD)
@@ -217,11 +216,9 @@ def tile_moe_pre_lin_relu_kernel(tc, xT, w_words, w_scales, b, gate, offs, pos1,
         for l in (1, 2):
             for h in (1, 0):
                 fetch(0, l, h * HALF, HALF)
-        fetch(1, 1, 0, HALF)
-        third(1, HALF, HALF)
-        fetch(1, 2, 0, HALF)
-        finish(1, HALF, HALF)
-        for h in range(2):
-            third(2, h * HALF, HALF)
+        third(1, 0, T)
+        third(2, 0, HALF)
+        finish(1, 0, T)
+        third(2, HALF, HALF)
         for t0, n in LAST_PIECES:
             finish(2, t0, n)

@@ -27,9 +27,10 @@ BANK = 512
 ROW_TILES = N // P
 HALF = T // 2
 
-CHUNKS = [(0, 736), (736, 800), (1536, 768)]
-WINDOW = 832
-FIRST_GATES = [(0, 128), (128, 256), (384, 352)]
+CHUNKS = [(0, 640), (640, 896), (1536, 768)]
+WINDOW = 928
+HEAD = 384
+OVERLAP = 32
 LAST_PIECES = [(0, 384), (384, 256), (640, 128)]
 
 
@@ -47,8 +48,12 @@ def tile_moe_pre_lin_relu_kernel(tc, xT, w_words, w_scales, b, gate, offs, pos1,
             return data.tile(shape, dtype, name=name, tag=tag or name, align_bytes=256)
 
         planes = [tile([P, WINDOW], F32, "plane%d" % j) for j in range(PACK)]
-        gate_sb = [tile([P, n], F32, "gate%d" % c, "shared" if c == 0 else None) for c, (s0, n) in enumerate(CHUNKS)]
-        stages = [tile([P, PACK * n], F32, "stage%d" % c, "shared" if c == 2 else None)[:] for c, (s0, n) in enumerate(CHUNKS)]
+        n0, n1, n2 = [n for s0, n in CHUNKS]
+        at2 = PACK * n0 - OVERLAP
+        shared = tile([P, at2 + PACK * n2], F32, "shared")
+        stages = [shared[:, 0:PACK * n0], tile([P, PACK * n1], F32, "stage1")[:], shared[:, at2:at2 + PACK * n2]]
+        gate_at = at2 + 2 * n2 - OVERLAP
+        gate_sb = [shared[:, gate_at:gate_at + n0], tile([P, n1], F32, "gate1"), tile([P, n2], F32, "gate2")]
 
         def gates(s0, n):
             c = max(i for i, (first, count) in enumerate(CHUNKS) if first <= s0)
@@ -80,8 +85,7 @@ def tile_moe_pre_lin_relu_kernel(tc, xT, w_words, w_scales, b, gate, offs, pos1,
 
         nc.sync.dma_start(planes[0][:, 0:T], x_rows[:, 0, :])
         nc.sync.dma_start(offs_sb[:], offs)
-        for at, n in FIRST_GATES:
-            load_gate(at, n)
+        load_gate(*CHUNKS[0])
         for j in range(1, PACK):
             nc.sync.dma_start(planes[j][:, 0:T], x_rows[:, j, :])
         load_gate(*CHUNKS[1])
@@ -99,13 +103,11 @@ def tile_moe_pre_lin_relu_kernel(tc, xT, w_words, w_scales, b, gate, offs, pos1,
         def gather_times_gate():
             s0, n = CHUNKS[0]
             for j in range(PACK):
-                for at, count in (FIRST_GATES if j == 0 else [(0, n)]):
-                    nc.vector.tensor_tensor(stages[0][:, j * n + at:j * n + at + count], window(j, s0 + at, count), gates(s0 + at, count), MULT)
+                nc.vector.tensor_tensor(stages[0][:, j * n:(j + 1) * n], window(j, s0, n), gates(s0, n), MULT)
 
-        def gather(c):
+        def gather(c, j, count):
             s0, n = CHUNKS[c]
-            for j in range(PACK):
-                nc.scalar.activation(stages[c][:, j * n:(j + 1) * n], window(j, s0, n), COPY)
+            nc.scalar.activation(stages[c][:, j * n:j * n + count], window(j, s0, count), COPY)
 
         def woven(s0, n):
             if s0 >= 6 * C:
@@ -159,10 +161,14 @@ def tile_moe_pre_lin_relu_kernel(tc, xT, w_words, w_scales, b, gate, offs, pos1,
             if l == 2:
                 nc.sync.dma_start(out[r * P:(r + 1) * P, t0:t0 + n], sums[r][l][:, t0:t0 + n])
 
+        nc.vector.tensor_copy(stages[2][:, n2 - HEAD:n2], window(0, S - HEAD, HEAD))
         gather_times_gate()
-        gather(1)
-        gather(2)
+        for j in range(PACK):
+            gather(1, j, n1)
+        for j in range(1, PACK):
+            gather(2, j, n2)
         weave(0, *CHUNKS[0])
+        gather(2, 0, n2 - HEAD)
         weave(1, *CHUNKS[1])
         for e in (0, 2, 4):
             quantize(e * C, 2 * C)

@@ -26,6 +26,8 @@ PACK = 4
 BANK = 512
 ROW_TILES = N // P
 HALF = T // 2
+STRETCH = 60 * 1024
+WIDTH = {F32: 4, U32: 4, BF16: 2, U8: 1}
 
 CHUNKS = [(0, 640), (640, 896), (1536, 768)]
 WINDOW = 928
@@ -44,37 +46,41 @@ def tile_moe_pre_lin_relu_kernel(tc, xT, w_words, w_scales, b, gate, offs, pos1,
         offs_sb = keep.tile([P, S // 16], U16, name="offs_sb")
         pos_sb = [keep.tile([P, T // 16], U16, name="pos_sb%d" % l) for l in range(3)]
 
-        def tile(shape, dtype, name, tag=None):
-            return data.tile(shape, dtype, name=name, tag=tag or name, align_bytes=256)
+        free = [q * STRETCH for q in range(4)]
 
-        planes = [tile([P, WINDOW], F32, "plane%d" % j) for j in range(PACK)]
+        def tile(q, columns, dtype, name):
+            at = free[q]
+            free[q] = at + -(-columns * WIDTH[dtype] // 256) * 256
+            return data.tile([P, columns], dtype, name=name, align_bytes=256, offset=at)
+
+        planes = [tile(j, WINDOW, F32, "plane%d" % j) for j in range(PACK)]
         n0, n1, n2 = [n for s0, n in CHUNKS]
         at2 = PACK * n0 - OVERLAP
-        shared = tile([P, at2 + PACK * n2], F32, "shared")
-        stages = [shared[:, 0:PACK * n0], tile([P, PACK * n1], F32, "stage1")[:], shared[:, at2:at2 + PACK * n2]]
+        shared = tile(0, at2 + PACK * n2, F32, "shared")
+        stages = [shared[:, 0:PACK * n0], tile(1, PACK * n1, F32, "stage1")[:], shared[:, at2:at2 + PACK * n2]]
         gate_at = at2 + 2 * n2 - OVERLAP
-        gate_sb = [shared[:, gate_at:gate_at + n0], tile([P, n1], F32, "gate1"), tile([P, n2], F32, "gate2")]
+        gate_sb = [shared[:, gate_at:gate_at + n0], tile(2, n1, F32, "gate1"), tile(2, n2, F32, "gate2")]
 
         def gates(s0, n):
             c = max(i for i, (first, count) in enumerate(CHUNKS) if first <= s0)
             return gate_sb[c][:, s0 - CHUNKS[c][0]:s0 + n - CHUNKS[c][0]]
 
-        x_bf = tile([P, 6 * C * PACK], BF16, "x_bf")
-        ys = [tile([P, S], F32, "y%d" % r) for r in range(ROW_TILES)]
-        w_sb = tile([P, E, 2 * N], U8, "w_sb")
-        ws_sb = tile([P, E, N], U8, "ws_sb")
-        x_codes = tile([P, S], U32, "x_codes")
-        x_scales = tile([P, S], U8, "x_scales")
-        bias = tile([P, ROW_TILES, E], F32, "bias")
-        sums = [[tile([P, T], F32, "sum%d_%d" % (r, l)) for l in range(3)] for r in range(ROW_TILES)]
-        extra = [None] + [tile([P, T], F32, "extra%d" % r) for r in (1, 2)]
+        x_bf = tile(3, 6 * C * PACK, BF16, "x_bf")
+        ys = [tile(r, S, F32, "y%d" % r) for r in range(ROW_TILES)]
+        w_sb = tile(2, E * 2 * N, U8, "w_sb")[:].rearrange("p (e n) -> p e n", e=E)
+        ws_sb = tile(1, E * N, U8, "ws_sb")[:].rearrange("p (e n) -> p e n", e=E)
+        x_codes = tile(2, S, U32, "x_codes")
+        x_scales = tile(1, S, U8, "x_scales")
+        bias = tile(3, ROW_TILES * E, F32, "bias")[:].rearrange("p (r e) -> p r e", e=E)
+        sums = [[tile(3, T, F32, "sum%d_%d" % (r, l)) for l in range(3)] for r in range(ROW_TILES)]
+        extra = [None] + [tile(3, T, F32, "extra%d" % r) for r in (1, 2)]
         banks = [psum.tile([P, BANK], F32, name="bank%d" % i) for i in range(8)]
 
-        spare = tile([P, 2], F32, "spare")
+        spare = tile(3, 2, F32, "spare")
         nc.gpsimd.memset(spare[:, 0:1], 0.0)
         nc.scalar.activation(spare[:, 1:2], spare[:, 0:1], RELU)
 
-        nc.gpsimd.memset(ws_sb[:].rearrange("p e n -> p (e n)").bitcast(I32), 0)
+        nc.gpsimd.memset(ws_sb.rearrange("p e n -> p (e n)").bitcast(I32), 0)
 
         x_rows = xT.rearrange("(p j) t -> p j t", j=PACK)
         scale_rows = w_scales.rearrange("e a q n -> q (e a) n").bitcast(I32)
@@ -91,8 +97,8 @@ def tile_moe_pre_lin_relu_kernel(tc, xT, w_words, w_scales, b, gate, offs, pos1,
         load_gate(*CHUNKS[1])
         for q in range(4):
             nc.sync.dma_start(ws_sb[32 * q:32 * q + 4, :, :].bitcast(I32), scale_rows[4 * q:4 * q + 4, :, :])
-        nc.sync.dma_start(w_sb[:].bitcast(I32), word_rows)
-        nc.sync.dma_start(bias[:], b.rearrange("(r p) e -> p r e", p=P))
+        nc.sync.dma_start(w_sb.bitcast(I32), word_rows)
+        nc.sync.dma_start(bias, b.rearrange("(r p) e -> p r e", p=P))
         load_gate(*CHUNKS[2])
         for l, pos in enumerate((pos1, pos2, pos3)):
             nc.sync.dma_start(pos_sb[l][:], pos)

@@ -29,11 +29,10 @@ HALF = T // 2
 STRETCH = 60 * 1024
 WIDTH = {F32: 4, U32: 4, BF16: 2, U8: 1}
 
-CHUNKS = [(0, 640), (640, 896), (1536, 768)]
+CHUNKS = [(0, 640), (640, 896), (1536, 512), (2048, 256)]
 WINDOW = 928
-HEAD = 384
 OVERLAP = 32
-LAST_PIECES = [(0, 384), (384, 256), (640, 128)]
+LAST_PIECES = [(384, 256), (640, 128)]
 
 
 def tile_moe_pre_lin_relu_kernel(tc, xT, w_words, w_scales, b, gate, offs, pos1, pos2, pos3, out):
@@ -54,15 +53,14 @@ def tile_moe_pre_lin_relu_kernel(tc, xT, w_words, w_scales, b, gate, offs, pos1,
             return data.tile([P, columns], dtype, name=name, align_bytes=256, offset=at)
 
         planes = [tile(j, WINDOW, F32, "plane%d" % j) for j in range(PACK)]
-        n0, n1, n2 = [n for s0, n in CHUNKS]
-        at2 = PACK * n0 - OVERLAP
-        shared = tile(0, at2 + PACK * n2, F32, "shared")
-        stages = [shared[:, 0:PACK * n0], tile(1, PACK * n1, F32, "stage1")[:], shared[:, at2:at2 + PACK * n2]]
-        gate_at = at2 + 2 * n2 - OVERLAP
-        gate_sb = [shared[:, gate_at:gate_at + n0], tile(2, n1, F32, "gate1"), tile(2, n2, F32, "gate2")]
+        n0, n1, n2, n3 = [n for s0, n in CHUNKS]
+        stages = [tile(c, PACK * n, F32, "stage%d" % c)[:] for c, n in enumerate((n0, n1, n2))]
+        stages.append(stages[0][:, 0:PACK * n3])
+        gate_at = 2 * n2 - OVERLAP
+        gate_sb = [stages[2][:, gate_at:gate_at + n0], tile(2, n1, F32, "gate1"), tile(3, n2 + n3, F32, "gate2")]
 
         def gates(s0, n):
-            c = max(i for i, (first, count) in enumerate(CHUNKS) if first <= s0)
+            c = max(i for i, (first, count) in enumerate(CHUNKS[:3]) if first <= s0)
             return gate_sb[c][:, s0 - CHUNKS[c][0]:s0 + n - CHUNKS[c][0]]
 
         x_bf = tile(3, 6 * C * PACK, BF16, "x_bf")
@@ -99,7 +97,7 @@ def tile_moe_pre_lin_relu_kernel(tc, xT, w_words, w_scales, b, gate, offs, pos1,
             nc.sync.dma_start(ws_sb[32 * q:32 * q + 4, :, :].bitcast(I32), scale_rows[4 * q:4 * q + 4, :, :])
         nc.sync.dma_start(w_sb.bitcast(I32), word_rows)
         nc.sync.dma_start(bias, b.rearrange("(r p) e -> p r e", p=P))
-        load_gate(*CHUNKS[2])
+        load_gate(CHUNKS[2][0], n2 + n3)
         for l, pos in enumerate((pos1, pos2, pos3)):
             nc.sync.dma_start(pos_sb[l][:], pos)
 
@@ -111,13 +109,14 @@ def tile_moe_pre_lin_relu_kernel(tc, xT, w_words, w_scales, b, gate, offs, pos1,
             for j in range(PACK):
                 nc.vector.tensor_tensor(stages[0][:, j * n:(j + 1) * n], window(j, s0, n), gates(s0, n), MULT)
 
-        def gather(c, j, count):
+        def gather(c, which):
             s0, n = CHUNKS[c]
-            nc.scalar.activation(stages[c][:, j * n:j * n + count], window(j, s0, count), COPY)
+            for j in which:
+                nc.scalar.activation(stages[c][:, j * n:(j + 1) * n], window(j, s0, n), COPY)
 
         def woven(s0, n):
             if s0 >= 6 * C:
-                s0 = s0 % C + (2, 4, 0)[s0 // C - 6] * C
+                s0 = s0 % C + (2, 3, 0)[s0 // C - 6] * C
             return x_bf[:, PACK * s0:PACK * (s0 + n)]
 
         def weave(c, s0, n):
@@ -167,56 +166,43 @@ def tile_moe_pre_lin_relu_kernel(tc, xT, w_words, w_scales, b, gate, offs, pos1,
             if l == 2:
                 nc.sync.dma_start(out[r * P:(r + 1) * P, t0:t0 + n], sums[r][l][:, t0:t0 + n])
 
-        nc.vector.tensor_copy(stages[2][:, n2 - HEAD:n2], window(0, S - HEAD, HEAD))
+        nc.vector.tensor_copy(stages[2][:, 0:n2], window(0, *CHUNKS[2]))
         gather_times_gate()
-        for j in range(PACK):
-            gather(1, j, n1)
-        for j in range(1, PACK):
-            gather(2, j, n2)
+        gather(1, range(PACK))
+        gather(2, range(1, PACK))
         weave(0, *CHUNKS[0])
-        gather(2, 0, n2 - HEAD)
+        gather(3, range(PACK))
         weave(1, *CHUNKS[1])
         for e in (0, 2, 4):
             quantize(e * C, 2 * C)
-        for e in range(2):
-            multiply(e, 0, 0, e * C, C)
-            relu(e, 0, 0, e * C, C, on_vector=True)
-        early = [(r, e) for r in (1, 2) for e in (0, 1)] + [(r, e) for r in range(3) for e in (2, 3)] + [(0, 4), (0, 5), (1, 4), (1, 5)]
+        early = [(r, e) for first in (0, 2, 4) for r in range(ROW_TILES) for e in (first, first + 1)][:-1]
         for i, (r, e) in enumerate(early):
-            expert((2 + i) % 8, r, e)
-        weave(2, 6 * C, C)
-        weave(2, 7 * C, C)
-        quantize(6 * C, C)
+            expert(i % 8, r, e)
+        weave(2, *CHUNKS[2])
+        weave(3, *CHUNKS[3])
+        quantize(6 * C, 2 * C)
         multiply(1, 0, 0, 6 * C, C)
-        multiply(1, C, 2, 5 * C, C)
-        multiply(4, 0, 1, 6 * C, C)
-        weave(2, 8 * C, C)
-        quantize(7 * C, C)
-        multiply(2, C, 2, 4 * C, C)
+        multiply(2, C, 2, 5 * C, C)
         multiply(2, 0, 0, 7 * C, C)
         for h in range(2):
             quantize(8 * C + h * P, P)
-            multiply(3 + h, C, 0, 8 * C + h * P, P)
-        for h in range(2):
+            multiply(3, h * P, 0, 8 * C + h * P, P)
+        for h in range(3):
             relu(1 + h, 0, 0, (6 + h) * C, C, on_vector=True)
-        for h in range(2):
-            relu(3 + h, C, 0, 8 * C + h * P, P)
-        for h in range(2):
-            relu(2 - h, C, 2, (4 + h) * C, C, on_vector=True)
+        relu(2, C, 2, 5 * C, C, on_vector=True)
 
         fetch(0, 0, 0, HALF)
         fetch(0, 0, HALF, HALF, on_scalar=True)
-        relu(4, 0, 1, 6 * C, C)
-        for bank, e in ((5, 8), (3, 7)):
+        for bank, e in ((1, 6), (4, 8), (2, 7)):
             expert(bank, 1, e)
         fetch(1, 0, 0, T, on_scalar=True)
-        for bank, e in ((6, 8), (4, 6), (2, 7)):
+        for bank, e in ((5, 8), (3, 6), (1, 7)):
             expert(bank, 2, e)
         fetch(2, 0, 0, HALF, on_scalar=True)
         fetch(1, 1, 0, T, on_scalar=True)
-        fetch(2, 0, HALF, HALF, on_scalar=True)
-        for h in range(2):
-            fetch(2, 1, h * HALF, HALF, on_scalar=True)
+        fetch(2, 1, 0, HALF, on_scalar=True)
+        for l in range(2):
+            fetch(2, l, HALF, HALF, on_scalar=True)
 
         def third(r, t0, n):
             nc.vector.tensor_tensor(extra[r][:, t0:t0 + n], ys[r][:].indirect(pos_sb[2][:, t0 // 16:(t0 + n) // 16]), sums[r][0][:, t0:t0 + n], ADD)
@@ -231,6 +217,8 @@ def tile_moe_pre_lin_relu_kernel(tc, xT, w_words, w_scales, b, gate, offs, pos1,
         third(1, 0, T)
         third(2, 0, HALF)
         finish(1, 0, T)
-        third(2, HALF, HALF)
+        finish(2, 0, HALF)
+        for t0, n in LAST_PIECES:
+            third(2, t0, n)
         for t0, n in LAST_PIECES:
             finish(2, t0, n)

@@ -92,9 +92,9 @@ def tile_moe_pre_lin_relu_kernel(tc, xT, w_words, w_scales, b, gate, offs, pos1,
         load_gate(*CHUNKS[0])
         for j in range(1, PACK):
             nc.sync.dma_start(planes[j][:, 0:T], x_rows[:, j, :])
-        load_gate(*CHUNKS[1])
         for q in range(4):
             nc.sync.dma_start(ws_sb[32 * q:32 * q + 4, :, :].bitcast(I32), scale_rows[4 * q:4 * q + 4, :, :])
+        load_gate(*CHUNKS[1])
         nc.sync.dma_start(w_sb.bitcast(I32), word_rows)
         nc.sync.dma_start(bias, b.rearrange("(r p) e -> p r e", p=P))
         load_gate(CHUNKS[2][0], n2 + n3)
@@ -106,8 +106,8 @@ def tile_moe_pre_lin_relu_kernel(tc, xT, w_words, w_scales, b, gate, offs, pos1,
 
         def gather_times_gate():
             s0, n = CHUNKS[0]
-            for j in range(PACK):
-                nc.vector.tensor_tensor(stages[0][:, j * n:(j + 1) * n], window(j, s0, n), gates(s0, n), MULT)
+            for j, at, count in [(j, 0, n) for j in range(PACK - 1)] + [(PACK - 1, 0, 2 * C), (PACK - 1, 2 * C, n - 2 * C)]:
+                nc.vector.tensor_tensor(stages[0][:, j * n + at:j * n + at + count], window(j, at, count), gates(at, count), MULT)
 
         def gather(c, which):
             s0, n = CHUNKS[c]
@@ -116,7 +116,7 @@ def tile_moe_pre_lin_relu_kernel(tc, xT, w_words, w_scales, b, gate, offs, pos1,
 
         def woven(s0, n):
             if s0 >= 6 * C:
-                s0 = s0 % C + (2, 3, 0)[s0 // C - 6] * C
+                s0 = s0 % C + (0, 1, 2)[s0 // C - 6] * C
             return x_bf[:, PACK * s0:PACK * (s0 + n)]
 
         def weave(c, s0, n):
@@ -151,9 +151,14 @@ def tile_moe_pre_lin_relu_kernel(tc, xT, w_words, w_scales, b, gate, offs, pos1,
             else:
                 nc.scalar.activation(ys[r][:, s0:s0 + n], banks[bank][:, at:at + n], RELU, bias=bias[:, r, e:e + 1])
 
-        def expert(bank, r, e):
-            multiply(bank, 0, r, e * C, C)
-            relu(bank, 0, r, e * C, C)
+        def products(bank, *units):
+            for i, (r, e) in enumerate(units):
+                multiply(bank, i * C, r, e * C, C)
+
+        def pair(bank, *units):
+            products(bank, *units)
+            for i, (r, e) in enumerate(units):
+                relu(bank, i * C, r, e * C, C)
 
         def fetch(r, l, t0, n, on_scalar=False):
             found = ys[r][:].indirect(pos_sb[l][:, t0 // 16:(t0 + n) // 16])
@@ -170,34 +175,34 @@ def tile_moe_pre_lin_relu_kernel(tc, xT, w_words, w_scales, b, gate, offs, pos1,
         gather_times_gate()
         gather(1, range(PACK))
         gather(2, range(1, PACK))
-        weave(0, *CHUNKS[0])
+        weave(0, 0, 2 * C)
+        weave(0, 2 * C, n0 - 2 * C)
         gather(3, range(PACK))
+        quantize(0, 2 * C)
         weave(1, *CHUNKS[1])
-        for e in (0, 2, 4):
+        weave(2, 6 * C, C)
+        for e in (2, 4):
             quantize(e * C, 2 * C)
-        early = [(r, e) for first in (0, 2, 4) for r in range(ROW_TILES) for e in (first, first + 1)][:-1]
-        for i, (r, e) in enumerate(early):
-            expert(i % 8, r, e)
-        weave(2, *CHUNKS[2])
+        for bank, (r, e) in enumerate([(r, e) for e in (0, 2, 4) for r in range(ROW_TILES)][:-1]):
+            pair(bank, (r, e), (r, e + 1))
+        weave(2, 7 * C, C)
+        quantize(6 * C, C)
+        products(0, (0, 6), (2, 5))
+        pair(1, (1, 6), (2, 6))
         weave(3, *CHUNKS[3])
-        quantize(6 * C, 2 * C)
-        multiply(1, 0, 0, 6 * C, C)
-        multiply(2, C, 2, 5 * C, C)
-        multiply(2, 0, 0, 7 * C, C)
+        quantize(7 * C, C)
+        products(2, (2, 4), (0, 7))
         for h in range(2):
             quantize(8 * C + h * P, P)
             multiply(3, h * P, 0, 8 * C + h * P, P)
-        for h in range(3):
-            relu(1 + h, 0, 0, (6 + h) * C, C, on_vector=True)
-        relu(2, C, 2, 5 * C, C, on_vector=True)
+        for bank, at, r, e in ((0, 0, 0, 6), (2, C, 0, 7), (3, 0, 0, 8), (0, C, 2, 5), (2, 0, 2, 4)):
+            relu(bank, at, r, e * C, C, on_vector=True)
 
         fetch(0, 0, 0, HALF)
         fetch(0, 0, HALF, HALF, on_scalar=True)
-        for bank, e in ((1, 6), (4, 8), (2, 7)):
-            expert(bank, 1, e)
+        pair(4, (1, 8), (1, 7))
         fetch(1, 0, 0, T, on_scalar=True)
-        for bank, e in ((5, 8), (3, 6), (1, 7)):
-            expert(bank, 2, e)
+        pair(5, (2, 8), (2, 7))
         fetch(2, 0, 0, HALF, on_scalar=True)
         fetch(1, 1, 0, T, on_scalar=True)
         fetch(2, 1, 0, HALF, on_scalar=True)

@@ -1,6 +1,7 @@
 from contextlib import ExitStack
 
 import concourse.mybir as mybir
+from concourse.masks import make_identity
 
 K, T, E, C, N = 512, 768, 9, 256, 384
 S = E * C
@@ -26,12 +27,15 @@ PACK = 4
 BANK = 512
 ROW_TILES = N // P
 HALF = T // 2
-STRETCH = 60 * 1024
+ALIGN = 64
 WIDTH = {F32: 4, U32: 4, BF16: 2, U8: 1}
 
-CHUNKS = [(0, 640), (640, 896), (1536, 512), (2048, 256)]
-WINDOW = 928
-OVERLAP = 32
+CH_A = (0, 384)
+CH_B = (384, 384)
+CH_C1 = (768, 512)
+CH_D = (1280, 256)
+CH_C2 = (1536, 512)
+CH_E = (2048, 256)
 LAST_PIECES = [(384, 256), (640, 128)]
 
 
@@ -45,120 +49,135 @@ def tile_moe_pre_lin_relu_kernel(tc, xT, w_words, w_scales, b, gate, offs, pos1,
         offs_sb = keep.tile([P, S // 16], U16, name="offs_sb")
         pos_sb = [keep.tile([P, T // 16], U16, name="pos_sb%d" % l) for l in range(3)]
 
-        free = [q * STRETCH for q in range(4)]
+        free = [0]
 
-        def tile(q, columns, dtype, name):
-            at = free[q]
-            free[q] = at + -(-columns * WIDTH[dtype] // 256) * 256
-            return data.tile([P, columns], dtype, name=name, align_bytes=256, offset=at)
+        def tile(columns, dtype, name, at=None):
+            if at is None:
+                at = free[0]
+            free[0] = max(free[0], at + -(-columns * WIDTH[dtype] // ALIGN) * ALIGN)
+            return data.tile([P, columns], dtype, name=name, align_bytes=ALIGN, offset=at)
 
-        planes = [tile(j, WINDOW, F32, "plane%d" % j) for j in range(PACK)]
-        n0, n1, n2, n3 = [n for s0, n in CHUNKS]
-        stages = [tile(c, PACK * n, F32, "stage%d" % c)[:] for c, n in enumerate((n0, n1, n2))]
-        stages.append(stages[0][:, 0:PACK * n3])
-        gate_at = 2 * n2 - OVERLAP
-        gate_sb = [stages[2][:, gate_at:gate_at + n0], tile(2, n1, F32, "gate1"), tile(3, n2 + n3, F32, "gate2")]
+        planes = [tile(T, F32, "plane%d" % j) for j in range(PACK)]
+        stage = {}
+        stage[CH_C1] = tile(PACK * CH_C1[1], F32, "stage_c1")
+        gate_a = tile(CH_A[1], F32, "gate_a", at=free[0] - 2 * CH_A[1])
+        stage[CH_C2] = tile(PACK * CH_C2[1], F32, "stage_c2", at=free[0] - 2 * CH_A[1])
+        at_a = free[0]
+        stage[CH_A] = tile(PACK * CH_A[1], F32, "stage_a")
+        stage[CH_E] = tile(PACK * CH_E[1], F32, "stage_e", at=at_a)
+        stage[CH_B] = tile(PACK * CH_B[1], F32, "stage_b")
+        stage[CH_D] = tile(PACK * CH_D[1], F32, "stage_d")
+        gate_b = tile(CH_B[1], F32, "gate_b")
+        gate_de = tile(2 * C, F32, "gate_de")
+        gate_cols = tile(2 * PACK, F32, "gate_cols")
+        identity = tile(P, F32, "identity")
 
-        def gates(s0, n):
-            c = max(i for i, (first, count) in enumerate(CHUNKS[:3]) if first <= s0)
-            return gate_sb[c][:, s0 - CHUNKS[c][0]:s0 + n - CHUNKS[c][0]]
-
-        x_bf = tile(3, 6 * C * PACK, BF16, "x_bf")
-        ys = [tile(r, S, F32, "y%d" % r) for r in range(ROW_TILES)]
-        w_sb = tile(2, E * 2 * N, U8, "w_sb")[:].rearrange("p (e n) -> p e n", e=E)
-        ws_sb = tile(1, E * N, U8, "ws_sb")[:].rearrange("p (e n) -> p e n", e=E)
-        x_codes = tile(2, S, U32, "x_codes")
-        x_scales = tile(1, S, U8, "x_scales")
-        bias = tile(3, ROW_TILES * E, F32, "bias")[:].rearrange("p (r e) -> p r e", e=E)
-        sums = [[tile(3, T, F32, "sum%d_%d" % (r, l)) for l in range(3)] for r in range(ROW_TILES)]
-        extra = [None] + [tile(3, T, F32, "extra%d" % r) for r in (1, 2)]
+        x_bf = tile(3 * C * PACK, BF16, "x_bf")
+        ys = [tile(S, F32, "y%d" % r) for r in range(ROW_TILES)]
+        w_sb = tile(E * 2 * N, U8, "w_sb")[:].rearrange("p (e n) -> p e n", e=E)
+        ws_sb = tile(E * N, U8, "ws_sb")[:].rearrange("p (e n) -> p e n", e=E)
+        x_codes = tile(S, U32, "x_codes")
+        x_scales = tile(S, U8, "x_scales")
+        bias = tile(ROW_TILES * E, F32, "bias")[:].rearrange("p (r e) -> p r e", e=E)
+        sums = [[tile(T, F32, "sum%d_%d" % (r, l)) for l in range(3)] for r in range(ROW_TILES)]
+        extra = [None] + [tile(T, F32, "extra%d" % r) for r in (1, 2)]
         banks = [psum.tile([P, BANK], F32, name="bank%d" % i) for i in range(8)]
 
-        spare = tile(3, 2, F32, "spare")
+        spare = tile(2, F32, "spare")
         nc.gpsimd.memset(spare[:, 0:1], 0.0)
         nc.scalar.activation(spare[:, 1:2], spare[:, 0:1], RELU)
 
         nc.gpsimd.memset(ws_sb.rearrange("p e n -> p (e n)").bitcast(I32), 0)
+        make_identity(nc, identity[:])
 
         x_rows = xT.rearrange("(p j) t -> p j t", j=PACK)
         scale_rows = w_scales.rearrange("e a q n -> q (e a) n").bitcast(I32)
         word_rows = w_words.rearrange("e a p n -> p (e a) n").bitcast(I32)
 
-        def load_gate(s0, n):
-            nc.sync.dma_start(gates(s0, n), gate[0:P, s0:s0 + n])
-
-        nc.sync.dma_start(planes[0][:, 0:T], x_rows[:, 0, :])
+        nc.sync.dma_start(planes[0][:], x_rows[:, 0, :])
         nc.sync.dma_start(offs_sb[:], offs)
-        load_gate(*CHUNKS[0])
+        nc.sync.dma_start(gate_a[:], gate[0:P, 0:CH_A[1]])
         for j in range(1, PACK):
-            nc.sync.dma_start(planes[j][:, 0:T], x_rows[:, j, :])
+            nc.sync.dma_start(planes[j][:], x_rows[:, j, :])
+        nc.sync.dma_start(gate_b[:], gate[0:P, CH_B[0]:CH_C1[0]])
+        nc.sync.dma_start(
+            gate_cols[:].rearrange("p (g i) -> p g i", i=PACK),
+            gate[0, CH_C1[0]:S].rearrange("(g s) -> g s", g=2)[:, 0:2 * C].rearrange("g (p i) -> p g i", i=PACK),
+        )
         for q in range(4):
             nc.sync.dma_start(ws_sb[32 * q:32 * q + 4, :, :].bitcast(I32), scale_rows[4 * q:4 * q + 4, :, :])
-        load_gate(*CHUNKS[1])
+        nc.sync.dma_start(
+            gate_de[:].rearrange("p (g s) -> p g s", g=2),
+            gate[0:P, CH_C1[0]:S].rearrange("p (g s) -> p g s", g=2)[:, :, 2 * C:3 * C],
+        )
         nc.sync.dma_start(w_sb.bitcast(I32), word_rows)
         nc.sync.dma_start(bias, b.rearrange("(r p) e -> p r e", p=P))
-        load_gate(CHUNKS[2][0], n2 + n3)
         for l, pos in enumerate((pos1, pos2, pos3)):
             nc.sync.dma_start(pos_sb[l][:], pos)
 
-        def window(j, s0, n):
-            return planes[j][:].indirect(offs_sb[:, s0 // 16:(s0 + n) // 16])
+        for g in range(2):
+            for i in range(PACK):
+                nc.tensor.transpose(banks[g][:, i * P:(i + 1) * P], gate_cols[:, PACK * g + i:PACK * g + i + 1].to_broadcast([P, P]), identity[:])
 
-        def gather_times_gate():
-            s0, n = CHUNKS[0]
-            for j, at, count in [(j, 0, n) for j in range(PACK - 1)] + [(PACK - 1, 0, 2 * C), (PACK - 1, 2 * C, n - 2 * C)]:
-                nc.vector.tensor_tensor(stages[0][:, j * n + at:j * n + at + count], window(j, at, count), gates(at, count), MULT)
-
-        def gather(c, which):
-            s0, n = CHUNKS[c]
-            for j in which:
-                nc.scalar.activation(stages[c][:, j * n:(j + 1) * n], window(j, s0, n), COPY)
-
-        def woven(s0, n):
-            if s0 >= 6 * C:
-                s0 = s0 % C + (0, 1, 2)[s0 // C - 6] * C
-            return x_bf[:, PACK * s0:PACK * (s0 + n)]
-
-        def weave(c, s0, n):
-            at = s0 - CHUNKS[c][0]
-            staged = stages[c].rearrange("p (t s) -> p t s", t=PACK)[:, :, at:at + n].rearrange("p t (c i) -> p c t i", i=4)
-            to = woven(s0, n).rearrange("p (c i t) -> p c t i", i=4, t=PACK)
-            if c == 0:
-                nc.vector.tensor_copy(to, staged)
+        def gather(chunk, j, how):
+            s0, n = chunk
+            found = planes[j][:].indirect(offs_sb[:, s0 // 16:(s0 + n) // 16])
+            to = stage[chunk][:, j * n:(j + 1) * n]
+            if how == "scalar":
+                nc.scalar.activation(to, found, COPY)
+            elif how == "vector":
+                nc.vector.tensor_copy(to, found)
             else:
-                weights = gates(s0, n).rearrange("p (c i) -> p c i", i=4).unsqueeze(2).to_broadcast([P, n // 4, PACK, 4])
-                nc.vector.tensor_tensor(to, staged, weights, MULT)
+                nc.vector.tensor_tensor(to, found, gate_a[:], MULT)
 
-        def quantize(s0, n):
-            nc.vector.quantize_mx(out=x_codes[:, s0:s0 + n].bitcast(FP8X4), scales=x_scales[:, s0:s0 + n], in_=woven(s0, n))
+        def woven(place, n):
+            return x_bf[:, PACK * place:PACK * (place + n)]
 
-        def multiply(bank, at, r, s0, n):
-            e = s0 // C
+        def weave_plain(chunk, place):
+            staged = stage[chunk][:].rearrange("p (t s) -> p s t", t=PACK)
+            nc.gpsimd.tensor_scalar(woven(place, chunk[1]).rearrange("p (s t) -> p s t", t=PACK), staged, 1.0, 0.0, MULT, ADD)
+
+        def weave_whole(chunk, weights, place):
+            n = chunk[1]
+            staged = stage[chunk][:].rearrange("p (t s) -> p s t", t=PACK)
+            nc.gpsimd.tensor_tensor(
+                woven(place, n).rearrange("p (s t) -> p s t", t=PACK), staged, weights.unsqueeze(2).to_broadcast([P, n, PACK]), MULT
+            )
+
+        def weave_vector(chunk, bank, place):
+            staged = stage[chunk][:].rearrange("p (t c i) -> p c t i", t=PACK, i=PACK)
+            to = woven(place, chunk[1]).rearrange("p (c i t) -> p c t i", i=PACK, t=PACK)
+            weights = banks[bank][:].rearrange("p (i c) -> p c i", i=PACK).unsqueeze(2).to_broadcast([P, P, PACK, PACK])
+            nc.vector.tensor_tensor(to, staged, weights, MULT)
+
+        def quantize(column, place, n):
+            nc.vector.quantize_mx(out=x_codes[:, column:column + n].bitcast(FP8X4), scales=x_scales[:, column:column + n], in_=woven(place, n))
+
+        def multiply(bank, at, r, e):
             nc.tensor.matmul_mx(
-                out=banks[bank][:, at:at + n],
+                out=banks[bank][:, at:at + C],
                 lhsT=w_sb[:, e, 2 * P * r:2 * P * (r + 1)].bitcast(FP4X4),
                 lhsT_scale=ws_sb[:, e, P * r:P * (r + 1)],
-                rhs=x_codes[:, s0:s0 + n].bitcast(FP8X4),
-                rhs_scale=x_scales[:, s0:s0 + n],
+                rhs=x_codes[:, e * C:(e + 1) * C].bitcast(FP8X4),
+                rhs_scale=x_scales[:, e * C:(e + 1) * C],
                 start=True,
                 stop=True,
             )
 
-        def relu(bank, at, r, s0, n, on_vector=False):
-            e = s0 // C
+        def relu(bank, at, r, e, on_vector=False):
+            to = ys[r][:, e * C:(e + 1) * C]
             if on_vector:
-                nc.vector.tensor_scalar(ys[r][:, s0:s0 + n], banks[bank][:, at:at + n], bias[:, r, e:e + 1], 0.0, ADD, MAX)
+                nc.vector.tensor_scalar(to, banks[bank][:, at:at + C], bias[:, r, e:e + 1], 0.0, ADD, MAX)
             else:
-                nc.scalar.activation(ys[r][:, s0:s0 + n], banks[bank][:, at:at + n], RELU, bias=bias[:, r, e:e + 1])
+                nc.scalar.activation(to, banks[bank][:, at:at + C], RELU, bias=bias[:, r, e:e + 1])
 
         def products(bank, *units):
             for i, (r, e) in enumerate(units):
-                multiply(bank, i * C, r, e * C, C)
+                multiply(bank, i * C, r, e)
 
-        def pair(bank, *units):
-            products(bank, *units)
+        def relus(bank, *units, on_vector=False):
             for i, (r, e) in enumerate(units):
-                relu(bank, i * C, r, e * C, C)
+                relu(bank, i * C, r, e, on_vector)
 
         def fetch(r, l, t0, n, on_scalar=False):
             found = ys[r][:].indirect(pos_sb[l][:, t0 // 16:(t0 + n) // 16])
@@ -171,38 +190,64 @@ def tile_moe_pre_lin_relu_kernel(tc, xT, w_words, w_scales, b, gate, offs, pos1,
             if l == 2:
                 nc.sync.dma_start(out[r * P:(r + 1) * P, t0:t0 + n], sums[r][l][:, t0:t0 + n])
 
-        nc.vector.tensor_copy(stages[2][:, 0:n2], window(0, *CHUNKS[2]))
-        gather_times_gate()
-        gather(1, range(PACK))
-        gather(2, range(1, PACK))
-        weave(0, 0, 2 * C)
-        weave(0, 2 * C, n0 - 2 * C)
-        gather(3, range(PACK))
-        quantize(0, 2 * C)
-        weave(1, *CHUNKS[1])
-        weave(2, 6 * C, C)
-        for e in (2, 4):
-            quantize(e * C, 2 * C)
-        for bank, (r, e) in enumerate([(r, e) for e in (0, 2, 4) for r in range(ROW_TILES)][:-1]):
-            pair(bank, (r, e), (r, e + 1))
-        weave(2, 7 * C, C)
-        quantize(6 * C, C)
-        products(0, (0, 6), (2, 5))
-        pair(1, (1, 6), (2, 6))
-        weave(3, *CHUNKS[3])
-        quantize(7 * C, C)
-        products(2, (2, 4), (0, 7))
-        for h in range(2):
-            quantize(8 * C + h * P, P)
-            multiply(3, h * P, 0, 8 * C + h * P, P)
-        for bank, at, r, e in ((0, 0, 0, 6), (2, C, 0, 7), (3, 0, 0, 8), (0, C, 2, 5), (2, 0, 2, 4)):
-            relu(bank, at, r, e * C, C, on_vector=True)
+        gather(CH_D, 0, "vector")
+        for j in range(PACK):
+            gather(CH_A, j, "times gate")
+            gather(CH_B, j, "scalar")
+            if j in (1, 2):
+                gather(CH_D, j, "scalar")
+        gather(CH_D, 3, "vector")
+        weave_plain(CH_A, 0)
+        weave_whole(CH_B, gate_b[:], CH_A[1])
+        for j in range(PACK):
+            gather(CH_C1, j, "vector")
+        for chunk in (CH_C2, CH_E):
+            for j in range(PACK):
+                gather(chunk, j, "scalar")
+
+        quantize(0, 0, 2 * C)
+        quantize(2 * C, 2 * C, C)
+        weave_whole(CH_D, gate_de[:, 0:C], 2 * C)
+        weave_vector(CH_C1, 0, 0)
+        first = [(2, (0, 0), (0, 1)), (3, (1, 0), (1, 1)), (4, (2, 0), (2, 1)), (5, (0, 2), (1, 2))]
+        for bank, *units in first:
+            products(bank, *units)
+        products(6, (2, 2))
+        relus(6, (2, 2), on_vector=True)
+        for bank, *units in first:
+            relus(bank, *units)
+
+        quantize(3 * C, 0, C)
+        quantize(4 * C, C, 2 * C)
+        weave_whole(CH_E, gate_de[:, C:2 * C], 2 * C)
+        weave_vector(CH_C2, 1, 0)
+        second = [(7, (0, 3), (1, 3)), (0, (0, 4), (0, 5)), (2, (1, 4), (1, 5)), (3, (2, 4), (2, 5))]
+        products(6, (2, 3))
+        for bank, *units in second:
+            products(bank, *units)
+        relus(6, (2, 3), on_vector=True)
+        for bank, *units in second:
+            relus(bank, *units)
+
+        quantize(6 * C, 0, 2 * C)
+        quantize(8 * C, 2 * C, C)
+        products(1, (0, 6))
+        products(4, (0, 7))
+        products(5, (0, 8))
+        products(6, (1, 6), (1, 7))
+        relus(1, (0, 6))
+        relus(4, (0, 7), on_vector=True)
+        relus(5, (0, 8))
+        relus(6, (1, 6), (1, 7), on_vector=True)
 
         fetch(0, 0, 0, HALF)
         fetch(0, 0, HALF, HALF, on_scalar=True)
-        pair(4, (1, 8), (1, 7))
+        products(7, (1, 8), (2, 8))
+        products(0, (2, 6), (2, 7))
+        relu(7, 0, 1, 8)
         fetch(1, 0, 0, T, on_scalar=True)
-        pair(5, (2, 8), (2, 7))
+        relu(7, C, 2, 8)
+        relus(0, (2, 6), (2, 7))
         fetch(2, 0, 0, HALF, on_scalar=True)
         fetch(1, 1, 0, T, on_scalar=True)
         fetch(2, 1, 0, HALF, on_scalar=True)

@@ -33,9 +33,9 @@ WIDTH = {F32: 4, U32: 4, BF16: 2, U8: 1}
 CH_A = (0, 384)
 CH_B = (384, 384)
 CH_C1 = (768, 512)
-CH_D = (1280, 256)
-CH_C2 = (1536, 512)
-CH_E = (2048, 256)
+CH_C2 = (1280, 512)
+CH_C3 = (1792, 256)
+CH_D = (2048, 256)
 LAST_PIECES = [(384, 256), (640, 128)]
 
 
@@ -64,15 +64,16 @@ def tile_moe_pre_lin_relu_kernel(tc, xT, w_words, w_scales, b, gate, offs, pos1,
         stage[CH_C2] = tile(PACK * CH_C2[1], F32, "stage_c2", at=free[0] - 2 * CH_A[1])
         at_a = free[0]
         stage[CH_A] = tile(PACK * CH_A[1], F32, "stage_a")
-        stage[CH_E] = tile(PACK * CH_E[1], F32, "stage_e", at=at_a)
+        stage[CH_C3] = tile(PACK * CH_C3[1], F32, "stage_c3", at=at_a)
         stage[CH_B] = tile(PACK * CH_B[1], F32, "stage_b")
         stage[CH_D] = tile(PACK * CH_D[1], F32, "stage_d")
         gate_b = tile(CH_B[1], F32, "gate_b")
-        gate_de = tile(2 * C, F32, "gate_de")
+        gate_d = tile(C, F32, "gate_d")
         gate_cols = tile(2 * PACK, F32, "gate_cols")
+        gate_pairs = tile(2, F32, "gate_pairs")
         identity = tile(P, F32, "identity")
 
-        x_bf = tile(3 * C * PACK, BF16, "x_bf")
+        x_bf = tile(5 * C * PACK, BF16, "x_bf")
         ys = [tile(S, F32, "y%d" % r) for r in range(ROW_TILES)]
         w_sb = tile(E * 2 * N, U8, "w_sb")[:].rearrange("p (e n) -> p e n", e=E)
         ws_sb = tile(E * N, U8, "ws_sb")[:].rearrange("p (e n) -> p e n", e=E)
@@ -80,7 +81,7 @@ def tile_moe_pre_lin_relu_kernel(tc, xT, w_words, w_scales, b, gate, offs, pos1,
         x_scales = tile(S, U8, "x_scales")
         bias = tile(ROW_TILES * E, F32, "bias")[:].rearrange("p (r e) -> p r e", e=E)
         sums = [[tile(T, F32, "sum%d_%d" % (r, l)) for l in range(3)] for r in range(ROW_TILES)]
-        extra = [None] + [tile(T, F32, "extra%d" % r) for r in (1, 2)]
+        extra = [None, tile(HALF, F32, "extra1"), tile(T, F32, "extra2")]
         banks = [psum.tile([P, BANK], F32, name="bank%d" % i) for i in range(8)]
 
         spare = tile(2, F32, "spare")
@@ -102,14 +103,12 @@ def tile_moe_pre_lin_relu_kernel(tc, xT, w_words, w_scales, b, gate, offs, pos1,
         nc.sync.dma_start(gate_b[:], gate[0:P, CH_B[0]:CH_C1[0]])
         nc.sync.dma_start(
             gate_cols[:].rearrange("p (g i) -> p g i", i=PACK),
-            gate[0, CH_C1[0]:S].rearrange("(g s) -> g s", g=2)[:, 0:2 * C].rearrange("g (p i) -> p g i", i=PACK),
+            gate[0, CH_C1[0]:CH_C3[0]].rearrange("(g p i) -> p g i", p=P, i=PACK),
         )
+        nc.sync.dma_start(gate_pairs[:], gate[0, CH_C3[0]:CH_D[0]].rearrange("(p i) -> p i", i=2))
         for q in range(4):
             nc.sync.dma_start(ws_sb[32 * q:32 * q + 4, :, :].bitcast(I32), scale_rows[4 * q:4 * q + 4, :, :])
-        nc.sync.dma_start(
-            gate_de[:].rearrange("p (g s) -> p g s", g=2),
-            gate[0:P, CH_C1[0]:S].rearrange("p (g s) -> p g s", g=2)[:, :, 2 * C:3 * C],
-        )
+        nc.sync.dma_start(gate_d[:], gate[0:P, CH_D[0]:S])
         nc.sync.dma_start(w_sb.bitcast(I32), word_rows)
         nc.sync.dma_start(bias, b.rearrange("(r p) e -> p r e", p=P))
         for l, pos in enumerate((pos1, pos2, pos3)):
@@ -118,6 +117,8 @@ def tile_moe_pre_lin_relu_kernel(tc, xT, w_words, w_scales, b, gate, offs, pos1,
         for g in range(2):
             for i in range(PACK):
                 nc.tensor.transpose(banks[g][:, i * P:(i + 1) * P], gate_cols[:, PACK * g + i:PACK * g + i + 1].to_broadcast([P, P]), identity[:])
+        for i in range(2):
+            nc.tensor.transpose(banks[2][:, i * P:(i + 1) * P], gate_pairs[:, i:i + 1].to_broadcast([P, P]), identity[:])
 
         def gather(chunk, j, how):
             s0, n = chunk
@@ -145,21 +146,23 @@ def tile_moe_pre_lin_relu_kernel(tc, xT, w_words, w_scales, b, gate, offs, pos1,
             )
 
         def weave_vector(chunk, bank, place):
-            staged = stage[chunk][:].rearrange("p (t c i) -> p c t i", t=PACK, i=PACK)
-            to = woven(place, chunk[1]).rearrange("p (c i t) -> p c t i", i=PACK, t=PACK)
-            weights = banks[bank][:].rearrange("p (i c) -> p c i", i=PACK).unsqueeze(2).to_broadcast([P, P, PACK, PACK])
+            run = chunk[1] // P
+            staged = stage[chunk][:].rearrange("p (t c i) -> p c t i", t=PACK, i=run)
+            to = woven(place, chunk[1]).rearrange("p (c i t) -> p c t i", i=run, t=PACK)
+            weights = banks[bank][:, 0:chunk[1]].rearrange("p (i c) -> p c i", i=run).unsqueeze(2).to_broadcast([P, P, PACK, run])
             nc.vector.tensor_tensor(to, staged, weights, MULT)
 
         def quantize(column, place, n):
             nc.vector.quantize_mx(out=x_codes[:, column:column + n].bitcast(FP8X4), scales=x_scales[:, column:column + n], in_=woven(place, n))
 
         def multiply(bank, at, r, e):
+            column = (2, 3, 4, 0, 1, 5, 6, 7, 8)[e] * C
             nc.tensor.matmul_mx(
                 out=banks[bank][:, at:at + C],
                 lhsT=w_sb[:, e, 2 * P * r:2 * P * (r + 1)].bitcast(FP4X4),
                 lhsT_scale=ws_sb[:, e, P * r:P * (r + 1)],
-                rhs=x_codes[:, e * C:(e + 1) * C].bitcast(FP8X4),
-                rhs_scale=x_scales[:, e * C:(e + 1) * C],
+                rhs=x_codes[:, column:column + C].bitcast(FP8X4),
+                rhs_scale=x_scales[:, column:column + C],
                 start=True,
                 stop=True,
             )
@@ -197,62 +200,50 @@ def tile_moe_pre_lin_relu_kernel(tc, xT, w_words, w_scales, b, gate, offs, pos1,
             if j in (1, 2):
                 gather(CH_D, j, "scalar")
         gather(CH_D, 3, "vector")
-        weave_plain(CH_A, 0)
-        weave_whole(CH_B, gate_b[:], CH_A[1])
-        for j in range(PACK):
-            gather(CH_C1, j, "vector")
-        for chunk in (CH_C2, CH_E):
-            for j in range(PACK):
+        weave_plain(CH_A, 2 * C)
+        weave_whole(CH_B, gate_b[:], 2 * C + CH_A[1])
+        for chunk, j in ((CH_C1, 0), (CH_C1, 1), (CH_C2, 0)):
+            gather(chunk, j, "vector")
+        for chunk, first_plane in ((CH_C1, 2), (CH_C2, 1), (CH_C3, 0)):
+            for j in range(first_plane, PACK):
                 gather(chunk, j, "scalar")
-
-        quantize(0, 0, 2 * C)
-        quantize(2 * C, 2 * C, C)
-        weave_whole(CH_D, gate_de[:, 0:C], 2 * C)
         weave_vector(CH_C1, 0, 0)
-        first = [(2, (0, 0), (0, 1)), (3, (1, 0), (1, 1)), (4, (2, 0), (2, 1)), (5, (0, 2), (1, 2))]
-        for bank, *units in first:
+
+        def pair(bank, *units):
             products(bank, *units)
-        products(6, (2, 2))
-        relus(6, (2, 2), on_vector=True)
-        for bank, *units in first:
             relus(bank, *units)
 
-        quantize(3 * C, 0, C)
-        quantize(4 * C, C, 2 * C)
-        weave_whole(CH_E, gate_de[:, C:2 * C], 2 * C)
-        weave_vector(CH_C2, 1, 0)
-        second = [(7, (0, 3), (1, 3)), (0, (0, 4), (0, 5)), (2, (1, 4), (1, 5)), (3, (2, 4), (2, 5))]
-        products(6, (2, 3))
-        for bank, *units in second:
-            products(bank, *units)
-        relus(6, (2, 3), on_vector=True)
-        for bank, *units in second:
-            relus(bank, *units)
+        quantize(0, 0, 4 * C)
+        quantize(4 * C, 4 * C, C)
+        weave_whole(CH_D, gate_d[:], 4 * C)
+        weave_vector(CH_C2, 1, C)
+        weave_vector(CH_C3, 2, 3 * C)
+        pair(3, (0, 3), (0, 4))
+        pair(4, (0, 0), (0, 1))
+        pair(5, (1, 3), (1, 4))
+        pair(6, (0, 2), (1, 2))
+        pair(7, (1, 0), (1, 1))
+        pair(0, (2, 0), (2, 1))
+        pair(3, (2, 2), (2, 3))
 
-        quantize(6 * C, 0, 2 * C)
-        quantize(8 * C, 2 * C, C)
-        products(1, (0, 6))
-        products(4, (0, 7))
-        products(5, (0, 8))
-        products(6, (1, 6), (1, 7))
-        relus(1, (0, 6))
-        relus(4, (0, 7), on_vector=True)
-        relus(5, (0, 8))
-        relus(6, (1, 6), (1, 7), on_vector=True)
+        quantize(5 * C, C, 2 * C)
+        quantize(7 * C, 3 * C, C)
+        quantize(8 * C, 4 * C, C)
+        pair(1, (0, 5), (0, 6))
+        products(2, (0, 7), (1, 7))
+        products(4, (0, 8), (1, 8))
+        relus(2, (0, 7), (1, 7), on_vector=True)
+        relus(4, (0, 8), (1, 8), on_vector=True)
 
         fetch(0, 0, 0, HALF)
         fetch(0, 0, HALF, HALF, on_scalar=True)
-        products(7, (1, 8), (2, 8))
-        products(0, (2, 6), (2, 7))
-        relu(7, 0, 1, 8)
+        pair(2, (1, 5), (1, 6))
+        pair(4, (2, 4), (2, 5))
+        pair(2, (2, 6), (2, 7))
+        pair(4, (2, 8))
         fetch(1, 0, 0, T, on_scalar=True)
-        relu(7, C, 2, 8)
-        relus(0, (2, 6), (2, 7))
-        fetch(2, 0, 0, HALF, on_scalar=True)
-        fetch(1, 1, 0, T, on_scalar=True)
-        fetch(2, 1, 0, HALF, on_scalar=True)
-        for l in range(2):
-            fetch(2, l, HALF, HALF, on_scalar=True)
+        for r, l, h in ((2, 0, 0), (1, 1, 0), (2, 1, 0), (2, 0, 1), (2, 1, 1)):
+            fetch(r, l, h * HALF, HALF, on_scalar=True)
 
         def third(r, t0, n):
             nc.vector.tensor_tensor(extra[r][:, t0:t0 + n], ys[r][:].indirect(pos_sb[2][:, t0 // 16:(t0 + n) // 16]), sums[r][0][:, t0:t0 + n], ADD)
@@ -264,9 +255,11 @@ def tile_moe_pre_lin_relu_kernel(tc, xT, w_words, w_scales, b, gate, offs, pos1,
         for l in (1, 2):
             for h in (1, 0):
                 fetch(0, l, h * HALF, HALF)
-        third(1, 0, T)
+        fetch(1, 1, HALF, HALF)
+        third(1, 0, HALF)
+        fetch(1, 2, HALF, HALF)
         third(2, 0, HALF)
-        finish(1, 0, T)
+        finish(1, 0, HALF)
         finish(2, 0, HALF)
         for t0, n in LAST_PIECES:
             third(2, t0, n)

@@ -32,10 +32,12 @@ WIDTH = {F32: 4, U32: 4, BF16: 2, U8: 1}
 
 CH_A = (0, 384)
 CH_B = (384, 384)
-CH_C1 = (768, 512)
-CH_C2 = (1280, 512)
-CH_C3 = (1792, 256)
-CH_D = (2048, 256)
+CH_D = (768, 256)
+CH_C1 = (1024, 512)
+CH_C2 = (1536, 512)
+CH_C3 = (2048, 256)
+EXPERT = (0, 1, 2, 4, 5, 6, 7, 8, 3)
+SHARE = 576
 LAST_PIECES = [(384, 256), (640, 128)]
 
 
@@ -67,8 +69,7 @@ def tile_moe_pre_lin_relu_kernel(tc, xT, w_words, w_scales, b, gate, offs, pos1,
         stage[CH_C3] = tile(PACK * CH_C3[1], F32, "stage_c3", at=at_a)
         stage[CH_B] = tile(PACK * CH_B[1], F32, "stage_b")
         stage[CH_D] = tile(PACK * CH_D[1], F32, "stage_d")
-        gate_b = tile(CH_B[1], F32, "gate_b")
-        gate_d = tile(C, F32, "gate_d")
+        gate_bd = tile(CH_B[1] + CH_D[1], F32, "gate_bd")
         gate_cols = tile(2 * PACK, F32, "gate_cols")
         gate_pairs = tile(2, F32, "gate_pairs")
         identity = tile(P, F32, "identity")
@@ -81,7 +82,7 @@ def tile_moe_pre_lin_relu_kernel(tc, xT, w_words, w_scales, b, gate, offs, pos1,
         x_scales = tile(S, U8, "x_scales")
         bias = tile(ROW_TILES * E, F32, "bias")[:].rearrange("p (r e) -> p r e", e=E)
         sums = [[tile(T, F32, "sum%d_%d" % (r, l)) for l in range(3)] for r in range(ROW_TILES)]
-        extra = [None, tile(HALF, F32, "extra1"), tile(T, F32, "extra2")]
+        extra = [None, tile(SHARE, F32, "extra1"), tile(T, F32, "extra2")]
         banks = [psum.tile([P, BANK], F32, name="bank%d" % i) for i in range(8)]
 
         spare = tile(2, F32, "spare")
@@ -100,15 +101,14 @@ def tile_moe_pre_lin_relu_kernel(tc, xT, w_words, w_scales, b, gate, offs, pos1,
         nc.sync.dma_start(gate_a[:], gate[0:P, 0:CH_A[1]])
         for j in range(1, PACK):
             nc.sync.dma_start(planes[j][:], x_rows[:, j, :])
-        nc.sync.dma_start(gate_b[:], gate[0:P, CH_B[0]:CH_C1[0]])
+        nc.sync.dma_start(gate_bd[:], gate[0:P, CH_B[0]:CH_C1[0]])
         nc.sync.dma_start(
             gate_cols[:].rearrange("p (g i) -> p g i", i=PACK),
             gate[0, CH_C1[0]:CH_C3[0]].rearrange("(g p i) -> p g i", p=P, i=PACK),
         )
-        nc.sync.dma_start(gate_pairs[:], gate[0, CH_C3[0]:CH_D[0]].rearrange("(p i) -> p i", i=2))
+        nc.sync.dma_start(gate_pairs[:], gate[0, CH_C3[0]:S].rearrange("(p i) -> p i", i=2))
         for q in range(4):
             nc.sync.dma_start(ws_sb[32 * q:32 * q + 4, :, :].bitcast(I32), scale_rows[4 * q:4 * q + 4, :, :])
-        nc.sync.dma_start(gate_d[:], gate[0:P, CH_D[0]:S])
         nc.sync.dma_start(w_sb.bitcast(I32), word_rows)
         nc.sync.dma_start(bias, b.rearrange("(r p) e -> p r e", p=P))
         for l, pos in enumerate((pos1, pos2, pos3)):
@@ -157,6 +157,7 @@ def tile_moe_pre_lin_relu_kernel(tc, xT, w_words, w_scales, b, gate, offs, pos1,
 
         def multiply(bank, at, r, e):
             column = (2, 3, 4, 0, 1, 5, 6, 7, 8)[e] * C
+            e = EXPERT[e]
             nc.tensor.matmul_mx(
                 out=banks[bank][:, at:at + C],
                 lhsT=w_sb[:, e, 2 * P * r:2 * P * (r + 1)].bitcast(FP4X4),
@@ -168,6 +169,7 @@ def tile_moe_pre_lin_relu_kernel(tc, xT, w_words, w_scales, b, gate, offs, pos1,
             )
 
         def relu(bank, at, r, e, on_vector=False):
+            e = EXPERT[e]
             to = ys[r][:, e * C:(e + 1) * C]
             if on_vector:
                 nc.vector.tensor_scalar(to, banks[bank][:, at:at + C], bias[:, r, e:e + 1], 0.0, ADD, MAX)
@@ -190,8 +192,6 @@ def tile_moe_pre_lin_relu_kernel(tc, xT, w_words, w_scales, b, gate, offs, pos1,
                 nc.vector.tensor_copy(sums[r][l][:, t0:t0 + n], found)
             else:
                 nc.vector.tensor_tensor(sums[r][l][:, t0:t0 + n], found, sums[r][l - 1][:, t0:t0 + n], ADD)
-            if l == 2:
-                nc.sync.dma_start(out[r * P:(r + 1) * P, t0:t0 + n], sums[r][l][:, t0:t0 + n])
 
         gather(CH_D, 0, "vector")
         for j in range(PACK):
@@ -201,10 +201,10 @@ def tile_moe_pre_lin_relu_kernel(tc, xT, w_words, w_scales, b, gate, offs, pos1,
                 gather(CH_D, j, "scalar")
         gather(CH_D, 3, "vector")
         weave_plain(CH_A, 2 * C)
-        weave_whole(CH_B, gate_b[:], 2 * C + CH_A[1])
-        for chunk, j in ((CH_C1, 0), (CH_C1, 1), (CH_C2, 0)):
+        weave_whole(CH_B, gate_bd[:, 0:CH_B[1]], 2 * C + CH_A[1])
+        for chunk, j in ((CH_C1, 0), (CH_C1, 1), (CH_C2, 0), (CH_C3, 0)):
             gather(chunk, j, "vector")
-        for chunk, first_plane in ((CH_C1, 2), (CH_C2, 1), (CH_C3, 0)):
+        for chunk, first_plane in ((CH_C1, 2), (CH_C2, 1), (CH_C3, 1)):
             for j in range(first_plane, PACK):
                 gather(chunk, j, "scalar")
         weave_vector(CH_C1, 0, 0)
@@ -215,7 +215,7 @@ def tile_moe_pre_lin_relu_kernel(tc, xT, w_words, w_scales, b, gate, offs, pos1,
 
         quantize(0, 0, 4 * C)
         quantize(4 * C, 4 * C, C)
-        weave_whole(CH_D, gate_d[:], 4 * C)
+        weave_whole(CH_D, gate_bd[:, CH_B[1]:], 4 * C)
         weave_vector(CH_C2, 1, C)
         weave_vector(CH_C3, 2, 3 * C)
         pair(3, (0, 3), (0, 4))
@@ -225,6 +225,7 @@ def tile_moe_pre_lin_relu_kernel(tc, xT, w_words, w_scales, b, gate, offs, pos1,
         pair(7, (1, 0), (1, 1))
         pair(0, (2, 0), (2, 1))
         pair(3, (2, 2), (2, 3))
+        pair(5, (2, 4))
 
         quantize(5 * C, C, 2 * C)
         quantize(7 * C, 3 * C, C)
@@ -238,28 +239,33 @@ def tile_moe_pre_lin_relu_kernel(tc, xT, w_words, w_scales, b, gate, offs, pos1,
         fetch(0, 0, 0, HALF)
         fetch(0, 0, HALF, HALF, on_scalar=True)
         pair(2, (1, 5), (1, 6))
-        pair(4, (2, 4), (2, 5))
-        pair(2, (2, 6), (2, 7))
-        pair(4, (2, 8))
+        pair(4, (2, 5), (2, 6))
+        pair(2, (2, 7), (2, 8))
         fetch(1, 0, 0, T, on_scalar=True)
-        for r, l, h in ((2, 0, 0), (1, 1, 0), (2, 1, 0), (2, 0, 1), (2, 1, 1)):
-            fetch(r, l, h * HALF, HALF, on_scalar=True)
+        fetch(2, 0, 0, HALF, on_scalar=True)
+        fetch(1, 1, 0, SHARE, on_scalar=True)
+        for l, h in ((1, 0), (0, 1), (1, 1)):
+            fetch(2, l, h * HALF, HALF, on_scalar=True)
 
         def third(r, t0, n):
             nc.vector.tensor_tensor(extra[r][:, t0:t0 + n], ys[r][:].indirect(pos_sb[2][:, t0 // 16:(t0 + n) // 16]), sums[r][0][:, t0:t0 + n], ADD)
 
+        def store(r, t0, n):
+            nc.sync.dma_start(out[r * P:(r + 1) * P, t0:t0 + n], sums[r][2][:, t0:t0 + n])
+
         def finish(r, t0, n):
             nc.vector.tensor_tensor(sums[r][2][:, t0:t0 + n], extra[r][:, t0:t0 + n], sums[r][1][:, t0:t0 + n], ADD)
-            nc.sync.dma_start(out[r * P:(r + 1) * P, t0:t0 + n], sums[r][2][:, t0:t0 + n])
+            store(r, t0, T if r == 1 else n)
 
         for l in (1, 2):
             for h in (1, 0):
                 fetch(0, l, h * HALF, HALF)
-        fetch(1, 1, HALF, HALF)
-        third(1, 0, HALF)
-        fetch(1, 2, HALF, HALF)
+        store(0, 0, T)
+        fetch(1, 1, SHARE, T - SHARE)
+        third(1, 0, SHARE)
+        fetch(1, 2, SHARE, T - SHARE)
         third(2, 0, HALF)
-        finish(1, 0, HALF)
+        finish(1, 0, SHARE)
         finish(2, 0, HALF)
         for t0, n in LAST_PIECES:
             third(2, t0, n)

@@ -32,12 +32,14 @@ WIDTH = {F32: 4, U32: 4, BF16: 2, U8: 1}
 
 CH_A = (0, 384)
 CH_B = (384, 384)
-CH_D = (768, 256)
+CH_C3 = (768, 256)
 CH_C1 = (1024, 512)
 CH_C2 = (1536, 512)
-CH_C3 = (2048, 256)
-EXPERT = (0, 1, 2, 4, 5, 6, 7, 8, 3)
-SHARE = 576
+CH_D = (2048, 256)
+EXPERT = (0, 1, 2, 4, 5, 6, 7, 3, 8)
+SHARE = 384
+FIRST = 512
+TAIL = 64
 LAST_PIECES = [(384, 256), (640, 128)]
 
 
@@ -68,17 +70,20 @@ def tile_moe_pre_lin_relu_kernel(tc, xT, w_words, w_scales, b, gate, offs, pos1,
         stage[CH_A] = tile(PACK * CH_A[1], F32, "stage_a")
         stage[CH_C3] = tile(PACK * CH_C3[1], F32, "stage_c3", at=at_a)
         stage[CH_B] = tile(PACK * CH_B[1], F32, "stage_b")
+        at_d = free[0]
         stage[CH_D] = tile(PACK * CH_D[1], F32, "stage_d")
-        gate_bd = tile(CH_B[1] + CH_D[1], F32, "gate_bd")
+        gate_b = tile(CH_B[1] - TAIL, F32, "gate_b")
+        gate_d = tile(CH_D[1], F32, "gate_d")
         gate_cols = tile(2 * PACK, F32, "gate_cols")
-        gate_pairs = tile(2, F32, "gate_pairs")
+        gate_ones = tile(3, F32, "gate_ones")
         identity = tile(P, F32, "identity")
 
         x_bf = tile(5 * C * PACK, BF16, "x_bf")
         ys = [tile(S, F32, "y%d" % r) for r in range(ROW_TILES)]
         w_sb = tile(E * 2 * N, U8, "w_sb")[:].rearrange("p (e n) -> p e n", e=E)
         ws_sb = tile(E * N, U8, "ws_sb")[:].rearrange("p (e n) -> p e n", e=E)
-        x_codes = tile(S, U32, "x_codes")
+        early_codes = tile(5 * C, U32, "early_codes")
+        late_codes = tile(4 * C, U32, "late_codes", at=at_d)
         x_scales = tile(S, U8, "x_scales")
         bias = tile(ROW_TILES * E, F32, "bias")[:].rearrange("p (r e) -> p r e", e=E)
         sums = [[tile(T, F32, "sum%d_%d" % (r, l)) for l in range(3)] for r in range(ROW_TILES)]
@@ -101,14 +106,16 @@ def tile_moe_pre_lin_relu_kernel(tc, xT, w_words, w_scales, b, gate, offs, pos1,
         nc.sync.dma_start(gate_a[:], gate[0:P, 0:CH_A[1]])
         for j in range(1, PACK):
             nc.sync.dma_start(planes[j][:], x_rows[:, j, :])
-        nc.sync.dma_start(gate_bd[:], gate[0:P, CH_B[0]:CH_C1[0]])
+        nc.sync.dma_start(gate_b[:], gate[0:P, CH_B[0]:CH_C3[0] - TAIL])
         nc.sync.dma_start(
             gate_cols[:].rearrange("p (g i) -> p g i", i=PACK),
-            gate[0, CH_C1[0]:CH_C3[0]].rearrange("(g p i) -> p g i", p=P, i=PACK),
+            gate[0, CH_C1[0]:CH_D[0]].rearrange("(g p i) -> p g i", p=P, i=PACK),
         )
-        nc.sync.dma_start(gate_pairs[:], gate[0, CH_C3[0]:S].rearrange("(p i) -> p i", i=2))
+        with nc.allow_non_contiguous_dma(reason="one gate value a partition and group of 128 slots"):
+            nc.sync.dma_start(gate_ones[:], gate[0, CH_C3[0] - P:CH_C1[0]].rearrange("(g p) -> p g", p=P))
         for q in range(4):
             nc.sync.dma_start(ws_sb[32 * q:32 * q + 4, :, :].bitcast(I32), scale_rows[4 * q:4 * q + 4, :, :])
+        nc.sync.dma_start(gate_d[:], gate[0:P, CH_D[0]:S])
         nc.sync.dma_start(w_sb.bitcast(I32), word_rows)
         nc.sync.dma_start(bias, b.rearrange("(r p) e -> p r e", p=P))
         for l, pos in enumerate((pos1, pos2, pos3)):
@@ -116,9 +123,9 @@ def tile_moe_pre_lin_relu_kernel(tc, xT, w_words, w_scales, b, gate, offs, pos1,
 
         for g in range(2):
             for i in range(PACK):
-                nc.tensor.transpose(banks[g][:, i * P:(i + 1) * P], gate_cols[:, PACK * g + i:PACK * g + i + 1].to_broadcast([P, P]), identity[:])
-        for i in range(2):
-            nc.tensor.transpose(banks[2][:, i * P:(i + 1) * P], gate_pairs[:, i:i + 1].to_broadcast([P, P]), identity[:])
+                nc.tensor.transpose(banks[g][:].rearrange("p (c i) -> p i c", i=PACK)[:, i, :], gate_cols[:, PACK * g + i:PACK * g + i + 1].to_broadcast([P, P]), identity[:])
+        for g in range(3):
+            nc.tensor.transpose(banks[2][:, g * P:(g + 1) * P], gate_ones[:, g:g + 1].to_broadcast([P, P]), identity[:])
 
         def gather(chunk, j, how):
             s0, n = chunk
@@ -138,22 +145,25 @@ def tile_moe_pre_lin_relu_kernel(tc, xT, w_words, w_scales, b, gate, offs, pos1,
             staged = stage[chunk][:].rearrange("p (t s) -> p s t", t=PACK)
             nc.gpsimd.tensor_scalar(woven(place, chunk[1]).rearrange("p (s t) -> p s t", t=PACK), staged, 1.0, 0.0, MULT, ADD)
 
-        def weave_whole(chunk, weights, place):
-            n = chunk[1]
-            staged = stage[chunk][:].rearrange("p (t s) -> p s t", t=PACK)
+        def weave_whole(chunk, n, weights, place):
+            staged = stage[chunk][:].rearrange("p (t s) -> p s t", t=PACK)[:, 0:n, :]
             nc.gpsimd.tensor_tensor(
                 woven(place, n).rearrange("p (s t) -> p s t", t=PACK), staged, weights.unsqueeze(2).to_broadcast([P, n, PACK]), MULT
             )
 
-        def weave_vector(chunk, bank, place):
-            run = chunk[1] // P
-            staged = stage[chunk][:].rearrange("p (t c i) -> p c t i", t=PACK, i=run)
-            to = woven(place, chunk[1]).rearrange("p (c i t) -> p c t i", i=run, t=PACK)
-            weights = banks[bank][:, 0:chunk[1]].rearrange("p (i c) -> p c i", i=run).unsqueeze(2).to_broadcast([P, P, PACK, run])
+        def weave_vector(chunk, n, weights, place):
+            staged = stage[chunk][:].rearrange("p (t s) -> p t s", t=PACK)[:, :, chunk[1] - n:].rearrange("p t (c i) -> p c t i", i=PACK)
+            to = woven(place, n).rearrange("p (c i t) -> p c t i", i=PACK, t=PACK)
+            weights = weights.rearrange("p (c i) -> p c i", i=PACK).unsqueeze(2).to_broadcast([P, n // PACK, PACK, PACK])
             nc.vector.tensor_tensor(to, staged, weights, MULT)
 
+        def codes(column, n):
+            if column < 5 * C:
+                return early_codes[:, column:column + n]
+            return late_codes[:, column - 5 * C:column - 5 * C + n]
+
         def quantize(column, place, n):
-            nc.vector.quantize_mx(out=x_codes[:, column:column + n].bitcast(FP8X4), scales=x_scales[:, column:column + n], in_=woven(place, n))
+            nc.vector.quantize_mx(out=codes(column, n).bitcast(FP8X4), scales=x_scales[:, column:column + n], in_=woven(place, n))
 
         def multiply(bank, at, r, e):
             column = (2, 3, 4, 0, 1, 5, 6, 7, 8)[e] * C
@@ -162,7 +172,7 @@ def tile_moe_pre_lin_relu_kernel(tc, xT, w_words, w_scales, b, gate, offs, pos1,
                 out=banks[bank][:, at:at + C],
                 lhsT=w_sb[:, e, 2 * P * r:2 * P * (r + 1)].bitcast(FP4X4),
                 lhsT_scale=ws_sb[:, e, P * r:P * (r + 1)],
-                rhs=x_codes[:, column:column + C].bitcast(FP8X4),
+                rhs=codes(column, C).bitcast(FP8X4),
                 rhs_scale=x_scales[:, column:column + C],
                 start=True,
                 stop=True,
@@ -201,13 +211,14 @@ def tile_moe_pre_lin_relu_kernel(tc, xT, w_words, w_scales, b, gate, offs, pos1,
                 gather(CH_D, j, "scalar")
         gather(CH_D, 3, "vector")
         weave_plain(CH_A, 2 * C)
-        weave_whole(CH_B, gate_bd[:, 0:CH_B[1]], 2 * C + CH_A[1])
-        for chunk, j in ((CH_C1, 0), (CH_C1, 1), (CH_C2, 0), (CH_C3, 0)):
+        weave_whole(CH_B, CH_B[1] - TAIL, gate_b[:], 2 * C + CH_A[1])
+        for chunk, j in ((CH_C1, 0), (CH_C1, 1), (CH_C2, 0)):
             gather(chunk, j, "vector")
-        for chunk, first_plane in ((CH_C1, 2), (CH_C2, 1), (CH_C3, 1)):
+        for chunk, first_plane in ((CH_C1, 2), (CH_C2, 1), (CH_C3, 0)):
             for j in range(first_plane, PACK):
                 gather(chunk, j, "scalar")
-        weave_vector(CH_C1, 0, 0)
+        weave_vector(CH_B, TAIL, banks[2][:, P - TAIL:P], 5 * C - TAIL)
+        weave_vector(CH_C1, CH_C1[1], banks[0][:], 0)
 
         def pair(bank, *units):
             products(bank, *units)
@@ -215,35 +226,39 @@ def tile_moe_pre_lin_relu_kernel(tc, xT, w_words, w_scales, b, gate, offs, pos1,
 
         quantize(0, 0, 4 * C)
         quantize(4 * C, 4 * C, C)
-        weave_whole(CH_D, gate_bd[:, CH_B[1]:], 4 * C)
-        weave_vector(CH_C2, 1, C)
-        weave_vector(CH_C3, 2, 3 * C)
+        weave_whole(CH_D, CH_D[1], gate_d[:], 4 * C)
+        weave_vector(CH_C2, CH_C2[1], banks[1][:], C)
+        weave_vector(CH_C3, CH_C3[1], banks[2][:, P:P + C], 3 * C)
         pair(3, (0, 3), (0, 4))
         pair(4, (0, 0), (0, 1))
         pair(5, (1, 3), (1, 4))
         pair(6, (0, 2), (1, 2))
         pair(7, (1, 0), (1, 1))
         pair(0, (2, 0), (2, 1))
-        pair(3, (2, 2), (2, 3))
-        pair(5, (2, 4))
+        pair(3, (2, 2))
+        multiply(1, C, 2, 3)
+        multiply(5, C, 2, 4)
 
-        quantize(5 * C, C, 2 * C)
-        quantize(7 * C, 3 * C, C)
-        quantize(8 * C, 4 * C, C)
-        pair(1, (0, 5), (0, 6))
-        products(2, (0, 7), (1, 7))
-        products(4, (0, 8), (1, 8))
-        relus(2, (0, 7), (1, 7), on_vector=True)
-        relus(4, (0, 8), (1, 8), on_vector=True)
+        for e, place in ((5, C), (6, 2 * C), (7, 3 * C), (8, 4 * C)):
+            quantize(e * C, place, C)
+        pair(1, (0, 5))
+        relu(1, C, 2, 3)
+        for bank, e in ((2, 6), (4, 7), (5, 8)):
+            products(bank, (0, e))
+            relus(bank, (0, e), on_vector=True)
+        relu(5, C, 2, 4, on_vector=True)
 
-        fetch(0, 0, 0, HALF)
-        fetch(0, 0, HALF, HALF, on_scalar=True)
+        fetch(0, 0, 0, FIRST)
+        fetch(0, 0, FIRST, T - FIRST, on_scalar=True)
         pair(2, (1, 5), (1, 6))
-        pair(4, (2, 5), (2, 6))
-        pair(2, (2, 7), (2, 8))
+        pair(4, (1, 7), (1, 8))
+        products(5, (2, 5), (2, 6))
+        relu(5, 0, 2, 5)
         fetch(1, 0, 0, T, on_scalar=True)
-        fetch(2, 0, 0, HALF, on_scalar=True)
+        relu(5, C, 2, 6)
+        pair(1, (2, 7), (2, 8))
         fetch(1, 1, 0, SHARE, on_scalar=True)
+        fetch(2, 0, 0, HALF, on_scalar=True)
         for l, h in ((1, 0), (0, 1), (1, 1)):
             fetch(2, l, h * HALF, HALF, on_scalar=True)
 
@@ -258,8 +273,8 @@ def tile_moe_pre_lin_relu_kernel(tc, xT, w_words, w_scales, b, gate, offs, pos1,
             store(r, t0, T if r == 1 else n)
 
         for l in (1, 2):
-            for h in (1, 0):
-                fetch(0, l, h * HALF, HALF)
+            fetch(0, l, FIRST, T - FIRST)
+            fetch(0, l, 0, FIRST)
         store(0, 0, T)
         fetch(1, 1, SHARE, T - SHARE)
         third(1, 0, SHARE)

@@ -38,8 +38,8 @@ CH_C2 = (1536, 512)
 CH_D = (2048, 256)
 EXPERT = (0, 1, 2, 4, 5, 6, 7, 3, 8)
 SHARE = 384
-FIRST = 512
-TAIL = 64
+FIRST = 448
+TAIL = 32
 LAST_PIECES = [(384, 256), (640, 128)]
 
 
@@ -142,8 +142,8 @@ def tile_moe_pre_lin_relu_kernel(tc, xT, w_words, w_scales, b, gate, offs, pos1,
             return x_bf[:, PACK * place:PACK * (place + n)]
 
         def weave_plain(chunk, place):
-            staged = stage[chunk][:].rearrange("p (t s) -> p s t", t=PACK)
-            nc.gpsimd.tensor_scalar(woven(place, chunk[1]).rearrange("p (s t) -> p s t", t=PACK), staged, 1.0, 0.0, MULT, ADD)
+            staged = stage[chunk][:].rearrange("p (t c i) -> p c t i", t=PACK, i=2)
+            nc.gpsimd.tensor_scalar(woven(place, chunk[1]).rearrange("p (c i t) -> p c t i", i=2, t=PACK), staged, 1.0, 0.0, MULT, ADD)
 
         def weave_whole(chunk, n, weights, place):
             staged = stage[chunk][:].rearrange("p (t s) -> p s t", t=PACK)[:, 0:n, :]
@@ -155,7 +155,7 @@ def tile_moe_pre_lin_relu_kernel(tc, xT, w_words, w_scales, b, gate, offs, pos1,
             staged = stage[chunk][:].rearrange("p (t s) -> p t s", t=PACK)[:, :, chunk[1] - n:].rearrange("p t (c i) -> p c t i", i=PACK)
             to = woven(place, n).rearrange("p (c i t) -> p c t i", i=PACK, t=PACK)
             weights = weights.rearrange("p (c i) -> p c i", i=PACK).unsqueeze(2).to_broadcast([P, n // PACK, PACK, PACK])
-            nc.vector.tensor_tensor(to, staged, weights, MULT)
+            nc.vector.tensor_tensor(to, weights, staged, MULT)
 
         def codes(column, n):
             if column < 5 * C:
@@ -229,33 +229,34 @@ def tile_moe_pre_lin_relu_kernel(tc, xT, w_words, w_scales, b, gate, offs, pos1,
         weave_whole(CH_D, CH_D[1], gate_d[:], 4 * C)
         weave_vector(CH_C2, CH_C2[1], banks[1][:], C)
         weave_vector(CH_C3, CH_C3[1], banks[2][:, P:P + C], 3 * C)
-        pair(3, (0, 3), (0, 4))
+        pair(5, (0, 3), (0, 4))
         pair(4, (0, 0), (0, 1))
-        pair(5, (1, 3), (1, 4))
+        pair(3, (1, 3), (1, 4))
         pair(6, (0, 2), (1, 2))
         pair(7, (1, 0), (1, 1))
-        pair(0, (2, 0), (2, 1))
-        pair(3, (2, 2))
+        multiply(0, C, 2, 4)
+        pair(5, (2, 0), (2, 1))
         multiply(1, C, 2, 3)
-        multiply(5, C, 2, 4)
+        multiply(2, C, 2, 2)
 
         for e, place in ((5, C), (6, 2 * C), (7, 3 * C), (8, 4 * C)):
             quantize(e * C, place, C)
         pair(1, (0, 5))
         relu(1, C, 2, 3)
-        for bank, e in ((2, 6), (4, 7), (5, 8)):
+        for bank, e in ((2, 6), (4, 7), (0, 8)):
             products(bank, (0, e))
             relus(bank, (0, e), on_vector=True)
-        relu(5, C, 2, 4, on_vector=True)
+        relu(0, C, 2, 4, on_vector=True)
+        relu(2, C, 2, 2)
 
         fetch(0, 0, 0, FIRST)
         fetch(0, 0, FIRST, T - FIRST, on_scalar=True)
-        pair(2, (1, 5), (1, 6))
-        pair(4, (1, 7), (1, 8))
-        products(5, (2, 5), (2, 6))
-        relu(5, 0, 2, 5)
+        pair(4, (1, 5), (1, 6))
+        pair(2, (1, 7), (1, 8))
+        products(0, (2, 5), (2, 6))
+        relu(0, 0, 2, 5)
         fetch(1, 0, 0, T, on_scalar=True)
-        relu(5, C, 2, 6)
+        relu(0, C, 2, 6)
         pair(1, (2, 7), (2, 8))
         fetch(1, 1, 0, SHARE, on_scalar=True)
         fetch(2, 0, 0, HALF, on_scalar=True)

from contextlib import ExitStack

import concourse.mybir as mybir
from concourse.masks import make_identity

K, T, E, C, N = 512, 768, 9, 256, 384
S = E * C
FLOPS = 2 * K * N * S
BYTES = 4 * K * T + E * K * N // 2 + E * (K // 32) * N + 4 * N * E + 4 * S + 2 * 128 * (S + 3 * T) // 16 + 4 * N * T

F32 = mybir.dt.float32
BF16 = mybir.dt.bfloat16
I32 = mybir.dt.int32
U32 = mybir.dt.uint32
U16 = mybir.dt.uint16
U8 = mybir.dt.uint8
FP8X4 = mybir.dt.float8_e4m3fn_x4
FP4X4 = mybir.dt.float4_e2m1fn_x4
MULT = mybir.AluOpType.mult
ADD = mybir.AluOpType.add
MAX = mybir.AluOpType.max
RELU = mybir.ActivationFunctionType.Relu
COPY = mybir.ActivationFunctionType.Copy

P = 128
PACK = 4
BANK = 512
ROW_TILES = N // P
HALF = T // 2
ALIGN = 64
WIDTH = {F32: 4, U32: 4, BF16: 2, U8: 1}

CH_A = (0, 384)
CH_B = (384, 384)
CH_C3 = (768, 256)
CH_C1 = (1024, 512)
CH_C2 = (1536, 512)
CH_D = (2048, 256)
EXPERT = (0, 1, 2, 4, 5, 6, 7, 3, 8)
SHARE = 384
FIRST = 448
TAIL = 32
LAST_PIECES = [(384, 256), (640, 128)]


def tile_moe_pre_lin_relu_kernel(tc, xT, w_words, w_scales, b, gate, offs, pos1, pos2, pos3, out):
    nc = tc.nc
    with ExitStack() as ctx:
        keep = ctx.enter_context(tc.tile_pool(name="keep", bufs=1))
        data = ctx.enter_context(tc.tile_pool(name="data", bufs=1))
        psum = ctx.enter_context(tc.psum_pool(name="psum", bufs=1))

        offs_sb = keep.tile([P, S // 16], U16, name="offs_sb")
        pos_sb = [keep.tile([P, T // 16], U16, name="pos_sb%d" % l) for l in range(3)]

        free = [0]

        def tile(columns, dtype, name, at=None):
            if at is None:
                at = free[0]
            free[0] = max(free[0], at + -(-columns * WIDTH[dtype] // ALIGN) * ALIGN)
            return data.tile([P, columns], dtype, name=name, align_bytes=ALIGN, offset=at)

        planes = [tile(T, F32, "plane%d" % j) for j in range(PACK)]
        stage = {}
        stage[CH_C1] = tile(PACK * CH_C1[1], F32, "stage_c1")
        gate_a = tile(CH_A[1], F32, "gate_a", at=free[0] - 2 * CH_A[1])
        stage[CH_C2] = tile(PACK * CH_C2[1], F32, "stage_c2", at=free[0] - 2 * CH_A[1])
        at_a = free[0]
        stage[CH_A] = tile(PACK * CH_A[1], F32, "stage_a")
        stage[CH_C3] = tile(PACK * CH_C3[1], F32, "stage_c3", at=at_a)
        stage[CH_B] = tile(PACK * CH_B[1], F32, "stage_b")
        at_d = free[0]
        stage[CH_D] = tile(PACK * CH_D[1], F32, "stage_d")
        gate_b = tile(CH_B[1] - TAIL, F32, "gate_b")
        gate_d = tile(CH_D[1], F32, "gate_d")
        gate_cols = tile(2 * PACK, F32, "gate_cols")
        gate_ones = tile(3, F32, "gate_ones")
        identity = tile(P, F32, "identity")

        x_bf = tile(5 * C * PACK, BF16, "x_bf")
        ys = [tile(S, F32, "y%d" % r) for r in range(ROW_TILES)]
        w_sb = tile(E * 2 * N, U8, "w_sb")[:].rearrange("p (e n) -> p e n", e=E)
        ws_sb = tile(E * N, U8, "ws_sb")[:].rearrange("p (e n) -> p e n", e=E)
        early_codes = tile(5 * C, U32, "early_codes")
        late_codes = tile(4 * C, U32, "late_codes", at=at_d)
        x_scales = tile(S, U8, "x_scales")
        bias = tile(ROW_TILES * E, F32, "bias")[:].rearrange("p (r e) -> p r e", e=E)
        sums = [[tile(T, F32, "sum%d_%d" % (r, l)) for l in range(3)] for r in range(ROW_TILES)]
        extra = [None, tile(SHARE, F32, "extra1"), tile(T, F32, "extra2")]
        banks = [psum.tile([P, BANK], F32, name="bank%d" % i) for i in range(8)]

        spare = tile(2, F32, "spare")
        nc.gpsimd.memset(spare[:, 0:1], 0.0)
        nc.scalar.activation(spare[:, 1:2], spare[:, 0:1], RELU)

        nc.gpsimd.memset(ws_sb.rearrange("p e n -> p (e n)").bitcast(I32), 0)
        make_identity(nc, identity[:])

        x_rows = xT.rearrange("(p j) t -> p j t", j=PACK)
        scale_rows = w_scales.rearrange("e a q n -> q (e a) n").bitcast(I32)
        word_rows = w_words.rearrange("e a p n -> p (e a) n").bitcast(I32)

        nc.sync.dma_start(planes[0][:], x_rows[:, 0, :])
        nc.sync.dma_start(offs_sb[:], offs)
        nc.sync.dma_start(gate_a[:], gate[0:P, 0:CH_A[1]])
        for j in range(1, PACK):
            nc.sync.dma_start(planes[j][:], x_rows[:, j, :])
        nc.sync.dma_start(gate_b[:], gate[0:P, CH_B[0]:CH_C3[0] - TAIL])
        nc.sync.dma_start(
            gate_cols[:].rearrange("p (g i) -> p g i", i=PACK),
            gate[0, CH_C1[0]:CH_D[0]].rearrange("(g p i) -> p g i", p=P, i=PACK),
        )
        with nc.allow_non_contiguous_dma(reason="one gate value a partition and group of 128 slots"):
            nc.sync.dma_start(gate_ones[:], gate[0, CH_C3[0] - P:CH_C1[0]].rearrange("(g p) -> p g", p=P))
        for q in range(4):
            nc.sync.dma_start(ws_sb[32 * q:32 * q + 4, :, :].bitcast(I32), scale_rows[4 * q:4 * q + 4, :, :])
        nc.sync.dma_start(gate_d[:], gate[0:P, CH_D[0]:S])
        nc.sync.dma_start(w_sb.bitcast(I32), word_rows)
        nc.sync.dma_start(bias, b.rearrange("(r p) e -> p r e", p=P))
        for l, pos in enumerate((pos1, pos2, pos3)):
            nc.sync.dma_start(pos_sb[l][:], pos)

        for g in range(2):
            for i in range(PACK):
                nc.tensor.transpose(banks[g][:].rearrange("p (c i) -> p i c", i=PACK)[:, i, :], gate_cols[:, PACK * g + i:PACK * g + i + 1].to_broadcast([P, P]), identity[:])
        for g in range(3):
            nc.tensor.transpose(banks[2][:, g * P:(g + 1) * P], gate_ones[:, g:g + 1].to_broadcast([P, P]), identity[:])

        def gather(chunk, j, how):
            s0, n = chunk
            found = planes[j][:].indirect(offs_sb[:, s0 // 16:(s0 + n) // 16])
            to = stage[chunk][:, j * n:(j + 1) * n]
            if how == "scalar":
                nc.scalar.activation(to, found, COPY)
            elif how == "vector":
                nc.vector.tensor_copy(to, found)
            else:
                nc.vector.tensor_tensor(to, found, gate_a[:], MULT)

        def woven(place, n):
            return x_bf[:, PACK * place:PACK * (place + n)]

        def weave_plain(chunk, place):
            staged = stage[chunk][:].rearrange("p (t c i) -> p c t i", t=PACK, i=2)
            nc.gpsimd.tensor_scalar(woven(place, chunk[1]).rearrange("p (c i t) -> p c t i", i=2, t=PACK), staged, 1.0, 0.0, MULT, ADD)

        def weave_whole(chunk, n, weights, place):
            staged = stage[chunk][:].rearrange("p (t s) -> p s t", t=PACK)[:, 0:n, :]
            nc.gpsimd.tensor_tensor(
                woven(place, n).rearrange("p (s t) -> p s t", t=PACK), staged, weights.unsqueeze(2).to_broadcast([P, n, PACK]), MULT
            )

        def weave_vector(chunk, n, weights, place):
            staged = stage[chunk][:].rearrange("p (t s) -> p t s", t=PACK)[:, :, chunk[1] - n:].rearrange("p t (c i) -> p c t i", i=PACK)
            to = woven(place, n).rearrange("p (c i t) -> p c t i", i=PACK, t=PACK)
            weights = weights.rearrange("p (c i) -> p c i", i=PACK).unsqueeze(2).to_broadcast([P, n // PACK, PACK, PACK])
            nc.vector.tensor_tensor(to, weights, staged, MULT)

        def codes(column, n):
            if column < 5 * C:
                return early_codes[:, column:column + n]
            return late_codes[:, column - 5 * C:column - 5 * C + n]

        def quantize(column, place, n):
            nc.vector.quantize_mx(out=codes(column, n).bitcast(FP8X4), scales=x_scales[:, column:column + n], in_=woven(place, n))

        def multiply(bank, at, r, e):
            column = (2, 3, 4, 0, 1, 5, 6, 7, 8)[e] * C
            e = EXPERT[e]
            nc.tensor.matmul_mx(
                out=banks[bank][:, at:at + C],
                lhsT=w_sb[:, e, 2 * P * r:2 * P * (r + 1)].bitcast(FP4X4),
                lhsT_scale=ws_sb[:, e, P * r:P * (r + 1)],
                rhs=codes(column, C).bitcast(FP8X4),
                rhs_scale=x_scales[:, column:column + C],
                start=True,
                stop=True,
            )

        def relu(bank, at, r, e, on_vector=False):
            e = EXPERT[e]
            to = ys[r][:, e * C:(e + 1) * C]
            if on_vector:
                nc.vector.tensor_scalar(to, banks[bank][:, at:at + C], bias[:, r, e:e + 1], 0.0, ADD, MAX)
            else:
                nc.scalar.activation(to, banks[bank][:, at:at + C], RELU, bias=bias[:, r, e:e + 1])

        def products(bank, *units):
            for i, (r, e) in enumerate(units):
                multiply(bank, i * C, r, e)

        def relus(bank, *units, on_vector=False):
            for i, (r, e) in enumerate(units):
                relu(bank, i * C, r, e, on_vector)

        def fetch(r, l, t0, n, on_scalar=False):
            found = ys[r][:].indirect(pos_sb[l][:, t0 // 16:(t0 + n) // 16])
            if on_scalar:
                nc.scalar.activation(sums[r][l][:, t0:t0 + n], found, COPY)
            elif l == 0:
                nc.vector.tensor_copy(sums[r][l][:, t0:t0 + n], found)
            else:
                nc.vector.tensor_tensor(sums[r][l][:, t0:t0 + n], found, sums[r][l - 1][:, t0:t0 + n], ADD)

        gather(CH_D, 0, "vector")
        for j in range(PACK):
            gather(CH_A, j, "times gate")
            gather(CH_B, j, "scalar")
            if j in (1, 2):
                gather(CH_D, j, "scalar")
        gather(CH_D, 3, "vector")
        weave_plain(CH_A, 2 * C)
        weave_whole(CH_B, CH_B[1] - TAIL, gate_b[:], 2 * C + CH_A[1])
        for chunk, j in ((CH_C1, 0), (CH_C1, 1), (CH_C2, 0)):
            gather(chunk, j, "vector")
        for chunk, first_plane in ((CH_C1, 2), (CH_C2, 1), (CH_C3, 0)):
            for j in range(first_plane, PACK):
                gather(chunk, j, "scalar")
        weave_vector(CH_B, TAIL, banks[2][:, P - TAIL:P], 5 * C - TAIL)
        weave_vector(CH_C1, CH_C1[1], banks[0][:], 0)

        def pair(bank, *units):
            products(bank, *units)
            relus(bank, *units)

        quantize(0, 0, 4 * C)
        quantize(4 * C, 4 * C, C)
        weave_whole(CH_D, CH_D[1], gate_d[:], 4 * C)
        weave_vector(CH_C2, CH_C2[1], banks[1][:], C)
        weave_vector(CH_C3, CH_C3[1], banks[2][:, P:P + C], 3 * C)
        pair(5, (0, 3), (0, 4))
        pair(4, (0, 0), (0, 1))
        pair(3, (1, 3), (1, 4))
        pair(6, (0, 2), (1, 2))
        pair(7, (1, 0), (1, 1))
        multiply(0, C, 2, 4)
        pair(5, (2, 0), (2, 1))
        multiply(1, C, 2, 3)
        multiply(2, C, 2, 2)

        for e, place in ((5, C), (6, 2 * C), (7, 3 * C), (8, 4 * C)):
            quantize(e * C, place, C)
        pair(1, (0, 5))
        relu(1, C, 2, 3)
        for bank, e in ((2, 6), (4, 7), (0, 8)):
            products(bank, (0, e))
            relus(bank, (0, e), on_vector=True)
        relu(0, C, 2, 4, on_vector=True)
        relu(2, C, 2, 2)

        fetch(0, 0, 0, FIRST)
        fetch(0, 0, FIRST, T - FIRST, on_scalar=True)
        pair(4, (1, 5), (1, 6))
        pair(2, (1, 7), (1, 8))
        products(0, (2, 5), (2, 6))
        relu(0, 0, 2, 5)
        fetch(1, 0, 0, T, on_scalar=True)
        relu(0, C, 2, 6)
        pair(1, (2, 7), (2, 8))
        fetch(1, 1, 0, SHARE, on_scalar=True)
        fetch(2, 0, 0, HALF, on_scalar=True)
        for l, h in ((1, 0), (0, 1), (1, 1)):
            fetch(2, l, h * HALF, HALF, on_scalar=True)

        def third(r, t0, n):
            nc.vector.tensor_tensor(extra[r][:, t0:t0 + n], ys[r][:].indirect(pos_sb[2][:, t0 // 16:(t0 + n) // 16]), sums[r][0][:, t0:t0 + n], ADD)

        def store(r, t0, n):
            nc.sync.dma_start(out[r * P:(r + 1) * P, t0:t0 + n], sums[r][2][:, t0:t0 + n])

        def finish(r, t0, n):
            nc.vector.tensor_tensor(sums[r][2][:, t0:t0 + n], extra[r][:, t0:t0 + n], sums[r][1][:, t0:t0 + n], ADD)
            store(r, t0, T if r == 1 else n)

        for l in (1, 2):
            fetch(0, l, FIRST, T - FIRST)
            fetch(0, l, 0, FIRST)
        store(0, 0, T)
        fetch(1, 1, SHARE, T - SHARE)
        third(1, 0, SHARE)
        fetch(1, 2, SHARE, T - SHARE)
        third(2, 0, HALF)
        finish(1, 0, SHARE)
        finish(2, 0, HALF)
        for t0, n in LAST_PIECES:
            third(2, t0, n)
        for t0, n in LAST_PIECES:
            finish(2, t0, n)
